import numpy as np
import ml_dtypes


def mxq(x, axis, fmt="e4m3"):
    dtype, down = {"e4m3": (ml_dtypes.float8_e4m3fn, 7), "e5m2": (ml_dtypes.float8_e5m2, 14)}[fmt]
    v = np.moveaxis(np.asarray(x, np.float32).astype(ml_dtypes.bfloat16).astype(np.float64), axis, -1)
    blocks = v.reshape(v.shape[:-1] + (-1, 32))
    amax = np.abs(blocks).max(-1, keepdims=True)
    byte = np.maximum(np.where(amax > 0, np.frexp(amax)[1] - 1 + 127, 0) - down, 1)
    scale = np.exp2(byte - 127.0)
    codes = (blocks / scale).astype(np.float32).astype(dtype).astype(np.float64)
    return np.moveaxis((codes * scale).reshape(v.shape), -1, axis)


WIDE = False


def mx_kscale(k):
    if not WIDE:
        return np.ones(k)
    levels = np.array([10, -10, 5, -5, 0])
    if k % 512:
        return np.exp2(np.random.permutation(np.resize(levels, k // 32))).repeat(32)
    a = np.empty((k // 512, 16))
    for p in range(k // 512):
        a[p, :8] = np.random.permutation(np.resize(levels, 8))
        for g in range(8):
            far = levels[np.abs(levels - a[p, g]) >= 10]
            a[p, g + 8] = far[np.random.randint(len(far))]
    return np.exp2(a.ravel()).repeat(32)


def f64(x):
    return np.asarray(x).astype(np.float64)


def striped(idx):
    return np.tile(np.asarray(idx).reshape(-1, 16).T, (8, 1)).astype(np.uint16)


def unstriped(offs):
    return offs[:16].T.reshape(-1).astype(np.int64)


B, N, T, D, DV, NQ = 2, 512, 2048, 512, 256, 128
PAGE = 64
DRAFT = 128


def setup_inputs():
    n = np.random.standard_normal
    pages = np.random.permutation(T // PAGE)[:B * N // PAGE]
    idx = (pages[:, None] * PAGE + np.arange(PAGE)[None, :]).reshape(-1)
    s = mx_kscale(D)[:, None]
    u = np.ones(T)
    u[idx] = mx_kscale(B * N)
    r = np.random.uniform(0.5, 2.0, T)
    rk = np.random.uniform(0.5, 2.0, T)
    k = n((D, T)) / s / rk
    v = n((DV, T)) / (u * r)
    when = np.zeros(T)
    when[idx] = np.concatenate([np.concatenate([np.arange(N - DRAFT), N - DRAFT + np.random.randint(0, 16, DRAFT)]) for b in range(B)])
    return {
        "qT": (n((B, D, NQ)) * s * (0.80 / np.sqrt(D))).astype(np.float32),
        "kT": k.astype(np.float32),
        "vT": v.astype(np.float32),
        "ks": np.tile(rk, (128, 1)).astype(np.float32),
        "vs": np.tile(u * r, (128, 1)).astype(np.float32),
        "pos": np.tile(when, (128, 1)).astype(np.float32),
        "qpos": np.random.randint(N - DRAFT, N - DRAFT + 16, (B, NQ, 1)).astype(np.float32),
        "offs": striped(idx),
    }


def reference(qT, kT, vT, ks, vs, pos, qpos, offs):
    idx = unstriped(offs)
    k = f64(kT)
    v = f64(vT)
    pick = lambda x: x[:, idx].reshape(x.shape[0], B, N).transpose(1, 0, 2)
    q = f64(qT)
    score = mxq(q, 1, "e4m3").transpose(0, 2, 1) @ mxq(pick(k), 1, "e4m3")
    score = score * pick(f64(ks))[:, :1, :]
    score = np.where(pick(f64(pos))[:, :1, :] <= f64(qpos), score, -30000.0)
    m = score.max(-1, keepdims=True)
    p = np.exp(score - m)
    total = p.sum(-1, keepdims=True)
    w = p * pick(f64(vs))[:, :1, :]
    y = mxq(w, 2, "e4m3") @ mxq(pick(v).transpose(0, 2, 1), 1, "e4m3")
    y = y / total
    return y

@@ -1,0 +1,265 @@
+from contextlib import ExitStack
+
+import concourse.mybir as mybir
+from concourse.masks import make_identity
+
+F32 = mybir.dt.float32
+BF16 = mybir.dt.bfloat16
+U32 = mybir.dt.uint32
+U16 = mybir.dt.uint16
+U8 = mybir.dt.uint8
+FP8X4 = mybir.dt.float8_e4m3fn_x4
+ALU = mybir.AluOpType
+ACT = mybir.ActivationFunctionType
+AXIS_X = mybir.AxisListType.X
+
+B, NQ, D, DV, N, T = 2, 128, 512, 256, 512, 2048
+P = 128
+PACK = 4
+CHUNKS = N // P
+E_BLOCKS = DV // P
+MASKED = 1.0e30
+VECTOR_COLS = 256
+
+FLOPS = 2 * B * NQ * N * (D + DV)
+BYTES = 4 * (B * D * NQ + (D + DV) * T + 3 * T + B * NQ + B * NQ * DV) + 2 * P * (B * N // 16)
+
+
+def tile_attend_x_ks_draft_kernel(tc, qT, kT, vT, ks, vs, pos, qpos, offs, out):
+    nc = tc.nc
+    with ExitStack() as ctx:
+        keep = ctx.enter_context(tc.tile_pool(name="keep", bufs=1))
+        psum = ctx.enter_context(tc.psum_pool(name="psum", bufs=8))
+
+        def bank():
+            return psum.tile([P, 512], F32, name="bank")
+
+        def per_seq(shape, dtype, name, align=32):
+            return [keep.tile(shape, dtype, name=f"{name}{s}", align_bytes=align) for s in range(B)]
+
+        def seq(s):
+            return slice(s * N, (s + 1) * N)
+
+        offsets = keep.tile([P, B * N // 16], U16, name="offsets")
+        nc.sync.dma_start(offsets[:], offs)
+        table = {}
+        for name, src, engine in (("pos", pos, nc.vector), ("ks", ks, nc.gpsimd), ("vs", vs, nc.vector)):
+            table[name] = keep.tile([P, T], F32, name=name + "_table")
+            engine.memset(table[name][:], 0.0)
+            nc.scalar.dma_start(table[name][0:1, :], src[0:1, :])
+        q_place = per_seq([P, 1], F32, "q_place")
+        for s in range(B):
+            nc.scalar.dma_start(q_place[s][:], qpos[s])
+        k_rows = kT.rearrange("(p t) n -> p t n", t=PACK)
+        k_pool = [keep.tile([P, T], F32, name=f"k_pool{t}") for t in range(PACK)]
+        v_pool = [keep.tile([P, T], F32, name=f"v_pool{e}") for e in range(E_BLOCKS)]
+        q_raw = keep.tile([P, B, PACK, NQ], F32, name="q_raw")
+        nc.sync.dma_start(k_pool[0][:], k_rows[:, 0, :])
+        nc.sync.dma_start(k_pool[1][:], k_rows[:, 1, :])
+        nc.sync.dma_start(q_raw[:], qT.rearrange("b (p t) q -> p b t q", t=PACK))
+        nc.sync.dma_start(k_pool[2][:], k_rows[:, 2, :])
+        nc.sync.dma_start(k_pool[3][:], k_rows[:, 3, :])
+        for e in range(E_BLOCKS):
+            nc.sync.dma_start(v_pool[e][:], vT[e * P : (e + 1) * P, :])
+
+        ident = keep.tile([P, P], F32, name="ident")
+        make_identity(nc, ident[:])
+        warm = keep.tile([P, 1], F32, name="warm")
+        nc.vector.memset(warm[:], 0.0)
+        nc.scalar.activation(warm[:], warm[:], ACT.Exp)
+
+        q_row = keep.tile([P, B, NQ], F32, name="q_row")
+        ps = bank()
+        for s in range(B):
+            nc.tensor.transpose(ps[:, s * NQ : (s + 1) * NQ], q_place[s][:].to_broadcast([P, P]), ident[:])
+        nc.scalar.copy(out=q_row[:].rearrange("p b q -> p (b q)"), in_=ps[:, 0 : B * NQ])
+
+        def gather_table(name):
+            got = keep.tile([P, B * N], F32, name=name + "_got")
+            nc.vector.tensor_copy(got[:], table[name][:].indirect(offsets[:]))
+            return got
+
+        def turn_table(name, got, start, step, scale):
+            col = per_seq([P, CHUNKS], F32, name + "_col")
+            for s in range(B):
+                ps = bank()
+                for c in range(CHUNKS):
+                    a = s * N + c * start
+                    nc.tensor.transpose(ps[:, c * P : (c + 1) * P], got[:, a : a + (P - 1) * step + 1 : step], ident[:])
+                nc.scalar.activation(col[s][:], ps[:, 0 : 512 : P], ACT.Copy, scale=scale)
+            return col
+
+        pos_col = turn_table("pos", gather_table("pos"), P, 1, 1.0)
+        limit = per_seq([P, CHUNKS, NQ], F32, "limit")
+
+        def mask(s):
+            for c in range(CHUNKS):
+                nc.vector.tensor_scalar(
+                    limit[s][:, c, :], q_row[:, s, :], pos_col[s][:, c : c + 1], MASKED, ALU.is_lt, ALU.mult
+                )
+
+        nks_col = turn_table("ks", gather_table("ks"), P, 1, -1.0)
+
+        k_got = keep.tile([P, PACK, B * N], F32, name="k_got")
+        k_bf = per_seq([P, N, PACK], BF16, "k_bf", 64)
+        k_codes = per_seq([P, N], U32, "k_codes", 64)
+        k_scales = per_seq([P, N], U8, "k_scales", 64)
+
+        def gather_k(t):
+            nc.vector.tensor_copy(k_got[:, t, :], k_pool[t][:].indirect(offsets[:]))
+
+        def gather_last_k(s):
+            list_s = offsets[:, s * (N // 16) : (s + 1) * (N // 16)]
+            nc.vector.tensor_copy(k_got[:, 3, seq(s)], k_pool[3][:].indirect(list_s))
+
+        def interleave(copy, s, t, a, z):
+            copy(out=k_bf[s][:, a:z, t : t + 2], in_=k_got[:, t : t + 2, s * N + a : s * N + z].rearrange("p t n -> p n t"))
+
+        def quantize_k(s):
+            nc.vector.quantize_mx(
+                out=k_codes[s][:].bitcast(FP8X4), scales=k_scales[s][:], in_=k_bf[s][:].rearrange("p n t -> p (n t)")
+            )
+
+        gather_k(0)
+        vs_col = turn_table("vs", gather_table("vs"), 1, PACK, 1.0)
+        gather_k(1)
+
+        q_bf = keep.tile([P, B, NQ, PACK], BF16, name="q_bf", align_bytes=64)
+        nc.scalar.copy(out=q_bf[:], in_=q_raw[:].rearrange("p b t q -> p b q t"))
+        q_codes = keep.tile([P, B * NQ], U32, name="q_codes", align_bytes=64)
+        q_scales = keep.tile([P, B * NQ], U8, name="q_scales", align_bytes=64)
+        nc.vector.quantize_mx(
+            out=q_codes[:].bitcast(FP8X4), scales=q_scales[:], in_=q_bf[:].rearrange("p b q t -> p (b q t)")
+        )
+        for s in range(B):
+            interleave(nc.scalar.copy, s, 0, 0, N)
+        gather_k(2)
+
+        scaled = per_seq([P, CHUNKS, NQ], F32, "scaled")
+        negmax = per_seq([P, 1], F32, "negmax")
+        total = per_seq([P, 1], F32, "total")
+        inv = per_seq([P, 1], F32, "inv")
+        prob = per_seq([P, PACK, P], F32, "prob")
+        w_bf = per_seq([P, NQ, PACK], BF16, "w_bf", 64)
+        w_codes = per_seq([P, NQ], U32, "w_codes", 64)
+        w_scales = per_seq([P, NQ], U8, "w_scales", 64)
+        v_got = [keep.tile([P, B * N], F32, name=f"v_got{e}") for e in range(E_BLOCKS)]
+        v_bf = per_seq([P, DV, PACK], BF16, "v_bf", 64)
+        v_codes = per_seq([P, DV], U32, "v_codes", 64)
+        v_scales = per_seq([P, DV], U8, "v_scales", 64)
+        result = per_seq([P, DV], F32, "result")
+        turned = {}
+
+        def scores(s):
+            ps = bank()
+            qc = slice(s * NQ, (s + 1) * NQ)
+            for c in range(CHUNKS):
+                kc = slice(c * P, (c + 1) * P)
+                nc.tensor.matmul_mx(
+                    out=ps[:, kc], lhsT=k_codes[s][:, kc].bitcast(FP8X4), lhsT_scale=k_scales[s][:, kc],
+                    rhs=q_codes[:, qc].bitcast(FP8X4), rhs_scale=q_scales[:, qc], start=True, stop=True,
+                )
+            turned["raw", s] = ps
+
+        def scale_and_mask(s):
+            ps = turned["raw", s]
+            for c in range(CHUNKS):
+                nc.scalar.activation(
+                    scaled[s][:, c, :], ps[:, c * P : (c + 1) * P], ACT.Copy, scale=nks_col[s][:, c : c + 1]
+                )
+
+        def turn_scores(s):
+            ps = bank()
+            for c in range(CHUNKS):
+                kc = slice(c * P, (c + 1) * P)
+                nc.tensor.matmul(ps[:, kc], limit[s][:, c, :], ident[:], is_transpose=True, start=True, stop=False)
+                nc.tensor.matmul(ps[:, kc], scaled[s][:, c, :], ident[:], is_transpose=True, start=False, stop=True)
+            turned["score", s] = ps
+
+        def row_max(s):
+            nc.vector.tensor_reduce(negmax[s][:], turned["score", s][:], AXIS_X, ALU.min)
+
+        def exponent(s):
+            nc.scalar.activation(
+                prob[s][:].rearrange("q t i -> q i t"), turned["score", s][:].rearrange("q (i t) -> q i t", t=PACK),
+                ACT.Exp, bias=negmax[s][:], scale=-1.0, accum_out=total[s][:],
+            )
+
+        def turn_prob(s):
+            ps = bank()
+            for t in range(PACK):
+                nc.tensor.transpose(ps[:, t * P : (t + 1) * P], prob[s][:, t, :], ident[:])
+            turned["prob", s] = ps
+
+        def weights(s):
+            nc.vector.tensor_tensor(
+                w_bf[s][:], turned["prob", s][:].rearrange("p (t q) -> p q t", t=PACK),
+                vs_col[s][:].unsqueeze(1).to_broadcast([P, NQ, PACK]), ALU.mult,
+            )
+
+        def quantize_w(s):
+            nc.vector.quantize_mx(
+                out=w_codes[s][:].bitcast(FP8X4), scales=w_scales[s][:], in_=w_bf[s][:].rearrange("p q t -> p (q t)")
+            )
+
+        def gather_v(e):
+            nc.vector.tensor_copy(v_got[e][:], v_pool[e][:].indirect(offsets[:]))
+
+        def turn_v(e, s):
+            ps = bank()
+            for t in range(PACK):
+                nc.tensor.transpose(ps[:, t * P : (t + 1) * P], v_got[e][:, s * N + t : (s + 1) * N : PACK], ident[:])
+            nc.scalar.copy(out=v_bf[s][:, e * P : (e + 1) * P, :], in_=ps[:].rearrange("p (t c) -> p c t", t=PACK))
+
+        def quantize_v(s):
+            nc.vector.quantize_mx(
+                out=v_codes[s][:].bitcast(FP8X4), scales=v_scales[s][:], in_=v_bf[s][:].rearrange("p c t -> p (c t)")
+            )
+
+        def values(s):
+            ps = bank()
+            nc.tensor.matmul_mx(
+                out=ps[:, 0:DV], lhsT=w_codes[s][:].bitcast(FP8X4), lhsT_scale=w_scales[s][:],
+                rhs=v_codes[s][:].bitcast(FP8X4), rhs_scale=v_scales[s][:], start=True, stop=True,
+            )
+            nc.scalar.activation(result[s][:], ps[:, 0:DV], ACT.Copy, scale=inv[s][:])
+            nc.sync.dma_start(out[s], result[s][:])
+
+        gather_last_k(0)
+        interleave(nc.scalar.copy, 0, 2, VECTOR_COLS, N)
+        gather_last_k(1)
+        interleave(nc.vector.tensor_copy, 0, 2, 0, VECTOR_COLS)
+        interleave(nc.scalar.copy, 1, 2, VECTOR_COLS, N)
+        interleave(nc.vector.tensor_copy, 1, 2, 0, VECTOR_COLS)
+        quantize_k(0)
+        quantize_k(1)
+        scores(0)
+        scores(1)
+        mask(0)
+        mask(1)
+        gather_v(0)
+        scale_and_mask(0)
+        scale_and_mask(1)
+        turn_scores(0)
+        turn_scores(1)
+        gather_v(1)
+        row_max(0)
+        row_max(1)
+        turn_v(0, 0)
+        exponent(0)
+        turn_v(0, 1)
+        exponent(1)
+        turn_prob(0)
+        weights(0)
+        turn_v(1, 0)
+        turn_prob(1)
+        turn_v(1, 1)
+        quantize_w(0)
+        weights(1)
+        nc.vector.reciprocal(inv[0][:], total[0][:])
+        nc.vector.reciprocal(inv[1][:], total[1][:])
+        quantize_v(0)
+        values(0)
+        quantize_w(1)
+        quantize_v(1)
+        values(1)

@@ -19,7 +19,7 @@ PACK = 4
 CHUNKS = N // P
 E_BLOCKS = DV // P
 MASKED = 1.0e30
-VECTOR_COLS = 256
+HALF = PACK // 2
 
 FLOPS = 2 * B * NQ * N * (D + DV)
 BYTES = 4 * (B * D * NQ + (D + DV) * T + 3 * T + B * NQ + B * NQ * DV) + 2 * P * (B * N // 16)
@@ -29,10 +29,10 @@ def tile_attend_x_ks_draft_kernel(tc, qT, kT, vT, ks, vs, pos, qpos, offs, out):
     nc = tc.nc
     with ExitStack() as ctx:
         keep = ctx.enter_context(tc.tile_pool(name="keep", bufs=1))
-        psum = ctx.enter_context(tc.psum_pool(name="psum", bufs=8))
+        psum = ctx.enter_context(tc.psum_pool(name="psum", bufs=1))
 
-        def bank():
-            return psum.tile([P, 512], F32, name="bank")
+        def bank(index):
+            return psum.tile([P, 512], F32, name=f"bank{index}")
 
         def per_seq(shape, dtype, name, align=32):
             return [keep.tile(shape, dtype, name=f"{name}{s}", align_bytes=align) for s in range(B)]
@@ -42,98 +42,97 @@ def tile_attend_x_ks_draft_kernel(tc, qT, kT, vT, ks, vs, pos, qpos, offs, out):
 
         offsets = keep.tile([P, B * N // 16], U16, name="offsets")
         nc.sync.dma_start(offsets[:], offs)
+
+        def list_of(s):
+            return offsets[:, s * (N // 16) : (s + 1) * (N // 16)]
+
         table = {}
-        for name, src, engine in (("pos", pos, nc.vector), ("ks", ks, nc.gpsimd), ("vs", vs, nc.vector)):
+        for name in ("pos", "vs", "ks"):
             table[name] = keep.tile([P, T], F32, name=name + "_table")
-            engine.memset(table[name][:], 0.0)
-            nc.scalar.dma_start(table[name][0:1, :], src[0:1, :])
-        q_place = per_seq([P, 1], F32, "q_place")
-        for s in range(B):
-            nc.scalar.dma_start(q_place[s][:], qpos[s])
+            nc.vector.memset(table[name][:].bitcast(U32), 0)
+        q_place = keep.tile([P, B], F32, name="q_place")
+        nc.scalar.dma_start(q_place[:], qpos.rearrange("b q o -> q (b o)"))
         k_rows = kT.rearrange("(p t) n -> p t n", t=PACK)
         k_pool = [keep.tile([P, T], F32, name=f"k_pool{t}") for t in range(PACK)]
         v_pool = [keep.tile([P, T], F32, name=f"v_pool{e}") for e in range(E_BLOCKS)]
         q_raw = keep.tile([P, B, PACK, NQ], F32, name="q_raw")
+        nc.sync.dma_start(q_raw[:], qT.rearrange("b (p t) q -> p b t q", t=PACK))
+        nc.sync.dma_start(table["pos"][0:1, :], pos[0:1, :])
         nc.sync.dma_start(k_pool[0][:], k_rows[:, 0, :])
         nc.sync.dma_start(k_pool[1][:], k_rows[:, 1, :])
-        nc.sync.dma_start(q_raw[:], qT.rearrange("b (p t) q -> p b t q", t=PACK))
+        nc.sync.dma_start(table["vs"][0:1, :], vs[0:1, :])
         nc.sync.dma_start(k_pool[2][:], k_rows[:, 2, :])
         nc.sync.dma_start(k_pool[3][:], k_rows[:, 3, :])
+        nc.sync.dma_start(table["ks"][0:1, :], ks[0:1, :])
         for e in range(E_BLOCKS):
             nc.sync.dma_start(v_pool[e][:], vT[e * P : (e + 1) * P, :])
 
         ident = keep.tile([P, P], F32, name="ident")
         make_identity(nc, ident[:])
         warm = keep.tile([P, 1], F32, name="warm")
-        nc.vector.memset(warm[:], 0.0)
-        nc.scalar.activation(warm[:], warm[:], ACT.Exp)
+        nc.scalar.activation(warm[:], ident[:, 0:1], ACT.Exp)
 
-        q_row = keep.tile([P, B, NQ], F32, name="q_row")
-        ps = bank()
+        q_row = bank(0)
         for s in range(B):
-            nc.tensor.transpose(ps[:, s * NQ : (s + 1) * NQ], q_place[s][:].to_broadcast([P, P]), ident[:])
-        nc.scalar.copy(out=q_row[:].rearrange("p b q -> p (b q)"), in_=ps[:, 0 : B * NQ])
+            nc.tensor.transpose(q_row[:, s * NQ : (s + 1) * NQ], q_place[:, s : s + 1].to_broadcast([P, P]), ident[:])
+
+        q_bf = keep.tile([P, B, NQ, PACK], BF16, name="q_bf", align_bytes=64)
+        nc.scalar.copy(out=q_bf[:], in_=q_raw[:].rearrange("p b t q -> p b q t"))
 
         def gather_table(name):
             got = keep.tile([P, B * N], F32, name=name + "_got")
             nc.vector.tensor_copy(got[:], table[name][:].indirect(offsets[:]))
             return got
 
-        def turn_table(name, got, start, step, scale):
+        def turn_table(name, got, start, step, scale, first_bank):
             col = per_seq([P, CHUNKS], F32, name + "_col")
             for s in range(B):
-                ps = bank()
+                ps = bank(first_bank + s)
                 for c in range(CHUNKS):
                     a = s * N + c * start
                     nc.tensor.transpose(ps[:, c * P : (c + 1) * P], got[:, a : a + (P - 1) * step + 1 : step], ident[:])
                 nc.scalar.activation(col[s][:], ps[:, 0 : 512 : P], ACT.Copy, scale=scale)
             return col
 
-        pos_col = turn_table("pos", gather_table("pos"), P, 1, 1.0)
+        pos_col = turn_table("pos", gather_table("pos"), P, 1, 1.0, 1)
+        ahead = per_seq([P, CHUNKS, NQ], F32, "ahead")
         limit = per_seq([P, CHUNKS, NQ], F32, "limit")
-
-        def mask(s):
+        for s in range(B):
             for c in range(CHUNKS):
-                nc.vector.tensor_scalar(
-                    limit[s][:, c, :], q_row[:, s, :], pos_col[s][:, c : c + 1], MASKED, ALU.is_lt, ALU.mult
+                nc.scalar.activation(
+                    ahead[s][:, c, :], q_row[:, s * NQ : (s + 1) * NQ], ACT.Sign, bias=pos_col[s][:, c : c + 1], scale=-1.0
                 )
+            nc.scalar.activation(limit[s][:], ahead[s][:], ACT.Relu, scale=MASKED)
 
-        nks_col = turn_table("ks", gather_table("ks"), P, 1, -1.0)
-
-        k_got = keep.tile([P, PACK, B * N], F32, name="k_got")
+        k_first = keep.tile([P, HALF, B * N], F32, name="pos_table")
         k_bf = per_seq([P, N, PACK], BF16, "k_bf", 64)
         k_codes = per_seq([P, N], U32, "k_codes", 64)
         k_scales = per_seq([P, N], U8, "k_scales", 64)
 
-        def gather_k(t):
-            nc.vector.tensor_copy(k_got[:, t, :], k_pool[t][:].indirect(offsets[:]))
-
-        def gather_last_k(s):
-            list_s = offsets[:, s * (N // 16) : (s + 1) * (N // 16)]
-            nc.vector.tensor_copy(k_got[:, 3, seq(s)], k_pool[3][:].indirect(list_s))
-
-        def interleave(copy, s, t, a, z):
-            copy(out=k_bf[s][:, a:z, t : t + 2], in_=k_got[:, t : t + 2, s * N + a : s * N + z].rearrange("p t n -> p n t"))
+        def interleave(copy, got, s, t, a, z):
+            copy(out=k_bf[s][:, a:z, t : t + HALF], in_=got[:, :, s * N + a : s * N + z].rearrange("p t n -> p n t"))
 
         def quantize_k(s):
             nc.vector.quantize_mx(
                 out=k_codes[s][:].bitcast(FP8X4), scales=k_scales[s][:], in_=k_bf[s][:].rearrange("p n t -> p (n t)")
             )
 
-        gather_k(0)
-        vs_col = turn_table("vs", gather_table("vs"), 1, PACK, 1.0)
-        gather_k(1)
-
-        q_bf = keep.tile([P, B, NQ, PACK], BF16, name="q_bf", align_bytes=64)
-        nc.scalar.copy(out=q_bf[:], in_=q_raw[:].rearrange("p b t q -> p b q t"))
+        nc.vector.tensor_copy(k_first[:, 0, :], k_pool[0][:].indirect(offsets[:]))
         q_codes = keep.tile([P, B * NQ], U32, name="q_codes", align_bytes=64)
         q_scales = keep.tile([P, B * NQ], U8, name="q_scales", align_bytes=64)
         nc.vector.quantize_mx(
             out=q_codes[:].bitcast(FP8X4), scales=q_scales[:], in_=q_bf[:].rearrange("p b q t -> p (b q t)")
         )
+        nc.vector.tensor_copy(k_first[:, 1, :], k_pool[1][:].indirect(offsets[:]))
         for s in range(B):
-            interleave(nc.scalar.copy, s, 0, 0, N)
-        gather_k(2)
+            interleave(nc.scalar.copy, k_first, s, 0, 0, N)
+        vs_col = turn_table("vs", gather_table("vs"), 1, PACK, 1.0, 3)
+        k_last = keep.tile([P, HALF, B * N], F32, name="vs_table")
+        nc.vector.tensor_copy(k_last[:, 0, :], k_pool[2][:].indirect(offsets[:]))
+        for s in range(B):
+            nc.vector.tensor_copy(k_last[:, 1, seq(s)], k_pool[3][:].indirect(list_of(s)))
+            interleave(nc.scalar.copy, k_last, s, HALF, 0, N)
+        nks_col = turn_table("ks", gather_table("ks"), P, 1, -1.0, 5)
 
         scaled = per_seq([P, CHUNKS, NQ], F32, "scaled")
         negmax = per_seq([P, 1], F32, "negmax")
@@ -143,15 +142,15 @@ def tile_attend_x_ks_draft_kernel(tc, qT, kT, vT, ks, vs, pos, qpos, offs, out):
         w_bf = per_seq([P, NQ, PACK], BF16, "w_bf", 64)
         w_codes = per_seq([P, NQ], U32, "w_codes", 64)
         w_scales = per_seq([P, NQ], U8, "w_scales", 64)
-        v_got = [keep.tile([P, B * N], F32, name=f"v_got{e}") for e in range(E_BLOCKS)]
-        v_bf = per_seq([P, DV, PACK], BF16, "v_bf", 64)
+        v_got = [per_seq([P, N], BF16, f"v_got{e}_") for e in range(E_BLOCKS)]
+        v_bf = per_seq([P, DV * PACK], BF16, "v_bf", 64)
         v_codes = per_seq([P, DV], U32, "v_codes", 64)
         v_scales = per_seq([P, DV], U8, "v_scales", 64)
         result = per_seq([P, DV], F32, "result")
         turned = {}
 
         def scores(s):
-            ps = bank()
+            ps = bank(1 + s)
             qc = slice(s * NQ, (s + 1) * NQ)
             for c in range(CHUNKS):
                 kc = slice(c * P, (c + 1) * P)
@@ -159,17 +158,13 @@ def tile_attend_x_ks_draft_kernel(tc, qT, kT, vT, ks, vs, pos, qpos, offs, out):
                     out=ps[:, kc], lhsT=k_codes[s][:, kc].bitcast(FP8X4), lhsT_scale=k_scales[s][:, kc],
                     rhs=q_codes[:, qc].bitcast(FP8X4), rhs_scale=q_scales[:, qc], start=True, stop=True,
                 )
-            turned["raw", s] = ps
-
-        def scale_and_mask(s):
-            ps = turned["raw", s]
             for c in range(CHUNKS):
                 nc.scalar.activation(
                     scaled[s][:, c, :], ps[:, c * P : (c + 1) * P], ACT.Copy, scale=nks_col[s][:, c : c + 1]
                 )
 
         def turn_scores(s):
-            ps = bank()
+            ps = bank(3 + s)
             for c in range(CHUNKS):
                 kc = slice(c * P, (c + 1) * P)
                 nc.tensor.matmul(ps[:, kc], limit[s][:, c, :], ident[:], is_transpose=True, start=True, stop=False)
@@ -186,7 +181,7 @@ def tile_attend_x_ks_draft_kernel(tc, qT, kT, vT, ks, vs, pos, qpos, offs, out):
             )
 
         def turn_prob(s):
-            ps = bank()
+            ps = bank(7 * s)
             for t in range(PACK):
                 nc.tensor.transpose(ps[:, t * P : (t + 1) * P], prob[s][:, t, :], ident[:])
             turned["prob", s] = ps
@@ -202,22 +197,25 @@ def tile_attend_x_ks_draft_kernel(tc, qT, kT, vT, ks, vs, pos, qpos, offs, out):
                 out=w_codes[s][:].bitcast(FP8X4), scales=w_scales[s][:], in_=w_bf[s][:].rearrange("p q t -> p (q t)")
             )
 
-        def gather_v(e):
-            nc.vector.tensor_copy(v_got[e][:], v_pool[e][:].indirect(offsets[:]))
+        def gather_v(e, s):
+            nc.vector.tensor_copy(v_got[e][s][:], v_pool[e][:].indirect(list_of(s)))
 
         def turn_v(e, s):
-            ps = bank()
-            for t in range(PACK):
-                nc.tensor.transpose(ps[:, t * P : (t + 1) * P], v_got[e][:, s * N + t : (s + 1) * N : PACK], ident[:])
-            nc.scalar.copy(out=v_bf[s][:, e * P : (e + 1) * P, :], in_=ps[:].rearrange("p (t c) -> p c t", t=PACK))
-
-        def quantize_v(s):
-            nc.vector.quantize_mx(
-                out=v_codes[s][:].bitcast(FP8X4), scales=v_scales[s][:], in_=v_bf[s][:].rearrange("p c t -> p (c t)")
+            ps = bank(1 + B * e + s)
+            words = v_got[e][s][:].bitcast(F32)
+            for u in range(HALF):
+                nc.tensor.transpose(ps[:, u * P : (u + 1) * P], words[:, u : N // 2 : HALF], ident[:])
+            place = v_bf[s][:].bitcast(F32)[:, e * P * HALF : (e + 1) * P * HALF]
+            nc.scalar.copy(
+                out=place.rearrange("p (c u) -> p c u", u=HALF),
+                in_=ps[:, 0 : HALF * P].rearrange("p (u c) -> p c u", u=HALF),
             )
 
+        def quantize_v(s):
+            nc.vector.quantize_mx(out=v_codes[s][:].bitcast(FP8X4), scales=v_scales[s][:], in_=v_bf[s][:])
+
         def values(s):
-            ps = bank()
+            ps = bank(5 + s)
             nc.tensor.matmul_mx(
                 out=ps[:, 0:DV], lhsT=w_codes[s][:].bitcast(FP8X4), lhsT_scale=w_scales[s][:],
                 rhs=v_codes[s][:].bitcast(FP8X4), rhs_scale=v_scales[s][:], start=True, stop=True,
@@ -225,41 +223,22 @@ def tile_attend_x_ks_draft_kernel(tc, qT, kT, vT, ks, vs, pos, qpos, offs, out):
             nc.scalar.activation(result[s][:], ps[:, 0:DV], ACT.Copy, scale=inv[s][:])
             nc.sync.dma_start(out[s], result[s][:])
 
-        gather_last_k(0)
-        interleave(nc.scalar.copy, 0, 2, VECTOR_COLS, N)
-        gather_last_k(1)
-        interleave(nc.vector.tensor_copy, 0, 2, 0, VECTOR_COLS)
-        interleave(nc.scalar.copy, 1, 2, VECTOR_COLS, N)
-        interleave(nc.vector.tensor_copy, 1, 2, 0, VECTOR_COLS)
-        quantize_k(0)
-        quantize_k(1)
-        scores(0)
-        scores(1)
-        mask(0)
-        mask(1)
-        gather_v(0)
-        scale_and_mask(0)
-        scale_and_mask(1)
-        turn_scores(0)
-        turn_scores(1)
-        gather_v(1)
-        row_max(0)
-        row_max(1)
-        turn_v(0, 0)
-        exponent(0)
-        turn_v(0, 1)
-        exponent(1)
-        turn_prob(0)
-        weights(0)
-        turn_v(1, 0)
-        turn_prob(1)
-        turn_v(1, 1)
-        quantize_w(0)
-        weights(1)
-        nc.vector.reciprocal(inv[0][:], total[0][:])
-        nc.vector.reciprocal(inv[1][:], total[1][:])
-        quantize_v(0)
-        values(0)
-        quantize_w(1)
-        quantize_v(1)
-        values(1)
+        for s in range(B):
+            quantize_k(s)
+            scores(s)
+            turn_scores(s)
+            gather_v(0, s)
+        for s in range(B):
+            row_max(s)
+            exponent(s)
+            turn_v(0, s)
+            turn_prob(s)
+            gather_v(1, s)
+        for s in range(B):
+            weights(s)
+            turn_v(1, s)
+            nc.vector.reciprocal(inv[s][:], total[s][:])
+        for s in range(B):
+            quantize_w(s)
+            quantize_v(s)
+            values(s)

@@ -20,6 +20,7 @@ CHUNKS = N // P
 E_BLOCKS = DV // P
 MASKED = 1.0e30
 HALF = PACK // 2
+VECTOR_COLS = 256
 
 FLOPS = 2 * B * NQ * N * (D + DV)
 BYTES = 4 * (B * D * NQ + (D + DV) * T + 3 * T + B * NQ + B * NQ * DV) + 2 * P * (B * N // 16)
@@ -47,7 +48,7 @@ def tile_attend_x_ks_draft_kernel(tc, qT, kT, vT, ks, vs, pos, qpos, offs, out):
             return offsets[:, s * (N // 16) : (s + 1) * (N // 16)]
 
         table = {}
-        for name in ("pos", "vs", "ks"):
+        for name in ("pos", "ks", "vs"):
             table[name] = keep.tile([P, T], F32, name=name + "_table")
             nc.vector.memset(table[name][:].bitcast(U32), 0)
         q_place = keep.tile([P, B], F32, name="q_place")
@@ -56,21 +57,22 @@ def tile_attend_x_ks_draft_kernel(tc, qT, kT, vT, ks, vs, pos, qpos, offs, out):
         k_pool = [keep.tile([P, T], F32, name=f"k_pool{t}") for t in range(PACK)]
         v_pool = [keep.tile([P, T], F32, name=f"v_pool{e}") for e in range(E_BLOCKS)]
         q_raw = keep.tile([P, B, PACK, NQ], F32, name="q_raw")
-        nc.sync.dma_start(q_raw[:], qT.rearrange("b (p t) q -> p b t q", t=PACK))
-        nc.sync.dma_start(table["pos"][0:1, :], pos[0:1, :])
         nc.sync.dma_start(k_pool[0][:], k_rows[:, 0, :])
+        nc.sync.dma_start(table["pos"][0:1, :], pos[0:1, :])
+        nc.sync.dma_start(q_raw[:], qT.rearrange("b (p t) q -> p b t q", t=PACK))
         nc.sync.dma_start(k_pool[1][:], k_rows[:, 1, :])
-        nc.sync.dma_start(table["vs"][0:1, :], vs[0:1, :])
-        nc.sync.dma_start(k_pool[2][:], k_rows[:, 2, :])
-        nc.sync.dma_start(k_pool[3][:], k_rows[:, 3, :])
         nc.sync.dma_start(table["ks"][0:1, :], ks[0:1, :])
+        nc.sync.dma_start(k_pool[2][:], k_rows[:, 2, :])
+        nc.sync.dma_start(table["vs"][0:1, :], vs[0:1, :])
+        nc.sync.dma_start(k_pool[3][:], k_rows[:, 3, :])
         for e in range(E_BLOCKS):
             nc.sync.dma_start(v_pool[e][:], vT[e * P : (e + 1) * P, :])
 
+        warm = keep.tile([P, 1], F32, name="warm")
+        nc.gpsimd.memset(warm[:], 0.0)
+        nc.scalar.activation(warm[:], warm[:], ACT.Exp)
         ident = keep.tile([P, P], F32, name="ident")
         make_identity(nc, ident[:])
-        warm = keep.tile([P, 1], F32, name="warm")
-        nc.scalar.activation(warm[:], ident[:, 0:1], ACT.Exp)
 
         q_row = bank(0)
         for s in range(B):
@@ -84,17 +86,17 @@ def tile_attend_x_ks_draft_kernel(tc, qT, kT, vT, ks, vs, pos, qpos, offs, out):
             nc.vector.tensor_copy(got[:], table[name][:].indirect(offsets[:]))
             return got
 
-        def turn_table(name, got, start, step, scale, first_bank):
+        def turn_table(name, got, scale, first_bank):
             col = per_seq([P, CHUNKS], F32, name + "_col")
             for s in range(B):
                 ps = bank(first_bank + s)
                 for c in range(CHUNKS):
-                    a = s * N + c * start
-                    nc.tensor.transpose(ps[:, c * P : (c + 1) * P], got[:, a : a + (P - 1) * step + 1 : step], ident[:])
+                    a = s * N + c * P
+                    nc.tensor.transpose(ps[:, c * P : (c + 1) * P], got[:, a : a + P], ident[:])
                 nc.scalar.activation(col[s][:], ps[:, 0 : 512 : P], ACT.Copy, scale=scale)
             return col
 
-        pos_col = turn_table("pos", gather_table("pos"), P, 1, 1.0, 1)
+        pos_col = turn_table("pos", gather_table("pos"), 1.0, 1)
         ahead = per_seq([P, CHUNKS, NQ], F32, "ahead")
         limit = per_seq([P, CHUNKS, NQ], F32, "limit")
         for s in range(B):
@@ -103,6 +105,12 @@ def tile_attend_x_ks_draft_kernel(tc, qT, kT, vT, ks, vs, pos, qpos, offs, out):
                     ahead[s][:, c, :], q_row[:, s * NQ : (s + 1) * NQ], ACT.Sign, bias=pos_col[s][:, c : c + 1], scale=-1.0
                 )
             nc.scalar.activation(limit[s][:], ahead[s][:], ACT.Relu, scale=MASKED)
+        score = [bank(3 + s) for s in range(B)]
+        for s in range(B):
+            for c in range(CHUNKS):
+                nc.tensor.matmul(
+                    score[s][:, c * P : (c + 1) * P], limit[s][:, c, :], ident[:], is_transpose=True, start=c == 0, stop=False
+                )
 
         k_first = keep.tile([P, HALF, B * N], F32, name="pos_table")
         k_bf = per_seq([P, N, PACK], BF16, "k_bf", 64)
@@ -126,13 +134,18 @@ def tile_attend_x_ks_draft_kernel(tc, qT, kT, vT, ks, vs, pos, qpos, offs, out):
         nc.vector.tensor_copy(k_first[:, 1, :], k_pool[1][:].indirect(offsets[:]))
         for s in range(B):
             interleave(nc.scalar.copy, k_first, s, 0, 0, N)
-        vs_col = turn_table("vs", gather_table("vs"), 1, PACK, 1.0, 3)
-        k_last = keep.tile([P, HALF, B * N], F32, name="vs_table")
+        nks_col = turn_table("ks", gather_table("ks"), -1.0, 5)
+        k_last = keep.tile([P, HALF, B * N], F32, name="ks_table")
         nc.vector.tensor_copy(k_last[:, 0, :], k_pool[2][:].indirect(offsets[:]))
+        vs_got = gather_table("vs")
+        vs_col = per_seq([P, PACK], F32, "vs_col")
+        for s in range(B):
+            nc.sync.dma_start(vs_col[s][:], vs_got[0:1, seq(s)].rearrange("o (p t) -> o p t", t=PACK))
         for s in range(B):
             nc.vector.tensor_copy(k_last[:, 1, seq(s)], k_pool[3][:].indirect(list_of(s)))
-            interleave(nc.scalar.copy, k_last, s, HALF, 0, N)
-        nks_col = turn_table("ks", gather_table("ks"), P, 1, -1.0, 5)
+            interleave(nc.scalar.copy, k_last, s, HALF, VECTOR_COLS, N)
+        for s in range(B):
+            interleave(nc.vector.tensor_copy, k_last, s, HALF, 0, VECTOR_COLS)
 
         scaled = per_seq([P, CHUNKS, NQ], F32, "scaled")
         negmax = per_seq([P, 1], F32, "negmax")
@@ -142,7 +155,7 @@ def tile_attend_x_ks_draft_kernel(tc, qT, kT, vT, ks, vs, pos, qpos, offs, out):
         w_bf = per_seq([P, NQ, PACK], BF16, "w_bf", 64)
         w_codes = per_seq([P, NQ], U32, "w_codes", 64)
         w_scales = per_seq([P, NQ], U8, "w_scales", 64)
-        v_got = [per_seq([P, N], BF16, f"v_got{e}_") for e in range(E_BLOCKS)]
+        v_got = []
         v_bf = per_seq([P, DV * PACK], BF16, "v_bf", 64)
         v_codes = per_seq([P, DV], U32, "v_codes", 64)
         v_scales = per_seq([P, DV], U8, "v_scales", 64)
@@ -164,19 +177,18 @@ def tile_attend_x_ks_draft_kernel(tc, qT, kT, vT, ks, vs, pos, qpos, offs, out):
                 )
 
         def turn_scores(s):
-            ps = bank(3 + s)
             for c in range(CHUNKS):
-                kc = slice(c * P, (c + 1) * P)
-                nc.tensor.matmul(ps[:, kc], limit[s][:, c, :], ident[:], is_transpose=True, start=True, stop=False)
-                nc.tensor.matmul(ps[:, kc], scaled[s][:, c, :], ident[:], is_transpose=True, start=False, stop=True)
-            turned["score", s] = ps
+                nc.tensor.matmul(
+                    score[s][:, c * P : (c + 1) * P], scaled[s][:, c, :], ident[:],
+                    is_transpose=True, start=False, stop=c == CHUNKS - 1,
+                )
 
         def row_max(s):
-            nc.vector.tensor_reduce(negmax[s][:], turned["score", s][:], AXIS_X, ALU.min)
+            nc.vector.tensor_reduce(negmax[s][:], score[s][:], AXIS_X, ALU.min)
 
         def exponent(s):
             nc.scalar.activation(
-                prob[s][:].rearrange("q t i -> q i t"), turned["score", s][:].rearrange("q (i t) -> q i t", t=PACK),
+                prob[s][:], score[s][:].rearrange("q (i t) -> q t i", t=PACK),
                 ACT.Exp, bias=negmax[s][:], scale=-1.0, accum_out=total[s][:],
             )
 
@@ -197,12 +209,13 @@ def tile_attend_x_ks_draft_kernel(tc, qT, kT, vT, ks, vs, pos, qpos, offs, out):
                 out=w_codes[s][:].bitcast(FP8X4), scales=w_scales[s][:], in_=w_bf[s][:].rearrange("p q t -> p (q t)")
             )
 
-        def gather_v(e, s):
-            nc.vector.tensor_copy(v_got[e][s][:], v_pool[e][:].indirect(list_of(s)))
+        def gather_v(e):
+            v_got.append(keep.tile([P, B * N], BF16, name=f"k_bf{e}", align_bytes=64))
+            nc.vector.tensor_copy(v_got[e][:], v_pool[e][:].indirect(offsets[:]))
 
         def turn_v(e, s):
-            ps = bank(1 + B * e + s)
-            words = v_got[e][s][:].bitcast(F32)
+            ps = bank(1 + 4 * e + s)
+            words = v_got[e][:, seq(s)].bitcast(F32)
             for u in range(HALF):
                 nc.tensor.transpose(ps[:, u * P : (u + 1) * P], words[:, u : N // 2 : HALF], ident[:])
             place = v_bf[s][:].bitcast(F32)[:, e * P * HALF : (e + 1) * P * HALF]
@@ -215,7 +228,7 @@ def tile_attend_x_ks_draft_kernel(tc, qT, kT, vT, ks, vs, pos, qpos, offs, out):
             nc.vector.quantize_mx(out=v_codes[s][:].bitcast(FP8X4), scales=v_scales[s][:], in_=v_bf[s][:])
 
         def values(s):
-            ps = bank(5 + s)
+            ps = bank(1 + s)
             nc.tensor.matmul_mx(
                 out=ps[:, 0:DV], lhsT=w_codes[s][:].bitcast(FP8X4), lhsT_scale=w_scales[s][:],
                 rhs=v_codes[s][:].bitcast(FP8X4), rhs_scale=v_scales[s][:], start=True, stop=True,
@@ -227,18 +240,19 @@ def tile_attend_x_ks_draft_kernel(tc, qT, kT, vT, ks, vs, pos, qpos, offs, out):
             quantize_k(s)
             scores(s)
             turn_scores(s)
-            gather_v(0, s)
+        for e in range(E_BLOCKS):
+            gather_v(e)
         for s in range(B):
             row_max(s)
             exponent(s)
-            turn_v(0, s)
             turn_prob(s)
-            gather_v(1, s)
+        for e in range(E_BLOCKS):
+            for s in range(B):
+                turn_v(e, s)
         for s in range(B):
             weights(s)
-            turn_v(1, s)
             nc.vector.reciprocal(inv[s][:], total[s][:])
         for s in range(B):
-            quantize_w(s)
             quantize_v(s)
+            quantize_w(s)
             values(s)

@@ -15,12 +15,13 @@ AXIS_X = mybir.AxisListType.X
 
 B, NQ, D, DV, N, T = 2, 128, 512, 256, 512, 2048
 P = 128
+ROW = P - 1
 PACK = 4
 CHUNKS = N // P
 E_BLOCKS = DV // P
 MASKED = 1.0e30
 HALF = PACK // 2
-VECTOR_COLS = 256
+SCALAR_COLS = 256
 
 FLOPS = 2 * B * NQ * N * (D + DV)
 BYTES = 4 * (B * D * NQ + (D + DV) * T + 3 * T + B * NQ + B * NQ * DV) + 2 * P * (B * N // 16)
@@ -38,33 +39,32 @@ def tile_attend_x_ks_draft_kernel(tc, qT, kT, vT, ks, vs, pos, qpos, offs, out):
         def per_seq(shape, dtype, name, align=32):
             return [keep.tile(shape, dtype, name=f"{name}{s}", align_bytes=align) for s in range(B)]
 
-        def seq(s):
-            return slice(s * N, (s + 1) * N)
-
         offsets = keep.tile([P, B * N // 16], U16, name="offsets")
         nc.sync.dma_start(offsets[:], offs)
 
-        def list_of(s):
-            return offsets[:, s * (N // 16) : (s + 1) * (N // 16)]
+        def slots(a, z):
+            return offsets[:, a // 16 : z // 16]
+
+        def gather_vector(dst, window, a, z):
+            nc.vector.tensor_copy(dst, window[:].indirect(slots(a, z)))
+
+        def gather_scalar(dst, window, a, z):
+            nc.scalar.activation(dst, window[:].indirect(slots(a, z)), ACT.Copy)
 
         table = {}
-        for name in ("pos", "ks", "vs"):
+        for name, source in (("pos", pos), ("ks", ks), ("vs", vs)):
             table[name] = keep.tile([P, T], F32, name=name + "_table")
-            nc.vector.memset(table[name][:].bitcast(U32), 0)
+            nc.sync.dma_start(table[name][ROW:P, :], source[0:1, :])
+            nc.vector.memset(table[name][0:ROW, :].bitcast(U32), 0)
         q_place = keep.tile([P, B], F32, name="q_place")
         nc.scalar.dma_start(q_place[:], qpos.rearrange("b q o -> q (b o)"))
+        q_raw = keep.tile([P, B, PACK, NQ], F32, name="q_raw")
+        nc.sync.dma_start(q_raw[:], qT.rearrange("b (p t) q -> p b t q", t=PACK))
         k_rows = kT.rearrange("(p t) n -> p t n", t=PACK)
         k_pool = [keep.tile([P, T], F32, name=f"k_pool{t}") for t in range(PACK)]
         v_pool = [keep.tile([P, T], F32, name=f"v_pool{e}") for e in range(E_BLOCKS)]
-        q_raw = keep.tile([P, B, PACK, NQ], F32, name="q_raw")
-        nc.sync.dma_start(k_pool[0][:], k_rows[:, 0, :])
-        nc.sync.dma_start(table["pos"][0:1, :], pos[0:1, :])
-        nc.sync.dma_start(q_raw[:], qT.rearrange("b (p t) q -> p b t q", t=PACK))
-        nc.sync.dma_start(k_pool[1][:], k_rows[:, 1, :])
-        nc.sync.dma_start(table["ks"][0:1, :], ks[0:1, :])
-        nc.sync.dma_start(k_pool[2][:], k_rows[:, 2, :])
-        nc.sync.dma_start(table["vs"][0:1, :], vs[0:1, :])
-        nc.sync.dma_start(k_pool[3][:], k_rows[:, 3, :])
+        for t in range(PACK):
+            nc.sync.dma_start(k_pool[t][:], k_rows[:, t, :])
         for e in range(E_BLOCKS):
             nc.sync.dma_start(v_pool[e][:], vT[e * P : (e + 1) * P, :])
 
@@ -78,74 +78,77 @@ def tile_attend_x_ks_draft_kernel(tc, qT, kT, vT, ks, vs, pos, qpos, offs, out):
         for s in range(B):
             nc.tensor.transpose(q_row[:, s * NQ : (s + 1) * NQ], q_place[:, s : s + 1].to_broadcast([P, P]), ident[:])
 
-        q_bf = keep.tile([P, B, NQ, PACK], BF16, name="q_bf", align_bytes=64)
-        nc.scalar.copy(out=q_bf[:], in_=q_raw[:].rearrange("p b t q -> p b q t"))
-
-        def gather_table(name):
+        def gather_table(name, gather):
             got = keep.tile([P, B * N], F32, name=name + "_got")
-            nc.vector.tensor_copy(got[:], table[name][:].indirect(offsets[:]))
+            gather(got[:], table[name], 0, B * N)
             return got
 
-        def turn_table(name, got, scale, first_bank):
+        def turn_table(name, got, scale, first_bank, pick):
             col = per_seq([P, CHUNKS], F32, name + "_col")
             for s in range(B):
                 ps = bank(first_bank + s)
                 for c in range(CHUNKS):
-                    a = s * N + c * P
-                    nc.tensor.transpose(ps[:, c * P : (c + 1) * P], got[:, a : a + P], ident[:])
-                nc.scalar.activation(col[s][:], ps[:, 0 : 512 : P], ACT.Copy, scale=scale)
+                    nc.tensor.transpose(ps[:, c * P : (c + 1) * P], got[:, pick(s, c)], ident[:])
+                nc.vector.tensor_scalar(col[s][:], ps[:, ROW:512:P], scale, None, ALU.mult)
             return col
 
-        pos_col = turn_table("pos", gather_table("pos"), 1.0, 1)
-        ahead = per_seq([P, CHUNKS, NQ], F32, "ahead")
+        def chunk(s, c):
+            return slice(s * N + c * P, s * N + (c + 1) * P)
+
+        def dealt(s, t):
+            return slice(s * N + t, (s + 1) * N, PACK)
+
+        pos_got = gather_table("pos", gather_scalar)
+        ks_got = gather_table("ks", gather_scalar)
+
+        q_bf = keep.tile([P, B, NQ, PACK], BF16, name="q_bf", align_bytes=64)
+        nc.vector.tensor_copy(out=q_bf[:], in_=q_raw[:].rearrange("p b t q -> p b q t"))
+        vs_got = gather_table("vs", gather_vector)
+        q_codes = keep.tile([P, B * NQ], U32, name="q_codes", align_bytes=64)
+        q_scales = keep.tile([P, B * NQ], U8, name="q_scales", align_bytes=64)
+        nc.vector.quantize_mx(
+            out=q_codes[:].bitcast(FP8X4), scales=q_scales[:], in_=q_bf[:].rearrange("p b q t -> p (b q t)")
+        )
+
+        pos_col = turn_table("pos", pos_got, 1.0, 1, chunk)
         limit = per_seq([P, CHUNKS, NQ], F32, "limit")
         for s in range(B):
             for c in range(CHUNKS):
-                nc.scalar.activation(
-                    ahead[s][:, c, :], q_row[:, s * NQ : (s + 1) * NQ], ACT.Sign, bias=pos_col[s][:, c : c + 1], scale=-1.0
+                nc.vector.tensor_scalar(
+                    limit[s][:, c, :], q_row[:, s * NQ : (s + 1) * NQ], pos_col[s][:, c : c + 1], MASKED, ALU.is_lt, ALU.mult
                 )
-            nc.scalar.activation(limit[s][:], ahead[s][:], ACT.Relu, scale=MASKED)
+        nks_col = turn_table("ks", ks_got, -1.0, 5, chunk)
         score = [bank(3 + s) for s in range(B)]
         for s in range(B):
             for c in range(CHUNKS):
                 nc.tensor.matmul(
                     score[s][:, c * P : (c + 1) * P], limit[s][:, c, :], ident[:], is_transpose=True, start=c == 0, stop=False
                 )
+        vs_col = turn_table("vs", vs_got, 1.0, 1, dealt)
 
-        k_first = keep.tile([P, HALF, B * N], F32, name="pos_table")
+        k_first = keep.tile([P, HALF, B * N], BF16, name="k_first")
+        k_last = per_seq([P, HALF, N], BF16, "k_last")
         k_bf = per_seq([P, N, PACK], BF16, "k_bf", 64)
         k_codes = per_seq([P, N], U32, "k_codes", 64)
         k_scales = per_seq([P, N], U8, "k_scales", 64)
 
         def interleave(copy, got, s, t, a, z):
-            copy(out=k_bf[s][:, a:z, t : t + HALF], in_=got[:, :, s * N + a : s * N + z].rearrange("p t n -> p n t"))
+            copy(out=k_bf[s][:, a:z, t : t + HALF], in_=got[:, :, a:z].rearrange("p t n -> p n t"))
 
         def quantize_k(s):
             nc.vector.quantize_mx(
                 out=k_codes[s][:].bitcast(FP8X4), scales=k_scales[s][:], in_=k_bf[s][:].rearrange("p n t -> p (n t)")
             )
 
-        nc.vector.tensor_copy(k_first[:, 0, :], k_pool[0][:].indirect(offsets[:]))
-        q_codes = keep.tile([P, B * NQ], U32, name="q_codes", align_bytes=64)
-        q_scales = keep.tile([P, B * NQ], U8, name="q_scales", align_bytes=64)
-        nc.vector.quantize_mx(
-            out=q_codes[:].bitcast(FP8X4), scales=q_scales[:], in_=q_bf[:].rearrange("p b q t -> p (b q t)")
-        )
-        nc.vector.tensor_copy(k_first[:, 1, :], k_pool[1][:].indirect(offsets[:]))
+        for t in range(HALF):
+            gather_scalar(k_first[:, t, :], k_pool[t], 0, B * N)
         for s in range(B):
-            interleave(nc.scalar.copy, k_first, s, 0, 0, N)
-        nks_col = turn_table("ks", gather_table("ks"), -1.0, 5)
-        k_last = keep.tile([P, HALF, B * N], F32, name="ks_table")
-        nc.vector.tensor_copy(k_last[:, 0, :], k_pool[2][:].indirect(offsets[:]))
-        vs_got = gather_table("vs")
-        vs_col = per_seq([P, PACK], F32, "vs_col")
+            interleave(nc.vector.tensor_copy, k_first[:, :, s * N : (s + 1) * N], s, 0, 0, N)
         for s in range(B):
-            nc.sync.dma_start(vs_col[s][:], vs_got[0:1, seq(s)].rearrange("o (p t) -> o p t", t=PACK))
-        for s in range(B):
-            nc.vector.tensor_copy(k_last[:, 1, seq(s)], k_pool[3][:].indirect(list_of(s)))
-            interleave(nc.scalar.copy, k_last, s, HALF, VECTOR_COLS, N)
-        for s in range(B):
-            interleave(nc.vector.tensor_copy, k_last, s, HALF, 0, VECTOR_COLS)
+            gather_scalar(k_last[s][:, 0, :], k_pool[2], s * N, (s + 1) * N)
+        gather_vector(k_last[0][:, 1, 0 : N // 2], k_pool[3], 0, N // 2)
+        gather_scalar(k_last[0][:, 1, N // 2 : N], k_pool[3], N // 2, N)
+        gather_scalar(k_last[1][:, 1, :], k_pool[3], N, 2 * N)
 
         scaled = per_seq([P, CHUNKS, NQ], F32, "scaled")
         negmax = per_seq([P, 1], F32, "negmax")
@@ -155,7 +158,7 @@ def tile_attend_x_ks_draft_kernel(tc, qT, kT, vT, ks, vs, pos, qpos, offs, out):
         w_bf = per_seq([P, NQ, PACK], BF16, "w_bf", 64)
         w_codes = per_seq([P, NQ], U32, "w_codes", 64)
         w_scales = per_seq([P, NQ], U8, "w_scales", 64)
-        v_got = []
+        v_got = [per_seq([P, N], BF16, f"v_got{e}_") for e in range(E_BLOCKS)]
         v_bf = per_seq([P, DV * PACK], BF16, "v_bf", 64)
         v_codes = per_seq([P, DV], U32, "v_codes", 64)
         v_scales = per_seq([P, DV], U8, "v_scales", 64)
@@ -209,13 +212,12 @@ def tile_attend_x_ks_draft_kernel(tc, qT, kT, vT, ks, vs, pos, qpos, offs, out):
                 out=w_codes[s][:].bitcast(FP8X4), scales=w_scales[s][:], in_=w_bf[s][:].rearrange("p q t -> p (q t)")
             )
 
-        def gather_v(e):
-            v_got.append(keep.tile([P, B * N], BF16, name=f"k_bf{e}", align_bytes=64))
-            nc.vector.tensor_copy(v_got[e][:], v_pool[e][:].indirect(offsets[:]))
+        def gather_v(e, s, gather):
+            gather(v_got[e][s][:], v_pool[e], s * N, (s + 1) * N)
 
         def turn_v(e, s):
-            ps = bank(1 + 4 * e + s)
-            words = v_got[e][:, seq(s)].bitcast(F32)
+            ps = bank(5 - 4 * e + s)
+            words = v_got[e][s][:].bitcast(F32)
             for u in range(HALF):
                 nc.tensor.transpose(ps[:, u * P : (u + 1) * P], words[:, u : N // 2 : HALF], ident[:])
             place = v_bf[s][:].bitcast(F32)[:, e * P * HALF : (e + 1) * P * HALF]
@@ -228,7 +230,7 @@ def tile_attend_x_ks_draft_kernel(tc, qT, kT, vT, ks, vs, pos, qpos, offs, out):
             nc.vector.quantize_mx(out=v_codes[s][:].bitcast(FP8X4), scales=v_scales[s][:], in_=v_bf[s][:])
 
         def values(s):
-            ps = bank(1 + s)
+            ps = bank(3 + s)
             nc.tensor.matmul_mx(
                 out=ps[:, 0:DV], lhsT=w_codes[s][:].bitcast(FP8X4), lhsT_scale=w_scales[s][:],
                 rhs=v_codes[s][:].bitcast(FP8X4), rhs_scale=v_scales[s][:], start=True, stop=True,
@@ -236,23 +238,29 @@ def tile_attend_x_ks_draft_kernel(tc, qT, kT, vT, ks, vs, pos, qpos, offs, out):
             nc.scalar.activation(result[s][:], ps[:, 0:DV], ACT.Copy, scale=inv[s][:])
             nc.sync.dma_start(out[s], result[s][:])
 
-        for s in range(B):
-            quantize_k(s)
-            scores(s)
-            turn_scores(s)
-        for e in range(E_BLOCKS):
-            gather_v(e)
+        interleave(nc.vector.tensor_copy, k_last[0], 0, HALF, 0, N)
+        interleave(nc.scalar.copy, k_last[1], 1, HALF, 0, SCALAR_COLS)
+        quantize_k(0)
+        interleave(nc.vector.tensor_copy, k_last[1], 1, HALF, SCALAR_COLS, N)
+        scores(0)
+        turn_scores(0)
+        quantize_k(1)
+        scores(1)
+        turn_scores(1)
         for s in range(B):
             row_max(s)
             exponent(s)
             turn_prob(s)
+        for s in range(B):
+            weights(s)
+            nc.vector.reciprocal(inv[s][:], total[s][:])
+            quantize_w(s)
+        for e in range(E_BLOCKS):
+            gather_v(e, 0, gather_scalar)
+            gather_v(e, 1, gather_vector)
         for e in range(E_BLOCKS):
             for s in range(B):
                 turn_v(e, s)
         for s in range(B):
-            weights(s)
-            nc.vector.reciprocal(inv[s][:], total[s][:])
-        for s in range(B):
             quantize_v(s)
-            quantize_w(s)
             values(s)

@@ -21,7 +21,8 @@ CHUNKS = N // P
 E_BLOCKS = DV // P
 MASKED = 1.0e30
 HALF = PACK // 2
-SCALAR_COLS = 256
+VECTOR_SLOTS = 256
+SHIFT = 16
 
 FLOPS = 2 * B * NQ * N * (D + DV)
 BYTES = 4 * (B * D * NQ + (D + DV) * T + 3 * T + B * NQ + B * NQ * DV) + 2 * P * (B * N // 16)
@@ -83,14 +84,16 @@ def tile_attend_x_ks_draft_kernel(tc, qT, kT, vT, ks, vs, pos, qpos, offs, out):
             gather(got[:], table[name], 0, B * N)
             return got
 
-        def turn_table(name, got, scale, first_bank, pick):
-            col = per_seq([P, CHUNKS], F32, name + "_col")
-            for s in range(B):
-                ps = bank(first_bank + s)
-                for c in range(CHUNKS):
-                    nc.tensor.transpose(ps[:, c * P : (c + 1) * P], got[:, pick(s, c)], ident[:])
-                nc.vector.tensor_scalar(col[s][:], ps[:, ROW:512:P], scale, None, ALU.mult)
-            return col
+        def turn_table(got, index, pick):
+            ps = bank(index)
+            for j in reversed(range(B * CHUNKS)):
+                nc.tensor.transpose(ps[:, j * SHIFT : j * SHIFT + P], got[:, pick(j // CHUNKS, j % CHUNKS)], ident[:])
+            return ps[:, ROW : ROW + B * CHUNKS * SHIFT : SHIFT]
+
+        def keep_columns(name, columns):
+            col = keep.tile([P, B * CHUNKS], F32, name=name + "_col")
+            nc.vector.tensor_copy(col[:], columns)
+            return [col[:, s * CHUNKS : (s + 1) * CHUNKS] for s in range(B)]
 
         def chunk(s, c):
             return slice(s * N + c * P, s * N + (c + 1) * P)
@@ -100,6 +103,8 @@ def tile_attend_x_ks_draft_kernel(tc, qT, kT, vT, ks, vs, pos, qpos, offs, out):
 
         pos_got = gather_table("pos", gather_scalar)
         ks_got = gather_table("ks", gather_scalar)
+        q_row_sb = keep.tile([P, B * NQ], F32, name="q_row_sb")
+        nc.scalar.copy(out=q_row_sb[:], in_=q_row[:, 0 : B * NQ])
 
         q_bf = keep.tile([P, B, NQ, PACK], BF16, name="q_bf", align_bytes=64)
         nc.vector.tensor_copy(out=q_bf[:], in_=q_raw[:].rearrange("p b t q -> p b q t"))
@@ -110,24 +115,25 @@ def tile_attend_x_ks_draft_kernel(tc, qT, kT, vT, ks, vs, pos, qpos, offs, out):
             out=q_codes[:].bitcast(FP8X4), scales=q_scales[:], in_=q_bf[:].rearrange("p b q t -> p (b q t)")
         )
 
-        pos_col = turn_table("pos", pos_got, 1.0, 1, chunk)
+        pos_col = turn_table(pos_got, 1, chunk)
         limit = per_seq([P, CHUNKS, NQ], F32, "limit")
         for s in range(B):
             for c in range(CHUNKS):
                 nc.vector.tensor_scalar(
-                    limit[s][:, c, :], q_row[:, s * NQ : (s + 1) * NQ], pos_col[s][:, c : c + 1], MASKED, ALU.is_lt, ALU.mult
+                    limit[s][:, c, :], q_row_sb[:, s * NQ : (s + 1) * NQ], pos_col[:, s * CHUNKS + c : s * CHUNKS + c + 1],
+                    -MASKED, ALU.is_lt, ALU.mult,
                 )
-        nks_col = turn_table("ks", ks_got, -1.0, 5, chunk)
         score = [bank(3 + s) for s in range(B)]
         for s in range(B):
             for c in range(CHUNKS):
                 nc.tensor.matmul(
                     score[s][:, c * P : (c + 1) * P], limit[s][:, c, :], ident[:], is_transpose=True, start=c == 0, stop=False
                 )
-        vs_col = turn_table("vs", vs_got, 1.0, 1, dealt)
+        vs_col = keep_columns("vs", turn_table(vs_got, 2, dealt))
+        ks_col = keep_columns("ks", turn_table(ks_got, 5, chunk))
 
-        k_first = keep.tile([P, HALF, B * N], BF16, name="k_first")
-        k_last = per_seq([P, HALF, N], BF16, "k_last")
+        k_first = keep.tile([P, HALF, B * N], F32, name="k_first")
+        k_last = per_seq([P, HALF, N], F32, "k_last")
         k_bf = per_seq([P, N, PACK], BF16, "k_bf", 64)
         k_codes = per_seq([P, N], U32, "k_codes", 64)
         k_scales = per_seq([P, N], U8, "k_scales", 64)
@@ -140,25 +146,24 @@ def tile_attend_x_ks_draft_kernel(tc, qT, kT, vT, ks, vs, pos, qpos, offs, out):
                 out=k_codes[s][:].bitcast(FP8X4), scales=k_scales[s][:], in_=k_bf[s][:].rearrange("p n t -> p (n t)")
             )
 
-        for t in range(HALF):
-            gather_scalar(k_first[:, t, :], k_pool[t], 0, B * N)
+        gather_scalar(k_first[:, 0, :], k_pool[0], 0, B * N)
+        gather_scalar(k_first[:, 1, :], k_pool[1], 0, B * N)
         for s in range(B):
             interleave(nc.vector.tensor_copy, k_first[:, :, s * N : (s + 1) * N], s, 0, 0, N)
         for s in range(B):
             gather_scalar(k_last[s][:, 0, :], k_pool[2], s * N, (s + 1) * N)
-        gather_vector(k_last[0][:, 1, 0 : N // 2], k_pool[3], 0, N // 2)
-        gather_scalar(k_last[0][:, 1, N // 2 : N], k_pool[3], N // 2, N)
-        gather_scalar(k_last[1][:, 1, :], k_pool[3], N, 2 * N)
+        gather_vector(k_last[0][:, 1, :], k_pool[3], 0, N)
+        gather_scalar(k_last[1][:, 1, :], k_pool[3], N, B * N)
 
-        scaled = per_seq([P, CHUNKS, NQ], F32, "scaled")
-        negmax = per_seq([P, 1], F32, "negmax")
+        scaled = per_seq([P, CHUNKS, NQ], F32, "scaled", 64)
+        negmax = per_seq([P, 1], F32, "negmax", 64)
         total = per_seq([P, 1], F32, "total")
         inv = per_seq([P, 1], F32, "inv")
         prob = per_seq([P, PACK, P], F32, "prob")
         w_bf = per_seq([P, NQ, PACK], BF16, "w_bf", 64)
         w_codes = per_seq([P, NQ], U32, "w_codes", 64)
         w_scales = per_seq([P, NQ], U8, "w_scales", 64)
-        v_got = [per_seq([P, N], BF16, f"v_got{e}_") for e in range(E_BLOCKS)]
+        v_got = {}
         v_bf = per_seq([P, DV * PACK], BF16, "v_bf", 64)
         v_codes = per_seq([P, DV], U32, "v_codes", 64)
         v_scales = per_seq([P, DV], U8, "v_scales", 64)
@@ -176,7 +181,7 @@ def tile_attend_x_ks_draft_kernel(tc, qT, kT, vT, ks, vs, pos, qpos, offs, out):
                 )
             for c in range(CHUNKS):
                 nc.scalar.activation(
-                    scaled[s][:, c, :], ps[:, c * P : (c + 1) * P], ACT.Copy, scale=nks_col[s][:, c : c + 1]
+                    scaled[s][:, c, :], ps[:, c * P : (c + 1) * P], ACT.Copy, scale=ks_col[s][:, c : c + 1]
                 )
 
         def turn_scores(s):
@@ -187,12 +192,12 @@ def tile_attend_x_ks_draft_kernel(tc, qT, kT, vT, ks, vs, pos, qpos, offs, out):
                 )
 
         def row_max(s):
-            nc.vector.tensor_reduce(negmax[s][:], score[s][:], AXIS_X, ALU.min)
+            nc.vector.tensor_reduce(negmax[s][:], score[s][:], AXIS_X, ALU.max, negate=True)
 
         def exponent(s):
             nc.scalar.activation(
                 prob[s][:], score[s][:].rearrange("q (i t) -> q t i", t=PACK),
-                ACT.Exp, bias=negmax[s][:], scale=-1.0, accum_out=total[s][:],
+                ACT.Exp, bias=negmax[s][:], accum_out=total[s][:],
             )
 
         def turn_prob(s):
@@ -204,7 +209,7 @@ def tile_attend_x_ks_draft_kernel(tc, qT, kT, vT, ks, vs, pos, qpos, offs, out):
         def weights(s):
             nc.vector.tensor_tensor(
                 w_bf[s][:], turned["prob", s][:].rearrange("p (t q) -> p q t", t=PACK),
-                vs_col[s][:].unsqueeze(1).to_broadcast([P, NQ, PACK]), ALU.mult,
+                vs_col[s].unsqueeze(1).to_broadcast([P, NQ, PACK]), ALU.mult,
             )
 
         def quantize_w(s):
@@ -212,12 +217,16 @@ def tile_attend_x_ks_draft_kernel(tc, qT, kT, vT, ks, vs, pos, qpos, offs, out):
                 out=w_codes[s][:].bitcast(FP8X4), scales=w_scales[s][:], in_=w_bf[s][:].rearrange("p q t -> p (q t)")
             )
 
-        def gather_v(e, s, gather):
-            gather(v_got[e][s][:], v_pool[e], s * N, (s + 1) * N)
+        def gather_v(e, s, name, on_vector):
+            v_got[e, s] = keep.tile([P, N], BF16, name=name, align_bytes=64)
+            if on_vector > 0:
+                gather_vector(v_got[e, s][:, 0:on_vector], v_pool[e], s * N, s * N + on_vector)
+            if on_vector < N:
+                gather_scalar(v_got[e, s][:, on_vector:N], v_pool[e], s * N + on_vector, (s + 1) * N)
 
         def turn_v(e, s):
             ps = bank(5 - 4 * e + s)
-            words = v_got[e][s][:].bitcast(F32)
+            words = v_got[e, s][:].bitcast(F32)
             for u in range(HALF):
                 nc.tensor.transpose(ps[:, u * P : (u + 1) * P], words[:, u : N // 2 : HALF], ident[:])
             place = v_bf[s][:].bitcast(F32)[:, e * P * HALF : (e + 1) * P * HALF]
@@ -238,15 +247,12 @@ def tile_attend_x_ks_draft_kernel(tc, qT, kT, vT, ks, vs, pos, qpos, offs, out):
             nc.scalar.activation(result[s][:], ps[:, 0:DV], ACT.Copy, scale=inv[s][:])
             nc.sync.dma_start(out[s], result[s][:])
 
-        interleave(nc.vector.tensor_copy, k_last[0], 0, HALF, 0, N)
-        interleave(nc.scalar.copy, k_last[1], 1, HALF, 0, SCALAR_COLS)
-        quantize_k(0)
-        interleave(nc.vector.tensor_copy, k_last[1], 1, HALF, SCALAR_COLS, N)
-        scores(0)
-        turn_scores(0)
-        quantize_k(1)
-        scores(1)
-        turn_scores(1)
+        for s in range(B):
+            interleave(nc.vector.tensor_copy, k_last[s], s, HALF, 0, N)
+        for s in range(B):
+            quantize_k(s)
+            scores(s)
+            turn_scores(s)
         for s in range(B):
             row_max(s)
             exponent(s)
@@ -255,9 +261,10 @@ def tile_attend_x_ks_draft_kernel(tc, qT, kT, vT, ks, vs, pos, qpos, offs, out):
             weights(s)
             nc.vector.reciprocal(inv[s][:], total[s][:])
             quantize_w(s)
-        for e in range(E_BLOCKS):
-            gather_v(e, 0, gather_scalar)
-            gather_v(e, 1, gather_vector)
+        gather_v(0, 0, "v_got0", 0)
+        gather_v(0, 1, "k_bf1", N)
+        gather_v(1, 0, "v_got1", VECTOR_SLOTS)
+        gather_v(1, 1, "scaled1", N)
         for e in range(E_BLOCKS):
             for s in range(B):
                 turn_v(e, s)

@@ -11,17 +11,18 @@ U8 = mybir.dt.uint8
 FP8X4 = mybir.dt.float8_e4m3fn_x4
 ALU = mybir.AluOpType
 ACT = mybir.ActivationFunctionType
-AXIS_X = mybir.AxisListType.X
 
 B, NQ, D, DV, N, T = 2, 128, 512, 256, 512, 2048
 P = 128
 ROW = P - 1
 PACK = 4
+PAIR = PACK // 2
 CHUNKS = N // P
+HALVES = 2
+H = N // HALVES
+PARTS = B * HALVES
 E_BLOCKS = DV // P
 MASKED = 1.0e30
-HALF = PACK // 2
-VECTOR_SLOTS = 256
 SHIFT = 16
 
 FLOPS = 2 * B * NQ * N * (D + DV)
@@ -37,20 +38,17 @@ def tile_attend_x_ks_draft_kernel(tc, qT, kT, vT, ks, vs, pos, qpos, offs, out):
         def bank(index):
             return psum.tile([P, 512], F32, name=f"bank{index}")
 
-        def per_seq(shape, dtype, name, align=32):
-            return [keep.tile(shape, dtype, name=f"{name}{s}", align_bytes=align) for s in range(B)]
+        def tiles(count, shape, dtype, name):
+            return [keep.tile(shape, dtype, name=f"{name}{i}", align_bytes=64) for i in range(count)]
 
         offsets = keep.tile([P, B * N // 16], U16, name="offsets")
         nc.sync.dma_start(offsets[:], offs)
 
-        def slots(a, z):
-            return offsets[:, a // 16 : z // 16]
-
         def gather_vector(dst, window, a, z):
-            nc.vector.tensor_copy(dst, window[:].indirect(slots(a, z)))
+            nc.vector.tensor_copy(dst, window[:].indirect(offsets[:, a // 16 : z // 16]))
 
         def gather_scalar(dst, window, a, z):
-            nc.scalar.activation(dst, window[:].indirect(slots(a, z)), ACT.Copy)
+            nc.scalar.activation(dst, window[:].indirect(offsets[:, a // 16 : z // 16]), ACT.Copy)
 
         table = {}
         for name, source in (("pos", pos), ("ks", ks), ("vs", vs)):
@@ -59,11 +57,16 @@ def tile_attend_x_ks_draft_kernel(tc, qT, kT, vT, ks, vs, pos, qpos, offs, out):
             nc.vector.memset(table[name][0:ROW, :].bitcast(U32), 0)
         q_place = keep.tile([P, B], F32, name="q_place")
         nc.scalar.dma_start(q_place[:], qpos.rearrange("b q o -> q (b o)"))
-        q_raw = keep.tile([P, B, PACK, NQ], F32, name="q_raw")
-        nc.sync.dma_start(q_raw[:], qT.rearrange("b (p t) q -> p b t q", t=PACK))
+        q_raw = tiles(B, [P, PACK, NQ], F32, "q_raw")
         k_rows = kT.rearrange("(p t) n -> p t n", t=PACK)
-        k_pool = [keep.tile([P, T], F32, name=f"k_pool{t}") for t in range(PACK)]
-        v_pool = [keep.tile([P, T], F32, name=f"v_pool{e}") for e in range(E_BLOCKS)]
+        k_pool = tiles(PACK, [P, T], F32, "k_pool")
+        v_pool = tiles(E_BLOCKS, [P, T], F32, "v_pool")
+
+        def load_q(s):
+            nc.sync.dma_start(q_raw[s][:], qT[s].rearrange("(p t) q -> p t q", t=PACK))
+
+        for s in range(B):
+            load_q(s)
         for t in range(PACK):
             nc.sync.dma_start(k_pool[t][:], k_rows[:, t, :])
         for e in range(E_BLOCKS):
@@ -75,7 +78,7 @@ def tile_attend_x_ks_draft_kernel(tc, qT, kT, vT, ks, vs, pos, qpos, offs, out):
         ident = keep.tile([P, P], F32, name="ident")
         make_identity(nc, ident[:])
 
-        q_row = bank(0)
+        q_row = bank(4)
         for s in range(B):
             nc.tensor.transpose(q_row[:, s * NQ : (s + 1) * NQ], q_place[:, s : s + 1].to_broadcast([P, P]), ident[:])
 
@@ -90,10 +93,10 @@ def tile_attend_x_ks_draft_kernel(tc, qT, kT, vT, ks, vs, pos, qpos, offs, out):
                 nc.tensor.transpose(ps[:, j * SHIFT : j * SHIFT + P], got[:, pick(j // CHUNKS, j % CHUNKS)], ident[:])
             return ps[:, ROW : ROW + B * CHUNKS * SHIFT : SHIFT]
 
-        def keep_columns(name, columns):
+        def keep_columns(name, columns, scale):
             col = keep.tile([P, B * CHUNKS], F32, name=name + "_col")
-            nc.vector.tensor_copy(col[:], columns)
-            return [col[:, s * CHUNKS : (s + 1) * CHUNKS] for s in range(B)]
+            nc.vector.tensor_scalar(col[:], columns, scale, None, ALU.mult)
+            return col
 
         def chunk(s, c):
             return slice(s * N + c * P, s * N + (c + 1) * P)
@@ -101,121 +104,145 @@ def tile_attend_x_ks_draft_kernel(tc, qT, kT, vT, ks, vs, pos, qpos, offs, out):
         def dealt(s, t):
             return slice(s * N + t, (s + 1) * N, PACK)
 
-        pos_got = gather_table("pos", gather_scalar)
-        ks_got = gather_table("ks", gather_scalar)
-        q_row_sb = keep.tile([P, B * NQ], F32, name="q_row_sb")
-        nc.scalar.copy(out=q_row_sb[:], in_=q_row[:, 0 : B * NQ])
+        q_bf = tiles(B, [P, NQ, PACK], BF16, "q_bf")
+        q_codes = tiles(B, [P, NQ], U32, "q_codes")
+        q_scales = tiles(B, [P, NQ], U8, "q_scales")
 
-        q_bf = keep.tile([P, B, NQ, PACK], BF16, name="q_bf", align_bytes=64)
-        nc.vector.tensor_copy(out=q_bf[:], in_=q_raw[:].rearrange("p b t q -> p b q t"))
-        vs_got = gather_table("vs", gather_vector)
-        q_codes = keep.tile([P, B * NQ], U32, name="q_codes", align_bytes=64)
-        q_scales = keep.tile([P, B * NQ], U8, name="q_scales", align_bytes=64)
-        nc.vector.quantize_mx(
-            out=q_codes[:].bitcast(FP8X4), scales=q_scales[:], in_=q_bf[:].rearrange("p b q t -> p (b q t)")
-        )
+        def interleave_q(s, copy):
+            copy(out=q_bf[s][:], in_=q_raw[s][:].rearrange("p t q -> p q t"))
 
-        pos_col = turn_table(pos_got, 1, chunk)
-        limit = per_seq([P, CHUNKS, NQ], F32, "limit")
-        for s in range(B):
-            for c in range(CHUNKS):
+        def quantize(codes, scales, values):
+            nc.vector.quantize_mx(out=codes[:].bitcast(FP8X4), scales=scales[:], in_=values)
+
+        def quantize_q(s):
+            quantize(q_codes[s], q_scales[s], q_bf[s][:].rearrange("p q t -> p (q t)"))
+
+        limit = tiles(B * CHUNKS, [P, NQ], F32, "limit")
+        score = [bank(i) for i in range(PARTS)]
+
+        def build_masks(pos_got):
+            q_row_sb = keep.tile([P, B * NQ], F32, name="q_row_sb")
+            nc.scalar.copy(out=q_row_sb[:], in_=q_row[:, 0 : B * NQ])
+            pos_col = turn_table(pos_got, 5, chunk)
+            for j in range(B * CHUNKS):
+                s = j // CHUNKS
                 nc.vector.tensor_scalar(
-                    limit[s][:, c, :], q_row_sb[:, s * NQ : (s + 1) * NQ], pos_col[:, s * CHUNKS + c : s * CHUNKS + c + 1],
-                    -MASKED, ALU.is_lt, ALU.mult,
+                    limit[j][:], q_row_sb[:, s * NQ : (s + 1) * NQ], pos_col[:, j : j + 1], MASKED, ALU.is_lt, ALU.mult
                 )
-        score = [bank(3 + s) for s in range(B)]
-        for s in range(B):
-            for c in range(CHUNKS):
+                c = j % 2
                 nc.tensor.matmul(
-                    score[s][:, c * P : (c + 1) * P], limit[s][:, c, :], ident[:], is_transpose=True, start=c == 0, stop=False
+                    score[j // 2][:, c * P : (c + 1) * P], limit[j][:], ident[:], is_transpose=True, start=c == 0, stop=False
                 )
-        vs_col = keep_columns("vs", turn_table(vs_got, 2, dealt))
-        ks_col = keep_columns("ks", turn_table(ks_got, 5, chunk))
 
-        k_first = keep.tile([P, HALF, B * N], F32, name="k_first")
-        k_last = per_seq([P, HALF, N], F32, "k_last")
-        k_bf = per_seq([P, N, PACK], BF16, "k_bf", 64)
-        k_codes = per_seq([P, N], U32, "k_codes", 64)
-        k_scales = per_seq([P, N], U8, "k_scales", 64)
+        k_first = keep.tile([P, PAIR, B * N], BF16, name="k_first")
+        k_last = tiles(PARTS, [P, PAIR, H], BF16, "k_last")
+        k_bf = tiles(PARTS, [P, H, PACK], BF16, "k_bf")
+        k_codes = tiles(PARTS, [P, H], U32, "k_codes")
+        k_scales = tiles(PARTS, [P, H], U8, "k_scales")
 
-        def interleave(copy, got, s, t, a, z):
-            copy(out=k_bf[s][:, a:z, t : t + HALF], in_=got[:, :, a:z].rearrange("p t n -> p n t"))
+        def gather_first(t, gather, a, z):
+            gather(k_first[:, t, a:z], k_pool[t], a, z)
 
-        def quantize_k(s):
-            nc.vector.quantize_mx(
-                out=k_codes[s][:].bitcast(FP8X4), scales=k_scales[s][:], in_=k_bf[s][:].rearrange("p n t -> p (n t)")
+        def gather_last(t, i, gather):
+            gather(k_last[i][:, t - PAIR, :], k_pool[t], i * H, (i + 1) * H)
+
+        def interleave_first(i):
+            nc.vector.tensor_copy(
+                out=k_bf[i][:, :, 0:PAIR], in_=k_first[:, :, i * H : (i + 1) * H].rearrange("p t n -> p n t")
             )
 
-        gather_scalar(k_first[:, 0, :], k_pool[0], 0, B * N)
-        gather_scalar(k_first[:, 1, :], k_pool[1], 0, B * N)
-        for s in range(B):
-            interleave(nc.vector.tensor_copy, k_first[:, :, s * N : (s + 1) * N], s, 0, 0, N)
-        for s in range(B):
-            gather_scalar(k_last[s][:, 0, :], k_pool[2], s * N, (s + 1) * N)
-        gather_vector(k_last[0][:, 1, :], k_pool[3], 0, N)
-        gather_scalar(k_last[1][:, 1, :], k_pool[3], N, B * N)
+        def interleave_last(i):
+            nc.vector.tensor_copy(out=k_bf[i][:, :, PAIR:PACK], in_=k_last[i][:].rearrange("p t n -> p n t"))
 
-        scaled = per_seq([P, CHUNKS, NQ], F32, "scaled", 64)
-        negmax = per_seq([P, 1], F32, "negmax", 64)
-        total = per_seq([P, 1], F32, "total")
-        inv = per_seq([P, 1], F32, "inv")
-        prob = per_seq([P, PACK, P], F32, "prob")
-        w_bf = per_seq([P, NQ, PACK], BF16, "w_bf", 64)
-        w_codes = per_seq([P, NQ], U32, "w_codes", 64)
-        w_scales = per_seq([P, NQ], U8, "w_scales", 64)
+        def quantize_k(i):
+            quantize(k_codes[i], k_scales[i], k_bf[i][:].rearrange("p n t -> p (n t)"))
+
+        pos_got = gather_table("pos", gather_scalar)
+        for s in range(B):
+            interleave_q(s, nc.vector.tensor_copy)
+        ks_got = gather_table("ks", gather_vector)
+        for s in range(B):
+            quantize_q(s)
+        build_masks(pos_got)
+        vs_got = gather_table("vs", gather_vector)
+        nks_col = keep_columns("ks", turn_table(ks_got, 6, chunk), -1.0)
+        gather_first(0, gather_scalar, 0, B * N)
+        gather_first(1, gather_scalar, 0, N)
+        gather_first(1, gather_vector, N, B * N)
+        for i in range(PARTS):
+            interleave_first(i)
+        vs_col = keep_columns("vs", turn_table(vs_got, 7, dealt), 1.0)
+        for i in range(PARTS):
+            gather_last(2, i, gather_scalar if i < PARTS - 1 else gather_vector)
+        for i in range(PARTS):
+            gather_last(3, i, gather_scalar if i > 0 else gather_vector)
+
+        scaled = tiles(B * CHUNKS, [P, NQ], F32, "scaled")
+        lowest = tiles(PARTS, [P, 1], F32, "lowest")
+        kept = tiles(B, [P, N], F32, "kept")
+        sums = tiles(B, [P, PAIR], F32, "sums")
+        total = tiles(B, [P, 1], F32, "total")
+        inv = tiles(B, [P, 1], F32, "inv")
+        prob = tiles(B * PAIR, [P, PAIR, P], F32, "prob")
+        w_bf = tiles(B, [P, NQ, PACK], BF16, "w_bf")
+        w_codes = tiles(B, [P, NQ], U32, "w_codes")
+        w_scales = tiles(B, [P, NQ], U8, "w_scales")
         v_got = {}
-        v_bf = per_seq([P, DV * PACK], BF16, "v_bf", 64)
-        v_codes = per_seq([P, DV], U32, "v_codes", 64)
-        v_scales = per_seq([P, DV], U8, "v_scales", 64)
-        result = per_seq([P, DV], F32, "result")
+        v_bf = tiles(B, [P, DV * PACK], BF16, "v_bf")
+        v_codes = tiles(B, [P, DV], U32, "v_codes")
+        v_scales = tiles(B, [P, DV], U8, "v_scales")
+        result = tiles(B, [P, DV], F32, "result")
         turned = {}
 
-        def scores(s):
-            ps = bank(1 + s)
-            qc = slice(s * NQ, (s + 1) * NQ)
-            for c in range(CHUNKS):
+        def scores(i):
+            s = i // HALVES
+            ps = bank(4 + i % HALVES)
+            for c in range(2):
                 kc = slice(c * P, (c + 1) * P)
                 nc.tensor.matmul_mx(
-                    out=ps[:, kc], lhsT=k_codes[s][:, kc].bitcast(FP8X4), lhsT_scale=k_scales[s][:, kc],
-                    rhs=q_codes[:, qc].bitcast(FP8X4), rhs_scale=q_scales[:, qc], start=True, stop=True,
+                    out=ps[:, kc], lhsT=k_codes[i][:, kc].bitcast(FP8X4), lhsT_scale=k_scales[i][:, kc],
+                    rhs=q_codes[s][:].bitcast(FP8X4), rhs_scale=q_scales[s][:], start=True, stop=True,
                 )
-            for c in range(CHUNKS):
-                nc.scalar.activation(
-                    scaled[s][:, c, :], ps[:, c * P : (c + 1) * P], ACT.Copy, scale=ks_col[s][:, c : c + 1]
-                )
-
-        def turn_scores(s):
-            for c in range(CHUNKS):
+            for c in range(2):
+                j = 2 * i + c
+                nc.scalar.activation(scaled[j][:], ps[:, c * P : (c + 1) * P], ACT.Copy, scale=nks_col[:, j : j + 1])
+            for c in range(2):
                 nc.tensor.matmul(
-                    score[s][:, c * P : (c + 1) * P], scaled[s][:, c, :], ident[:],
-                    is_transpose=True, start=False, stop=c == CHUNKS - 1,
+                    score[i][:, c * P : (c + 1) * P], scaled[2 * i + c][:], ident[:],
+                    is_transpose=True, start=False, stop=c == 1,
                 )
 
-        def row_max(s):
-            nc.vector.tensor_reduce(negmax[s][:], score[s][:], AXIS_X, ALU.max, negate=True)
-
-        def exponent(s):
-            nc.scalar.activation(
-                prob[s][:], score[s][:].rearrange("q (i t) -> q t i", t=PACK),
-                ACT.Exp, bias=negmax[s][:], accum_out=total[s][:],
+        def row_min(i):
+            start = lowest[i - 1][:] if i % HALVES else None
+            h = i % HALVES
+            nc.vector.tensor_scalar(
+                kept[i // HALVES][:, h * H : (h + 1) * H], score[i][:, 0:H], 1.0, start, ALU.mult, ALU.min, accum_out=lowest[i][:]
             )
 
+        def exponent(s):
+            for u in range(PAIR):
+                nc.scalar.activation(
+                    prob[s * PAIR + u][:].rearrange("q t n -> q n t"),
+                    kept[s][:].rearrange("q (n t) -> q n t", t=PACK)[:, :, u * PAIR : (u + 1) * PAIR],
+                    ACT.Exp, bias=lowest[s * HALVES + 1][:], scale=-1.0, accum_out=sums[s][:, u : u + 1],
+                )
+
         def turn_prob(s):
-            ps = bank(7 * s)
+            ps = bank(4 + s)
             for t in range(PACK):
-                nc.tensor.transpose(ps[:, t * P : (t + 1) * P], prob[s][:, t, :], ident[:])
-            turned["prob", s] = ps
+                nc.tensor.transpose(ps[:, t * P : (t + 1) * P], prob[s * PAIR + t // PAIR][:, t % PAIR, :], ident[:])
+            turned[s] = ps
 
         def weights(s):
             nc.vector.tensor_tensor(
-                w_bf[s][:], turned["prob", s][:].rearrange("p (t q) -> p q t", t=PACK),
-                vs_col[s].unsqueeze(1).to_broadcast([P, NQ, PACK]), ALU.mult,
+                w_bf[s][:], turned[s][:].rearrange("p (t q) -> p q t", t=PACK),
+                vs_col[:, s * PACK : (s + 1) * PACK].unsqueeze(1).to_broadcast([P, NQ, PACK]), ALU.mult,
             )
+            quantize(w_codes[s], w_scales[s], w_bf[s][:].rearrange("p q t -> p (q t)"))
 
-        def quantize_w(s):
-            nc.vector.quantize_mx(
-                out=w_codes[s][:].bitcast(FP8X4), scales=w_scales[s][:], in_=w_bf[s][:].rearrange("p q t -> p (q t)")
-            )
+        def row_sum(s):
+            nc.vector.tensor_reduce(total[s][:], sums[s][:], mybir.AxisListType.X, ALU.add)
+            nc.vector.reciprocal(inv[s][:], total[s][:])
 
         def gather_v(e, s, name, on_vector):
             v_got[e, s] = keep.tile([P, N], BF16, name=name, align_bytes=64)
@@ -225,21 +252,19 @@ def tile_attend_x_ks_draft_kernel(tc, qT, kT, vT, ks, vs, pos, qpos, offs, out):
                 gather_scalar(v_got[e, s][:, on_vector:N], v_pool[e], s * N + on_vector, (s + 1) * N)
 
         def turn_v(e, s):
-            ps = bank(5 - 4 * e + s)
+            ps = bank(6 + s)
             words = v_got[e, s][:].bitcast(F32)
-            for u in range(HALF):
-                nc.tensor.transpose(ps[:, u * P : (u + 1) * P], words[:, u : N // 2 : HALF], ident[:])
-            place = v_bf[s][:].bitcast(F32)[:, e * P * HALF : (e + 1) * P * HALF]
+            for u in range(PAIR):
+                nc.tensor.transpose(ps[:, u * P : (u + 1) * P], words[:, u : N // 2 : PAIR], ident[:])
+            place = v_bf[s][:].bitcast(F32)[:, e * P * PAIR : (e + 1) * P * PAIR]
             nc.scalar.copy(
-                out=place.rearrange("p (c u) -> p c u", u=HALF),
-                in_=ps[:, 0 : HALF * P].rearrange("p (u c) -> p c u", u=HALF),
+                out=place.rearrange("p (c u) -> p c u", u=PAIR),
+                in_=ps[:, 0 : PAIR * P].rearrange("p (u c) -> p c u", u=PAIR),
             )
 
-        def quantize_v(s):
-            nc.vector.quantize_mx(out=v_codes[s][:].bitcast(FP8X4), scales=v_scales[s][:], in_=v_bf[s][:])
-
         def values(s):
-            ps = bank(3 + s)
+            quantize(v_codes[s], v_scales[s], v_bf[s][:])
+            ps = bank(s * HALVES)
             nc.tensor.matmul_mx(
                 out=ps[:, 0:DV], lhsT=w_codes[s][:].bitcast(FP8X4), lhsT_scale=w_scales[s][:],
                 rhs=v_codes[s][:].bitcast(FP8X4), rhs_scale=v_scales[s][:], start=True, stop=True,
@@ -247,27 +272,22 @@ def tile_attend_x_ks_draft_kernel(tc, qT, kT, vT, ks, vs, pos, qpos, offs, out):
             nc.scalar.activation(result[s][:], ps[:, 0:DV], ACT.Copy, scale=inv[s][:])
             nc.sync.dma_start(out[s], result[s][:])
 
+        for i in range(PARTS):
+            interleave_last(i)
+            quantize_k(i)
+            scores(i)
+            row_min(i)
         for s in range(B):
-            interleave(nc.vector.tensor_copy, k_last[s], s, HALF, 0, N)
-        for s in range(B):
-            quantize_k(s)
-            scores(s)
-            turn_scores(s)
-        for s in range(B):
-            row_max(s)
             exponent(s)
             turn_prob(s)
-        for s in range(B):
             weights(s)
-            nc.vector.reciprocal(inv[s][:], total[s][:])
-            quantize_w(s)
-        gather_v(0, 0, "v_got0", 0)
-        gather_v(0, 1, "k_bf1", N)
-        gather_v(1, 0, "v_got1", VECTOR_SLOTS)
-        gather_v(1, 1, "scaled1", N)
+        gather_v(0, 0, "v_got0", 128)
+        gather_v(0, 1, "k_last3", N)
+        gather_v(1, 0, "scaled3", N)
+        gather_v(1, 1, "scaled7", H)
         for e in range(E_BLOCKS):
             for s in range(B):
                 turn_v(e, s)
         for s in range(B):
-            quantize_v(s)
+            row_sum(s)
             values(s)

@@ -14,7 +14,7 @@ ACT = mybir.ActivationFunctionType
 
 B, NQ, D, DV, N, T = 2, 128, 512, 256, 512, 2048
 P = 128
-ROW = P - 1
+ROW = {"pos": 127, "ks": 127, "vs": 127}
 PACK = 4
 PAIR = PACK // 2
 CHUNKS = N // P
@@ -51,26 +51,25 @@ def tile_attend_x_ks_draft_kernel(tc, qT, kT, vT, ks, vs, pos, qpos, offs, out):
             nc.scalar.activation(dst, window[:].indirect(offsets[:, a // 16 : z // 16]), ACT.Copy)
 
         table = {}
+        q_place = keep.tile([P, B], F32, name="q_place")
         for name, source in (("pos", pos), ("ks", ks), ("vs", vs)):
             table[name] = keep.tile([P, T], F32, name=name + "_table")
-            nc.sync.dma_start(table[name][ROW:P, :], source[0:1, :])
-            nc.vector.memset(table[name][0:ROW, :].bitcast(U32), 0)
-        q_place = keep.tile([P, B], F32, name="q_place")
-        nc.scalar.dma_start(q_place[:], qpos.rearrange("b q o -> q (b o)"))
+            row = ROW[name]
+            nc.vector.memset(table[name][0 : row if row == P - 1 else P, :].bitcast(U32), 0)
+            nc.scalar.dma_start(table[name][row : row + 1, :], source[0:1, :])
+            if name == "pos":
+                nc.scalar.dma_start(q_place[:], qpos.rearrange("b q o -> q (b o)"))
         q_raw = tiles(B, [P, PACK, NQ], F32, "q_raw")
         k_rows = kT.rearrange("(p t) n -> p t n", t=PACK)
         k_pool = tiles(PACK, [P, T], F32, "k_pool")
-        v_pool = tiles(E_BLOCKS, [P, T], F32, "v_pool")
 
         def load_q(s):
             nc.sync.dma_start(q_raw[s][:], qT[s].rearrange("(p t) q -> p t q", t=PACK))
 
-        for s in range(B):
-            load_q(s)
+        load_q(0)
         for t in range(PACK):
             nc.sync.dma_start(k_pool[t][:], k_rows[:, t, :])
-        for e in range(E_BLOCKS):
-            nc.sync.dma_start(v_pool[e][:], vT[e * P : (e + 1) * P, :])
+        load_q(1)
 
         warm = keep.tile([P, 1], F32, name="warm")
         nc.gpsimd.memset(warm[:], 0.0)
@@ -87,11 +86,12 @@ def tile_attend_x_ks_draft_kernel(tc, qT, kT, vT, ks, vs, pos, qpos, offs, out):
             gather(got[:], table[name], 0, B * N)
             return got
 
-        def turn_table(got, index, pick):
+        def turn_table(name, got, index, pick):
             ps = bank(index)
-            for j in reversed(range(B * CHUNKS)):
+            row = ROW[name]
+            for j in range(B * CHUNKS) if row < SHIFT else reversed(range(B * CHUNKS)):
                 nc.tensor.transpose(ps[:, j * SHIFT : j * SHIFT + P], got[:, pick(j // CHUNKS, j % CHUNKS)], ident[:])
-            return ps[:, ROW : ROW + B * CHUNKS * SHIFT : SHIFT]
+            return ps[:, row : row + B * CHUNKS * SHIFT : SHIFT]
 
         def keep_columns(name, columns, scale):
             col = keep.tile([P, B * CHUNKS], F32, name=name + "_col")
@@ -123,7 +123,7 @@ def tile_attend_x_ks_draft_kernel(tc, qT, kT, vT, ks, vs, pos, qpos, offs, out):
         def build_masks(pos_got):
             q_row_sb = keep.tile([P, B * NQ], F32, name="q_row_sb")
             nc.scalar.copy(out=q_row_sb[:], in_=q_row[:, 0 : B * NQ])
-            pos_col = turn_table(pos_got, 5, chunk)
+            pos_col = turn_table("pos", pos_got, 5, chunk)
             for j in range(B * CHUNKS):
                 s = j // CHUNKS
                 nc.vector.tensor_scalar(
@@ -152,31 +152,34 @@ def tile_attend_x_ks_draft_kernel(tc, qT, kT, vT, ks, vs, pos, qpos, offs, out):
             )
 
         def interleave_last(i):
-            nc.vector.tensor_copy(out=k_bf[i][:, :, PAIR:PACK], in_=k_last[i][:].rearrange("p t n -> p n t"))
+            copy = nc.scalar.copy if i in (3,) else nc.vector.tensor_copy
+            copy(out=k_bf[i][:, :, PAIR:PACK], in_=k_last[i][:].rearrange("p t n -> p n t"))
 
         def quantize_k(i):
             quantize(k_codes[i], k_scales[i], k_bf[i][:].rearrange("p n t -> p (n t)"))
 
         pos_got = gather_table("pos", gather_scalar)
-        for s in range(B):
-            interleave_q(s, nc.vector.tensor_copy)
+        interleave_q(0, nc.vector.tensor_copy)
+        quantize_q(0)
         ks_got = gather_table("ks", gather_vector)
-        for s in range(B):
-            quantize_q(s)
         build_masks(pos_got)
         vs_got = gather_table("vs", gather_vector)
-        nks_col = keep_columns("ks", turn_table(ks_got, 6, chunk), -1.0)
+        nks_col = keep_columns("ks", turn_table("ks", ks_got, 6, chunk), -1.0)
         gather_first(0, gather_scalar, 0, B * N)
-        gather_first(1, gather_scalar, 0, N)
-        gather_first(1, gather_vector, N, B * N)
+        gather_first(1, gather_scalar, 0, 768)
+        gather_first(1, gather_vector, 768, B * N)
         for i in range(PARTS):
             interleave_first(i)
-        vs_col = keep_columns("vs", turn_table(vs_got, 7, dealt), 1.0)
+        vs_col = keep_columns("vs", turn_table("vs", vs_got, 7, dealt), 1.0)
         for i in range(PARTS):
-            gather_last(2, i, gather_scalar if i < PARTS - 1 else gather_vector)
+            gather_last(2, i, gather_scalar if i < 4 else gather_vector)
         for i in range(PARTS):
-            gather_last(3, i, gather_scalar if i > 0 else gather_vector)
+            gather_last(3, i, gather_scalar if i >= 1 else gather_vector)
 
+
+        v_pool = tiles(E_BLOCKS, [P, T], F32, "v_pool")
+        for e in range(E_BLOCKS):
+            nc.sync.dma_start(v_pool[e][:], vT[e * P : (e + 1) * P, :])
         scaled = tiles(B * CHUNKS, [P, NQ], F32, "scaled")
         lowest = tiles(PARTS, [P, 1], F32, "lowest")
         kept = tiles(B, [P, N], F32, "kept")
@@ -196,7 +199,7 @@ def tile_attend_x_ks_draft_kernel(tc, qT, kT, vT, ks, vs, pos, qpos, offs, out):
 
         def scores(i):
             s = i // HALVES
-            ps = bank(4 + i % HALVES)
+            ps = bank(4 + i)
             for c in range(2):
                 kc = slice(c * P, (c + 1) * P)
                 nc.tensor.matmul_mx(
@@ -228,7 +231,7 @@ def tile_attend_x_ks_draft_kernel(tc, qT, kT, vT, ks, vs, pos, qpos, offs, out):
                 )
 
         def turn_prob(s):
-            ps = bank(4 + s)
+            ps = bank(6 + s)
             for t in range(PACK):
                 nc.tensor.transpose(ps[:, t * P : (t + 1) * P], prob[s * PAIR + t // PAIR][:, t % PAIR, :], ident[:])
             turned[s] = ps
@@ -248,11 +251,11 @@ def tile_attend_x_ks_draft_kernel(tc, qT, kT, vT, ks, vs, pos, qpos, offs, out):
             v_got[e, s] = keep.tile([P, N], BF16, name=name, align_bytes=64)
             if on_vector > 0:
                 gather_vector(v_got[e, s][:, 0:on_vector], v_pool[e], s * N, s * N + on_vector)
-            if on_vector < N:
-                gather_scalar(v_got[e, s][:, on_vector:N], v_pool[e], s * N + on_vector, (s + 1) * N)
+            for a in range(on_vector, N, H):
+                gather_scalar(v_got[e, s][:, a : a + H], v_pool[e], s * N + a, s * N + a + H)
 
         def turn_v(e, s):
-            ps = bank(6 + s)
+            ps = bank(4 - 4 * e + s)
             words = v_got[e, s][:].bitcast(F32)
             for u in range(PAIR):
                 nc.tensor.transpose(ps[:, u * P : (u + 1) * P], words[:, u : N // 2 : PAIR], ident[:])
@@ -264,7 +267,7 @@ def tile_attend_x_ks_draft_kernel(tc, qT, kT, vT, ks, vs, pos, qpos, offs, out):
 
         def values(s):
             quantize(v_codes[s], v_scales[s], v_bf[s][:])
-            ps = bank(s * HALVES)
+            ps = bank(2 + s)
             nc.tensor.matmul_mx(
                 out=ps[:, 0:DV], lhsT=w_codes[s][:].bitcast(FP8X4), lhsT_scale=w_scales[s][:],
                 rhs=v_codes[s][:].bitcast(FP8X4), rhs_scale=v_scales[s][:], start=True, stop=True,
@@ -275,16 +278,19 @@ def tile_attend_x_ks_draft_kernel(tc, qT, kT, vT, ks, vs, pos, qpos, offs, out):
         for i in range(PARTS):
             interleave_last(i)
             quantize_k(i)
+            if i == 2:
+                interleave_q(1, nc.vector.tensor_copy)
+                quantize_q(1)
             scores(i)
             row_min(i)
         for s in range(B):
             exponent(s)
             turn_prob(s)
             weights(s)
-        gather_v(0, 0, "v_got0", 128)
-        gather_v(0, 1, "k_last3", N)
-        gather_v(1, 0, "scaled3", N)
-        gather_v(1, 1, "scaled7", H)
+        gather_v(0, 0, "v_got0", 0)
+        gather_v(0, 1, "k_last3", 512)
+        gather_v(1, 0, "v_got2", 256)
+        gather_v(1, 1, "kept0", 256)
         for e in range(E_BLOCKS):
             for s in range(B):
                 turn_v(e, s)

@@ -18,9 +18,10 @@ ROW = {"pos": 127, "ks": 127, "vs": 127}
 PACK = 4
 PAIR = PACK // 2
 CHUNKS = N // P
-HALVES = 2
-H = N // HALVES
-PARTS = B * HALVES
+H = N // 2
+EXPS = 1
+SPANS = ((0, 512), (512, 1024))
+PARTS = len(SPANS)
 E_BLOCKS = DV // P
 MASKED = 1.0e30
 SHIFT = 16
@@ -66,10 +67,10 @@ def tile_attend_x_ks_draft_kernel(tc, qT, kT, vT, ks, vs, pos, qpos, offs, out):
         def load_q(s):
             nc.sync.dma_start(q_raw[s][:], qT[s].rearrange("(p t) q -> p t q", t=PACK))
 
-        load_q(0)
         for t in range(PACK):
             nc.sync.dma_start(k_pool[t][:], k_rows[:, t, :])
-        load_q(1)
+        for s in range(B):
+            load_q(s)
 
         warm = keep.tile([P, 1], F32, name="warm")
         nc.gpsimd.memset(warm[:], 0.0)
@@ -119,6 +120,7 @@ def tile_attend_x_ks_draft_kernel(tc, qT, kT, vT, ks, vs, pos, qpos, offs, out):
 
         limit = tiles(B * CHUNKS, [P, NQ], F32, "limit")
         score = [bank(i) for i in range(PARTS)]
+        part_of = [i for i, (a, z) in enumerate(SPANS) for j in range(a // P, z // P)]
 
         def build_masks(pos_got):
             q_row_sb = keep.tile([P, B * NQ], F32, name="q_row_sb")
@@ -129,64 +131,63 @@ def tile_attend_x_ks_draft_kernel(tc, qT, kT, vT, ks, vs, pos, qpos, offs, out):
                 nc.vector.tensor_scalar(
                     limit[j][:], q_row_sb[:, s * NQ : (s + 1) * NQ], pos_col[:, j : j + 1], MASKED, ALU.is_lt, ALU.mult
                 )
-                c = j % 2
+                c = j - SPANS[part_of[j]][0] // P
                 nc.tensor.matmul(
-                    score[j // 2][:, c * P : (c + 1) * P], limit[j][:], ident[:], is_transpose=True, start=c == 0, stop=False
+                    score[part_of[j]][:, c * P : (c + 1) * P], limit[j][:], ident[:], is_transpose=True, start=c == 0, stop=False
                 )
 
         k_first = keep.tile([P, PAIR, B * N], BF16, name="k_first")
-        k_last = tiles(PARTS, [P, PAIR, H], BF16, "k_last")
-        k_bf = tiles(PARTS, [P, H, PACK], BF16, "k_bf")
-        k_codes = tiles(PARTS, [P, H], U32, "k_codes")
-        k_scales = tiles(PARTS, [P, H], U8, "k_scales")
+        k_last = keep.tile([P, PAIR, B * N], BF16, name="k_last", align_bytes=64)
+        k_bf = [keep.tile([P, z - a, PACK], BF16, name=f"k_bf{i}", align_bytes=64) for i, (a, z) in enumerate(SPANS)]
+        k_codes = [keep.tile([P, z - a], U32, name=f"k_codes{i}", align_bytes=64) for i, (a, z) in enumerate(SPANS)]
+        k_scales = [keep.tile([P, z - a], U8, name=f"k_scales{i}", align_bytes=64) for i, (a, z) in enumerate(SPANS)]
 
         def gather_first(t, gather, a, z):
             gather(k_first[:, t, a:z], k_pool[t], a, z)
 
-        def gather_last(t, i, gather):
-            gather(k_last[i][:, t - PAIR, :], k_pool[t], i * H, (i + 1) * H)
+        def gather_last(t, gather, a, z):
+            gather(k_last[:, t - PAIR, a:z], k_pool[t], a, z)
 
         def interleave_first(i):
             nc.vector.tensor_copy(
-                out=k_bf[i][:, :, 0:PAIR], in_=k_first[:, :, i * H : (i + 1) * H].rearrange("p t n -> p n t")
+                out=k_bf[i][:, :, 0:PAIR], in_=k_first[:, :, SPANS[i][0] : SPANS[i][1]].rearrange("p t n -> p n t")
             )
 
         def interleave_last(i):
-            copy = nc.scalar.copy if i in (3,) else nc.vector.tensor_copy
-            copy(out=k_bf[i][:, :, PAIR:PACK], in_=k_last[i][:].rearrange("p t n -> p n t"))
+            a, z = SPANS[i]
+            cut = z - (256 if i == PARTS - 1 else 0)
+            if cut < z:
+                nc.scalar.copy(out=k_bf[i][:, cut - a : z - a, PAIR:PACK], in_=k_last[:, :, cut:z].rearrange("p t n -> p n t"))
+            nc.vector.tensor_copy(out=k_bf[i][:, 0 : cut - a, PAIR:PACK], in_=k_last[:, :, a:cut].rearrange("p t n -> p n t"))
 
         def quantize_k(i):
             quantize(k_codes[i], k_scales[i], k_bf[i][:].rearrange("p n t -> p (n t)"))
 
         pos_got = gather_table("pos", gather_scalar)
-        interleave_q(0, nc.vector.tensor_copy)
-        quantize_q(0)
+
         ks_got = gather_table("ks", gather_vector)
         build_masks(pos_got)
         vs_got = gather_table("vs", gather_vector)
         nks_col = keep_columns("ks", turn_table("ks", ks_got, 6, chunk), -1.0)
-        gather_first(0, gather_scalar, 0, B * N)
-        gather_first(1, gather_scalar, 0, 768)
-        gather_first(1, gather_vector, 768, B * N)
+        for t in range(PAIR):
+            gather_first(t, gather_scalar, 0, B * N)
         for i in range(PARTS):
             interleave_first(i)
         vs_col = keep_columns("vs", turn_table("vs", vs_got, 7, dealt), 1.0)
-        for i in range(PARTS):
-            gather_last(2, i, gather_scalar if i < 4 else gather_vector)
-        for i in range(PARTS):
-            gather_last(3, i, gather_scalar if i >= 1 else gather_vector)
-
+        gather_last(2, gather_scalar, 0, B * N)
+        gather_last(3, gather_vector, 0, N)
+        gather_last(3, gather_scalar, N, B * N)
 
         v_pool = tiles(E_BLOCKS, [P, T], F32, "v_pool")
         for e in range(E_BLOCKS):
             nc.sync.dma_start(v_pool[e][:], vT[e * P : (e + 1) * P, :])
-        scaled = tiles(B * CHUNKS, [P, NQ], F32, "scaled")
+        scaled = [keep.tile([P, (z - a) // P, NQ], F32, name=f"scaled{i}", align_bytes=64) for i, (a, z) in enumerate(SPANS)]
         lowest = tiles(PARTS, [P, 1], F32, "lowest")
         kept = tiles(B, [P, N], F32, "kept")
-        sums = tiles(B, [P, PAIR], F32, "sums")
+        sums = tiles(B, [P, EXPS], F32, "sums")
         total = tiles(B, [P, 1], F32, "total")
         inv = tiles(B, [P, 1], F32, "inv")
-        prob = tiles(B * PAIR, [P, PAIR, P], F32, "prob")
+        prob = tiles(B, [P, PACK, P], F32, "prob")
         w_bf = tiles(B, [P, NQ, PACK], BF16, "w_bf")
         w_codes = tiles(B, [P, NQ], U32, "w_codes")
         w_scales = tiles(B, [P, NQ], U8, "w_scales")
@@ -198,42 +199,57 @@ def tile_attend_x_ks_draft_kernel(tc, qT, kT, vT, ks, vs, pos, qpos, offs, out):
         turned = {}
 
         def scores(i):
-            s = i // HALVES
+            a, z = SPANS[i]
+            s, first, count = a // N, a // P, (z - a) // P
             ps = bank(4 + i)
-            for c in range(2):
+            for c in range(count):
                 kc = slice(c * P, (c + 1) * P)
                 nc.tensor.matmul_mx(
                     out=ps[:, kc], lhsT=k_codes[i][:, kc].bitcast(FP8X4), lhsT_scale=k_scales[i][:, kc],
                     rhs=q_codes[s][:].bitcast(FP8X4), rhs_scale=q_scales[s][:], start=True, stop=True,
                 )
-            for c in range(2):
-                j = 2 * i + c
-                nc.scalar.activation(scaled[j][:], ps[:, c * P : (c + 1) * P], ACT.Copy, scale=nks_col[:, j : j + 1])
-            for c in range(2):
+            if i in (0, 1):
+                nc.vector.tensor_tensor(
+                    scaled[i][:], ps[:, 0 : count * P].rearrange("p (c q) -> p c q", q=NQ),
+                    nks_col[:, first : first + count].unsqueeze(2).to_broadcast([P, count, NQ]), ALU.mult,
+                )
+            else:
+                for c in range(count):
+                    j = first + c
+                    nc.scalar.activation(scaled[i][:, c, :], ps[:, c * P : (c + 1) * P], ACT.Copy, scale=nks_col[:, j : j + 1])
+            for c in range(count):
                 nc.tensor.matmul(
-                    score[i][:, c * P : (c + 1) * P], scaled[2 * i + c][:], ident[:],
-                    is_transpose=True, start=False, stop=c == 1,
+                    score[i][:, c * P : (c + 1) * P], scaled[i][:, c, :], ident[:],
+                    is_transpose=True, start=False, stop=c == count - 1,
                 )
 
         def row_min(i):
-            start = lowest[i - 1][:] if i % HALVES else None
-            h = i % HALVES
+            a, z = SPANS[i]
+            if z - a == N:
+                nc.vector.tensor_reduce(lowest[i][:], score[i][:], mybir.AxisListType.X, ALU.min)
+                return
+            start = lowest[i - 1][:] if a % N else None
             nc.vector.tensor_scalar(
-                kept[i // HALVES][:, h * H : (h + 1) * H], score[i][:, 0:H], 1.0, start, ALU.mult, ALU.min, accum_out=lowest[i][:]
+                kept[a // N][:, a % N : a % N + z - a], score[i][:, 0 : z - a], 1.0, start, ALU.mult, ALU.min,
+                accum_out=lowest[i][:],
             )
 
         def exponent(s):
-            for u in range(PAIR):
+            last = part_of[(s + 1) * CHUNKS - 1]
+            whole = SPANS[last][1] - SPANS[last][0] == N
+            source = (score[last] if whole else kept[s])[:].rearrange("q (n t) -> q n t", t=PACK)
+            step = PACK // EXPS
+            for u in range(EXPS):
                 nc.scalar.activation(
-                    prob[s * PAIR + u][:].rearrange("q t n -> q n t"),
-                    kept[s][:].rearrange("q (n t) -> q n t", t=PACK)[:, :, u * PAIR : (u + 1) * PAIR],
-                    ACT.Exp, bias=lowest[s * HALVES + 1][:], scale=-1.0, accum_out=sums[s][:, u : u + 1],
+                    prob[s][:, u * step : (u + 1) * step, :].rearrange("q t n -> q n t"),
+                    source[:, :, u * step : (u + 1) * step],
+                    ACT.Exp, bias=lowest[last][:], scale=-1.0, accum_out=sums[s][:, u : u + 1],
                 )
 
         def turn_prob(s):
-            ps = bank(6 + s)
+            ps = bank(4 + s)
             for t in range(PACK):
-                nc.tensor.transpose(ps[:, t * P : (t + 1) * P], prob[s * PAIR + t // PAIR][:, t % PAIR, :], ident[:])
+                nc.tensor.transpose(ps[:, t * P : (t + 1) * P], prob[s][:, t, :], ident[:])
             turned[s] = ps
 
         def weights(s):
@@ -244,19 +260,17 @@ def tile_attend_x_ks_draft_kernel(tc, qT, kT, vT, ks, vs, pos, qpos, offs, out):
             quantize(w_codes[s], w_scales[s], w_bf[s][:].rearrange("p q t -> p (q t)"))
 
         def row_sum(s):
-            nc.vector.tensor_reduce(total[s][:], sums[s][:], mybir.AxisListType.X, ALU.add)
-            nc.vector.reciprocal(inv[s][:], total[s][:])
+            nc.vector.reciprocal(inv[s][:], sums[s][:])
 
-        def gather_v(e, s, name, on_vector):
-            v_got[e, s] = keep.tile([P, N], BF16, name=name, align_bytes=64)
-            if on_vector > 0:
-                gather_vector(v_got[e, s][:, 0:on_vector], v_pool[e], s * N, s * N + on_vector)
-            for a in range(on_vector, N, H):
-                gather_scalar(v_got[e, s][:, a : a + H], v_pool[e], s * N + a, s * N + a + H)
+        def gather_v(e, seqs, name, gather):
+            got = keep.tile([P, len(seqs) * N], BF16, name=name, align_bytes=64)
+            gather(got[:], v_pool[e], seqs[0] * N, (seqs[-1] + 1) * N)
+            for s in seqs:
+                v_got[e, s] = got[:, (s - seqs[0]) * N : (s - seqs[0] + 1) * N]
 
         def turn_v(e, s):
-            ps = bank(4 - 4 * e + s)
-            words = v_got[e, s][:].bitcast(F32)
+            ps = bank(6 - 4 * e + s)
+            words = v_got[e, s].bitcast(F32)
             for u in range(PAIR):
                 nc.tensor.transpose(ps[:, u * P : (u + 1) * P], words[:, u : N // 2 : PAIR], ident[:])
             place = v_bf[s][:].bitcast(F32)[:, e * P * PAIR : (e + 1) * P * PAIR]
@@ -267,7 +281,7 @@ def tile_attend_x_ks_draft_kernel(tc, qT, kT, vT, ks, vs, pos, qpos, offs, out):
 
         def values(s):
             quantize(v_codes[s], v_scales[s], v_bf[s][:])
-            ps = bank(2 + s)
+            ps = bank(s)
             nc.tensor.matmul_mx(
                 out=ps[:, 0:DV], lhsT=w_codes[s][:].bitcast(FP8X4), lhsT_scale=w_scales[s][:],
                 rhs=v_codes[s][:].bitcast(FP8X4), rhs_scale=v_scales[s][:], start=True, stop=True,
@@ -278,8 +292,11 @@ def tile_attend_x_ks_draft_kernel(tc, qT, kT, vT, ks, vs, pos, qpos, offs, out):
         for i in range(PARTS):
             interleave_last(i)
             quantize_k(i)
-            if i == 2:
-                interleave_q(1, nc.vector.tensor_copy)
+            if i == 0:
+                interleave_q(0, nc.vector.tensor_copy)
+                quantize_q(0)
+            if SPANS[i][0] == N:
+                interleave_q(1, nc.scalar.copy)
                 quantize_q(1)
             scores(i)
             row_min(i)
@@ -287,10 +304,9 @@ def tile_attend_x_ks_draft_kernel(tc, qT, kT, vT, ks, vs, pos, qpos, offs, out):
             exponent(s)
             turn_prob(s)
             weights(s)
-        gather_v(0, 0, "v_got0", 0)
-        gather_v(0, 1, "k_last3", 512)
-        gather_v(1, 0, "v_got2", 256)
-        gather_v(1, 1, "kept0", 256)
+        gather_v(0, (0, 1), "v_got0", gather_scalar)
+        gather_v(1, (0,), "v_got1", gather_scalar)
+        gather_v(1, (1,), "scaled1", gather_vector)
         for e in range(E_BLOCKS):
             for s in range(B):
                 turn_v(e, s)

@@ -57,7 +57,7 @@ def tile_attend_x_ks_draft_kernel(tc, qT, kT, vT, ks, vs, pos, qpos, offs, out):
             table[name] = keep.tile([P, T], F32, name=name + "_table")
             row = ROW[name]
             nc.vector.memset(table[name][0 : row if row == P - 1 else P, :].bitcast(U32), 0)
-            nc.scalar.dma_start(table[name][row : row + 1, :], source[0:1, :])
+            nc.sync.dma_start(table[name][row : row + 1, :], source[0:1, :])
             if name == "pos":
                 nc.scalar.dma_start(q_place[:], qpos.rearrange("b q o -> q (b o)"))
         q_raw = tiles(B, [P, PACK, NQ], F32, "q_raw")
@@ -169,12 +169,13 @@ def tile_attend_x_ks_draft_kernel(tc, qT, kT, vT, ks, vs, pos, qpos, offs, out):
         build_masks(pos_got)
         vs_got = gather_table("vs", gather_vector)
         nks_col = keep_columns("ks", turn_table("ks", ks_got, 6, chunk), -1.0)
-        for t in range(PAIR):
-            gather_first(t, gather_scalar, 0, B * N)
+        gather_first(0, gather_scalar, 0, B * N)
+        gather_first(1, gather_scalar, 0, 512)
+        gather_first(1, gather_vector, 512, B * N)
         for i in range(PARTS):
             interleave_first(i)
         vs_col = keep_columns("vs", turn_table("vs", vs_got, 7, dealt), 1.0)
-        gather_last(2, gather_scalar, 0, B * N)
+        gather_last(2, gather_scalar, 0, 1024)
         gather_last(3, gather_vector, 0, N)
         gather_last(3, gather_scalar, N, B * N)
 
@@ -247,7 +248,7 @@ def tile_attend_x_ks_draft_kernel(tc, qT, kT, vT, ks, vs, pos, qpos, offs, out):
                 )
 
         def turn_prob(s):
-            ps = bank(4 + s)
+            ps = bank(s + 2)
             for t in range(PACK):
                 nc.tensor.transpose(ps[:, t * P : (t + 1) * P], prob[s][:, t, :], ident[:])
             turned[s] = ps
@@ -269,7 +270,7 @@ def tile_attend_x_ks_draft_kernel(tc, qT, kT, vT, ks, vs, pos, qpos, offs, out):
                 v_got[e, s] = got[:, (s - seqs[0]) * N : (s - seqs[0] + 1) * N]
 
         def turn_v(e, s):
-            ps = bank(6 - 4 * e + s)
+            ps = bank(4 + 2 * e + s)
             words = v_got[e, s].bitcast(F32)
             for u in range(PAIR):
                 nc.tensor.transpose(ps[:, u * P : (u + 1) * P], words[:, u : N // 2 : PAIR], ident[:])
@@ -278,9 +279,10 @@ def tile_attend_x_ks_draft_kernel(tc, qT, kT, vT, ks, vs, pos, qpos, offs, out):
                 out=place.rearrange("p (c u) -> p c u", u=PAIR),
                 in_=ps[:, 0 : PAIR * P].rearrange("p (u c) -> p c u", u=PAIR),
             )
+            block = slice(e * P, (e + 1) * P)
+            quantize(v_codes[s][:, block], v_scales[s][:, block], v_bf[s][:, e * P * PACK : (e + 1) * P * PACK])
 
         def values(s):
-            quantize(v_codes[s], v_scales[s], v_bf[s][:])
             ps = bank(s)
             nc.tensor.matmul_mx(
                 out=ps[:, 0:DV], lhsT=w_codes[s][:].bitcast(FP8X4), lhsT_scale=w_scales[s][:],

@@ -25,6 +25,7 @@ PARTS = len(SPANS)
 E_BLOCKS = DV // P
 MASKED = 1.0e30
 SHIFT = 16
+FILL_VECTOR = {"pos": T, "ks": 0, "vs": T // 2}
 
 FLOPS = 2 * B * NQ * N * (D + DV)
 BYTES = 4 * (B * D * NQ + (D + DV) * T + 3 * T + B * NQ + B * NQ * DV) + 2 * P * (B * N // 16)
@@ -51,12 +52,21 @@ def tile_attend_x_ks_draft_kernel(tc, qT, kT, vT, ks, vs, pos, qpos, offs, out):
         def gather_scalar(dst, window, a, z):
             nc.scalar.activation(dst, window[:].indirect(offsets[:, a // 16 : z // 16]), ACT.Copy)
 
+        warm = keep.tile([P, 1], F32, name="warm")
+        nc.gpsimd.memset(warm[:], 0.0)
+        nc.scalar.activation(warm[:], warm[:], ACT.Exp)
+        ident = keep.tile([P, P], F32, name="ident")
+        make_identity(nc, ident[:])
         table = {}
         q_place = keep.tile([P, B], F32, name="q_place")
         for name, source in (("pos", pos), ("ks", ks), ("vs", vs)):
             table[name] = keep.tile([P, T], F32, name=name + "_table")
             row = ROW[name]
-            nc.vector.memset(table[name][0 : row if row == P - 1 else P, :].bitcast(U32), 0)
+            cut = FILL_VECTOR[name]
+            if cut > 0:
+                nc.vector.memset(table[name][0:row, 0:cut].bitcast(U32), 0)
+            if cut < T:
+                nc.gpsimd.memset(table[name][0:row, cut:T].bitcast(U32), 0)
             nc.sync.dma_start(table[name][row : row + 1, :], source[0:1, :])
             if name == "pos":
                 nc.scalar.dma_start(q_place[:], qpos.rearrange("b q o -> q (b o)"))
@@ -72,11 +82,6 @@ def tile_attend_x_ks_draft_kernel(tc, qT, kT, vT, ks, vs, pos, qpos, offs, out):
         for s in range(B):
             load_q(s)
 
-        warm = keep.tile([P, 1], F32, name="warm")
-        nc.gpsimd.memset(warm[:], 0.0)
-        nc.scalar.activation(warm[:], warm[:], ACT.Exp)
-        ident = keep.tile([P, P], F32, name="ident")
-        make_identity(nc, ident[:])
 
         q_row = bank(4)
         for s in range(B):
@@ -238,12 +243,11 @@ def tile_attend_x_ks_draft_kernel(tc, qT, kT, vT, ks, vs, pos, qpos, offs, out):
         def exponent(s):
             last = part_of[(s + 1) * CHUNKS - 1]
             whole = SPANS[last][1] - SPANS[last][0] == N
-            source = (score[last] if whole else kept[s])[:].rearrange("q (n t) -> q n t", t=PACK)
+            source = (score[last] if whole else kept[s])[:].rearrange("q (n t) -> q t n", t=PACK)
             step = PACK // EXPS
             for u in range(EXPS):
                 nc.scalar.activation(
-                    prob[s][:, u * step : (u + 1) * step, :].rearrange("q t n -> q n t"),
-                    source[:, :, u * step : (u + 1) * step],
+                    prob[s][:, u * step : (u + 1) * step, :], source[:, u * step : (u + 1) * step, :],
                     ACT.Exp, bias=lowest[last][:], scale=-1.0, accum_out=sums[s][:, u : u + 1],
                 )
 

@@ -24,8 +24,9 @@ SPANS = ((0, 512), (512, 1024))
 PARTS = len(SPANS)
 E_BLOCKS = DV // P
 MASKED = 1.0e30
-SHIFT = 16
 FILL_VECTOR = {"pos": T, "ks": 0, "vs": T // 2}
+FIRST_FILL = 256
+SHIFT = 16
 
 FLOPS = 2 * B * NQ * N * (D + DV)
 BYTES = 4 * (B * D * NQ + (D + DV) * T + 3 * T + B * NQ + B * NQ * DV) + 2 * P * (B * N // 16)
@@ -64,9 +65,12 @@ def tile_attend_x_ks_draft_kernel(tc, qT, kT, vT, ks, vs, pos, qpos, offs, out):
             row = ROW[name]
             cut = FILL_VECTOR[name]
             if cut > 0:
-                nc.vector.memset(table[name][0:row, 0:cut].bitcast(U32), 0)
+                nc.vector.memset(table[name][0 : row, 0:cut].bitcast(U32), 0)
+            if cut == 0:
+                cut = FIRST_FILL
+                nc.gpsimd.memset(table[name][0 : row, 0:cut].bitcast(U32), 0)
             if cut < T:
-                nc.gpsimd.memset(table[name][0:row, cut:T].bitcast(U32), 0)
+                nc.gpsimd.memset(table[name][0 : row, cut:T].bitcast(U32), 0)
             nc.sync.dma_start(table[name][row : row + 1, :], source[0:1, :])
             if name == "pos":
                 nc.scalar.dma_start(q_place[:], qpos.rearrange("b q o -> q (b o)"))
@@ -100,7 +104,7 @@ def tile_attend_x_ks_draft_kernel(tc, qT, kT, vT, ks, vs, pos, qpos, offs, out):
             return ps[:, row : row + B * CHUNKS * SHIFT : SHIFT]
 
         def keep_columns(name, columns, scale):
-            col = keep.tile([P, B * CHUNKS], F32, name=name + "_col")
+            col = keep.tile([P, B * CHUNKS], F32, name=name, align_bytes=64)
             nc.vector.tensor_scalar(col[:], columns, scale, None, ALU.mult)
             return col
 
@@ -123,7 +127,6 @@ def tile_attend_x_ks_draft_kernel(tc, qT, kT, vT, ks, vs, pos, qpos, offs, out):
         def quantize_q(s):
             quantize(q_codes[s], q_scales[s], q_bf[s][:].rearrange("p q t -> p (q t)"))
 
-        limit = tiles(B * CHUNKS, [P, NQ], F32, "limit")
         score = [bank(i) for i in range(PARTS)]
         part_of = [i for i, (a, z) in enumerate(SPANS) for j in range(a // P, z // P)]
 
@@ -131,14 +134,15 @@ def tile_attend_x_ks_draft_kernel(tc, qT, kT, vT, ks, vs, pos, qpos, offs, out):
             q_row_sb = keep.tile([P, B * NQ], F32, name="q_row_sb")
             nc.scalar.copy(out=q_row_sb[:], in_=q_row[:, 0 : B * NQ])
             pos_col = turn_table("pos", pos_got, 5, chunk)
+            limit = keep.tile([P, B * CHUNKS, NQ], F32, name="vs_table")
             for j in range(B * CHUNKS):
                 s = j // CHUNKS
                 nc.vector.tensor_scalar(
-                    limit[j][:], q_row_sb[:, s * NQ : (s + 1) * NQ], pos_col[:, j : j + 1], MASKED, ALU.is_lt, ALU.mult
+                    limit[:, j, :], q_row_sb[:, s * NQ : (s + 1) * NQ], pos_col[:, j : j + 1], MASKED, ALU.is_lt, ALU.mult
                 )
                 c = j - SPANS[part_of[j]][0] // P
                 nc.tensor.matmul(
-                    score[part_of[j]][:, c * P : (c + 1) * P], limit[j][:], ident[:], is_transpose=True, start=c == 0, stop=False
+                    score[part_of[j]][:, c * P : (c + 1) * P], limit[:, j, :], ident[:], is_transpose=True, start=c == 0, stop=False
                 )
 
         k_first = keep.tile([P, PAIR, B * N], BF16, name="k_first")
@@ -171,15 +175,15 @@ def tile_attend_x_ks_draft_kernel(tc, qT, kT, vT, ks, vs, pos, qpos, offs, out):
         pos_got = gather_table("pos", gather_scalar)
 
         ks_got = gather_table("ks", gather_vector)
-        build_masks(pos_got)
         vs_got = gather_table("vs", gather_vector)
-        nks_col = keep_columns("ks", turn_table("ks", ks_got, 6, chunk), -1.0)
+        build_masks(pos_got)
+        ks_turned = turn_table("ks", ks_got, 6, chunk)
         gather_first(0, gather_scalar, 0, B * N)
         gather_first(1, gather_scalar, 0, 512)
         gather_first(1, gather_vector, 512, B * N)
         for i in range(PARTS):
             interleave_first(i)
-        vs_col = keep_columns("vs", turn_table("vs", vs_got, 7, dealt), 1.0)
+        vs_turned = turn_table("vs", vs_got, 7, dealt)
         gather_last(2, gather_scalar, 0, 1024)
         gather_last(3, gather_vector, 0, N)
         gather_last(3, gather_scalar, N, B * N)
@@ -295,6 +299,7 @@ def tile_attend_x_ks_draft_kernel(tc, qT, kT, vT, ks, vs, pos, qpos, offs, out):
             nc.scalar.activation(result[s][:], ps[:, 0:DV], ACT.Copy, scale=inv[s][:])
             nc.sync.dma_start(out[s], result[s][:])
 
+        nks_col = keep_columns("k_pool3", ks_turned, -1.0)
         for i in range(PARTS):
             interleave_last(i)
             quantize_k(i)
@@ -306,6 +311,7 @@ def tile_attend_x_ks_draft_kernel(tc, qT, kT, vT, ks, vs, pos, qpos, offs, out):
                 quantize_q(1)
             scores(i)
             row_min(i)
+        vs_col = keep_columns("k_codes1", vs_turned, 1.0)
         for s in range(B):
             exponent(s)
             turn_prob(s)

@@ -19,8 +19,8 @@ PACK = 4
 PAIR = PACK // 2
 CHUNKS = N // P
 H = N // 2
-EXPS = 1
-SPANS = ((0, 512), (512, 1024))
+EXPS = 2
+SPANS = ((0, 256), (256, 512), (512, 768), (768, 1024))
 PARTS = len(SPANS)
 E_BLOCKS = DV // P
 MASKED = 1.0e30
@@ -53,9 +53,6 @@ def tile_attend_x_ks_draft_kernel(tc, qT, kT, vT, ks, vs, pos, qpos, offs, out):
         def gather_scalar(dst, window, a, z):
             nc.scalar.activation(dst, window[:].indirect(offsets[:, a // 16 : z // 16]), ACT.Copy)
 
-        warm = keep.tile([P, 1], F32, name="warm")
-        nc.gpsimd.memset(warm[:], 0.0)
-        nc.scalar.activation(warm[:], warm[:], ACT.Exp)
         ident = keep.tile([P, P], F32, name="ident")
         make_identity(nc, ident[:])
         table = {}
@@ -167,7 +164,8 @@ def tile_attend_x_ks_draft_kernel(tc, qT, kT, vT, ks, vs, pos, qpos, offs, out):
             cut = z - (256 if i == PARTS - 1 else 0)
             if cut < z:
                 nc.scalar.copy(out=k_bf[i][:, cut - a : z - a, PAIR:PACK], in_=k_last[:, :, cut:z].rearrange("p t n -> p n t"))
-            nc.vector.tensor_copy(out=k_bf[i][:, 0 : cut - a, PAIR:PACK], in_=k_last[:, :, a:cut].rearrange("p t n -> p n t"))
+            if cut > a:
+                nc.vector.tensor_copy(out=k_bf[i][:, 0 : cut - a, PAIR:PACK], in_=k_last[:, :, a:cut].rearrange("p t n -> p n t"))
 
         def quantize_k(i):
             quantize(k_codes[i], k_scales[i], k_bf[i][:].rearrange("p n t -> p (n t)"))
@@ -179,8 +177,7 @@ def tile_attend_x_ks_draft_kernel(tc, qT, kT, vT, ks, vs, pos, qpos, offs, out):
         build_masks(pos_got)
         ks_turned = turn_table("ks", ks_got, 6, chunk)
         gather_first(0, gather_scalar, 0, B * N)
-        gather_first(1, gather_scalar, 0, 512)
-        gather_first(1, gather_vector, 512, B * N)
+        gather_first(1, gather_scalar, 0, 1024)
         for i in range(PARTS):
             interleave_first(i)
         vs_turned = turn_table("vs", vs_got, 7, dealt)
@@ -218,7 +215,7 @@ def tile_attend_x_ks_draft_kernel(tc, qT, kT, vT, ks, vs, pos, qpos, offs, out):
                     out=ps[:, kc], lhsT=k_codes[i][:, kc].bitcast(FP8X4), lhsT_scale=k_scales[i][:, kc],
                     rhs=q_codes[s][:].bitcast(FP8X4), rhs_scale=q_scales[s][:], start=True, stop=True,
                 )
-            if i in (0, 1):
+            if i in ():
                 nc.vector.tensor_tensor(
                     scaled[i][:], ps[:, 0 : count * P].rearrange("p (c q) -> p c q", q=NQ),
                     nks_col[:, first : first + count].unsqueeze(2).to_broadcast([P, count, NQ]), ALU.mult,
@@ -247,16 +244,21 @@ def tile_attend_x_ks_draft_kernel(tc, qT, kT, vT, ks, vs, pos, qpos, offs, out):
         def exponent(s):
             last = part_of[(s + 1) * CHUNKS - 1]
             whole = SPANS[last][1] - SPANS[last][0] == N
-            source = (score[last] if whole else kept[s])[:].rearrange("q (n t) -> q t n", t=PACK)
             step = PACK // EXPS
             for u in range(EXPS):
+                places = slice(u * step, (u + 1) * step)
+                if whole:
+                    dst, src = prob[s][:, places, :], score[last][:].rearrange("q (n t) -> q t n", t=PACK)[:, places, :]
+                else:
+                    dst = prob[s][:, places, :].rearrange("q t n -> q n t")
+                    src = kept[s][:].rearrange("q (n t) -> q n t", t=PACK)[:, :, places]
                 nc.scalar.activation(
-                    prob[s][:, u * step : (u + 1) * step, :], source[:, u * step : (u + 1) * step, :],
+                    dst, src,
                     ACT.Exp, bias=lowest[last][:], scale=-1.0, accum_out=sums[s][:, u : u + 1],
                 )
 
         def turn_prob(s):
-            ps = bank(s + 2)
+            ps = bank(6 + s)
             for t in range(PACK):
                 nc.tensor.transpose(ps[:, t * P : (t + 1) * P], prob[s][:, t, :], ident[:])
             turned[s] = ps
@@ -269,7 +271,8 @@ def tile_attend_x_ks_draft_kernel(tc, qT, kT, vT, ks, vs, pos, qpos, offs, out):
             quantize(w_codes[s], w_scales[s], w_bf[s][:].rearrange("p q t -> p (q t)"))
 
         def row_sum(s):
-            nc.vector.reciprocal(inv[s][:], sums[s][:])
+            nc.vector.tensor_reduce(total[s][:], sums[s][:], mybir.AxisListType.X, ALU.add)
+            nc.vector.reciprocal(inv[s][:], total[s][:])
 
         def gather_v(e, seqs, name, gather):
             got = keep.tile([P, len(seqs) * N], BF16, name=name, align_bytes=64)
@@ -278,7 +281,7 @@ def tile_attend_x_ks_draft_kernel(tc, qT, kT, vT, ks, vs, pos, qpos, offs, out):
                 v_got[e, s] = got[:, (s - seqs[0]) * N : (s - seqs[0] + 1) * N]
 
         def turn_v(e, s):
-            ps = bank(4 + 2 * e + s)
+            ps = bank(4 - 4 * e + s)
             words = v_got[e, s].bitcast(F32)
             for u in range(PAIR):
                 nc.tensor.transpose(ps[:, u * P : (u + 1) * P], words[:, u : N // 2 : PAIR], ident[:])
@@ -291,7 +294,7 @@ def tile_attend_x_ks_draft_kernel(tc, qT, kT, vT, ks, vs, pos, qpos, offs, out):
             quantize(v_codes[s][:, block], v_scales[s][:, block], v_bf[s][:, e * P * PACK : (e + 1) * P * PACK])
 
         def values(s):
-            ps = bank(s)
+            ps = bank(2 + s)
             nc.tensor.matmul_mx(
                 out=ps[:, 0:DV], lhsT=w_codes[s][:].bitcast(FP8X4), lhsT_scale=w_scales[s][:],
                 rhs=v_codes[s][:].bitcast(FP8X4), rhs_scale=v_scales[s][:], start=True, stop=True,
@@ -310,15 +313,16 @@ def tile_attend_x_ks_draft_kernel(tc, qT, kT, vT, ks, vs, pos, qpos, offs, out):
                 interleave_q(1, nc.scalar.copy)
                 quantize_q(1)
             scores(i)
+            if i == 0:
+                vs_col = keep_columns("k_codes0", vs_turned, 1.0)
             row_min(i)
-        vs_col = keep_columns("k_codes1", vs_turned, 1.0)
         for s in range(B):
             exponent(s)
             turn_prob(s)
             weights(s)
         gather_v(0, (0, 1), "v_got0", gather_scalar)
         gather_v(1, (0,), "v_got1", gather_scalar)
-        gather_v(1, (1,), "scaled1", gather_vector)
+        gather_v(1, (1,), "scaled0", gather_vector)
         for e in range(E_BLOCKS):
             for s in range(B):
                 turn_v(e, s)

@@ -14,17 +14,15 @@ ACT = mybir.ActivationFunctionType
 
 B, NQ, D, DV, N, T = 2, 128, 512, 256, 512, 2048
 P = 128
-ROW = {"pos": 127, "ks": 127, "vs": 127}
+ROW = P - 1
 PACK = 4
 PAIR = PACK // 2
 CHUNKS = N // P
-H = N // 2
-EXPS = 2
-SPANS = ((0, 256), (256, 512), (512, 768), (768, 1024))
-PARTS = len(SPANS)
+PART = 256
+PARTS = B * N // PART
+PER_PART = PART // P
 E_BLOCKS = DV // P
 MASKED = 1.0e30
-FILL_VECTOR = {"pos": T, "ks": 0, "vs": T // 2}
 FIRST_FILL = 256
 SHIFT = 16
 
@@ -41,8 +39,11 @@ def tile_attend_x_ks_draft_kernel(tc, qT, kT, vT, ks, vs, pos, qpos, offs, out):
         def bank(index):
             return psum.tile([P, 512], F32, name=f"bank{index}")
 
+        def tile(shape, dtype, name):
+            return keep.tile(shape, dtype, name=name, align_bytes=64)
+
         def tiles(count, shape, dtype, name):
-            return [keep.tile(shape, dtype, name=f"{name}{i}", align_bytes=64) for i in range(count)]
+            return [tile(shape, dtype, f"{name}{i}") for i in range(count)]
 
         offsets = keep.tile([P, B * N // 16], U16, name="offsets")
         nc.sync.dma_start(offsets[:], offs)
@@ -53,248 +54,221 @@ def tile_attend_x_ks_draft_kernel(tc, qT, kT, vT, ks, vs, pos, qpos, offs, out):
         def gather_scalar(dst, window, a, z):
             nc.scalar.activation(dst, window[:].indirect(offsets[:, a // 16 : z // 16]), ACT.Copy)
 
-        ident = keep.tile([P, P], F32, name="ident")
+        warm = tile([P, 1], F32, "warm")
+        warm_out = tile([P, 1], F32, "warm_out")
+        nc.vector.memset(warm[:], 0.0)
+        nc.scalar.activation(warm_out[:], warm[:], ACT.Exp)
+        ident = tile([P, P], F32, "ident")
         make_identity(nc, ident[:])
-        table = {}
-        q_place = keep.tile([P, B], F32, name="q_place")
+        table = {name: tile([P, T], F32, name + "_table") for name in ("pos", "ks", "vs")}
+        q_place = tile([P, B], F32, "q_place")
+
+        def fill(engine, name, a, z):
+            engine.memset(table[name][0:ROW, a:z].bitcast(U32), 0)
+
+        fill(nc.vector, "pos", 0, T)
+        fill(nc.gpsimd, "ks", 0, FIRST_FILL)
+        fill(nc.gpsimd, "ks", FIRST_FILL, T)
+        fill(nc.vector, "vs", 0, T // 2)
+        fill(nc.gpsimd, "vs", T // 2, T)
         for name, source in (("pos", pos), ("ks", ks), ("vs", vs)):
-            table[name] = keep.tile([P, T], F32, name=name + "_table")
-            row = ROW[name]
-            cut = FILL_VECTOR[name]
-            if cut > 0:
-                nc.vector.memset(table[name][0 : row, 0:cut].bitcast(U32), 0)
-            if cut == 0:
-                cut = FIRST_FILL
-                nc.gpsimd.memset(table[name][0 : row, 0:cut].bitcast(U32), 0)
-            if cut < T:
-                nc.gpsimd.memset(table[name][0 : row, cut:T].bitcast(U32), 0)
-            nc.sync.dma_start(table[name][row : row + 1, :], source[0:1, :])
-            if name == "pos":
-                nc.scalar.dma_start(q_place[:], qpos.rearrange("b q o -> q (b o)"))
-        q_raw = tiles(B, [P, PACK, NQ], F32, "q_raw")
+            nc.sync.dma_start(table[name][ROW:P, :], source[0:1, :])
+        nc.scalar.dma_start(q_place[:], qpos.rearrange("b q o -> q (b o)"))
         k_rows = kT.rearrange("(p t) n -> p t n", t=PACK)
         k_pool = tiles(PACK, [P, T], F32, "k_pool")
-
-        def load_q(s):
-            nc.sync.dma_start(q_raw[s][:], qT[s].rearrange("(p t) q -> p t q", t=PACK))
-
         for t in range(PACK):
             nc.sync.dma_start(k_pool[t][:], k_rows[:, t, :])
+        q_raw = tiles(B, [P, PACK, NQ], F32, "q_raw")
         for s in range(B):
-            load_q(s)
-
-
+            nc.sync.dma_start(q_raw[s][:], qT[s].rearrange("(p t) q -> p t q", t=PACK))
+        v_pool = tiles(E_BLOCKS, [P, T], F32, "v_pool")
+        for e in range(E_BLOCKS):
+            nc.sync.dma_start(v_pool[e][:], vT[e * P : (e + 1) * P, :])
         q_row = bank(4)
         for s in range(B):
             nc.tensor.transpose(q_row[:, s * NQ : (s + 1) * NQ], q_place[:, s : s + 1].to_broadcast([P, P]), ident[:])
 
-        def gather_table(name, gather):
-            got = keep.tile([P, B * N], F32, name=name + "_got")
-            gather(got[:], table[name], 0, B * N)
-            return got
-
-        def turn_table(name, got, index, pick):
+        def turn(got, index):
             ps = bank(index)
-            row = ROW[name]
-            for j in range(B * CHUNKS) if row < SHIFT else reversed(range(B * CHUNKS)):
-                nc.tensor.transpose(ps[:, j * SHIFT : j * SHIFT + P], got[:, pick(j // CHUNKS, j % CHUNKS)], ident[:])
-            return ps[:, row : row + B * CHUNKS * SHIFT : SHIFT]
+            for j in reversed(range(B * CHUNKS)):
+                nc.tensor.transpose(ps[:, j * SHIFT : j * SHIFT + P], got[:, j * P : (j + 1) * P], ident[:])
+            return ps[:, ROW : ROW + B * CHUNKS * SHIFT : SHIFT]
 
-        def keep_columns(name, columns, scale):
-            col = keep.tile([P, B * CHUNKS], F32, name=name, align_bytes=64)
-            nc.vector.tensor_scalar(col[:], columns, scale, None, ALU.mult)
-            return col
+        pos_got = tile([P, B * N], F32, "pos_got")
+        ks_got = tile([P, B * N], F32, "ks_got")
+        vs_got = tile([P, B * N], F32, "vs_got")
+        gather_scalar(pos_got[:], table["pos"], 0, B * N)
+        gather_vector(ks_got[:], table["ks"], 0, B * N)
+        gather_vector(vs_got[:].rearrange("p (s t c) -> p s c t", s=B, t=PACK), table["vs"], 0, B * N)
 
-        def chunk(s, c):
-            return slice(s * N + c * P, s * N + (c + 1) * P)
+        score = [bank(i) for i in range(PARTS)]
+        q_row_sb = tile([P, B * NQ], F32, "q_row_sb")
+        nc.scalar.copy(out=q_row_sb[:], in_=q_row[:, 0 : B * NQ])
+        pos_col = turn(pos_got, 5)
+        ks_turned = turn(ks_got, 6)
+        limit = tile([P, B * CHUNKS, NQ], F32, "vs_table")
+        for j in range(B * CHUNKS):
+            s, c = j // CHUNKS, j % PER_PART
+            nc.vector.tensor_scalar(
+                limit[:, j, :], q_row_sb[:, s * NQ : (s + 1) * NQ], pos_col[:, j : j + 1], MASKED, ALU.is_lt, ALU.mult
+            )
+            nc.tensor.matmul(
+                score[j // PER_PART][:, c * P : (c + 1) * P], limit[:, j, :], ident[:], is_transpose=True, start=c == 0, stop=False
+            )
+        vs_turned = turn(vs_got, 7)
+        nks_col = tile([P, B * CHUNKS], F32, "nks_col")
+        vs_col = tile([P, B * CHUNKS], F32, "vs_col")
+        nc.vector.tensor_scalar(nks_col[:], ks_turned, -1.0, None, ALU.mult)
+        nc.vector.tensor_copy(vs_col[:], vs_turned)
 
-        def dealt(s, t):
-            return slice(s * N + t, (s + 1) * N, PACK)
+        k_first = tile([P, PAIR, B * N], BF16, "k_first")
+        k_bf = tiles(PARTS, [P, PART, PACK], BF16, "k_bf")
+        k_codes = tiles(PARTS, [P, PART], U32, "k_codes")
+        k_scales = tiles(PARTS, [P, PART], U8, "k_scales")
+        k_pair = tile([P, PAIR, B * N], BF16, "k_pair")
+        for t in range(PAIR):
+            gather_scalar(k_first[:, t, :], k_pool[t], 0, B * N)
+        for i in range(PARTS):
+            nc.vector.tensor_copy(
+                out=k_bf[i][:, :, 0:PAIR], in_=k_first[:, :, i * PART : (i + 1) * PART].rearrange("p t n -> p n t")
+            )
+        gather_scalar(k_pair[:, 0, :], k_pool[2], 0, B * N)
 
         q_bf = tiles(B, [P, NQ, PACK], BF16, "q_bf")
         q_codes = tiles(B, [P, NQ], U32, "q_codes")
         q_scales = tiles(B, [P, NQ], U8, "q_scales")
-
-        def interleave_q(s, copy):
-            copy(out=q_bf[s][:], in_=q_raw[s][:].rearrange("p t q -> p q t"))
-
-        def quantize(codes, scales, values):
-            nc.vector.quantize_mx(out=codes[:].bitcast(FP8X4), scales=scales[:], in_=values)
-
-        def quantize_q(s):
-            quantize(q_codes[s], q_scales[s], q_bf[s][:].rearrange("p q t -> p (q t)"))
-
-        score = [bank(i) for i in range(PARTS)]
-        part_of = [i for i, (a, z) in enumerate(SPANS) for j in range(a // P, z // P)]
-
-        def build_masks(pos_got):
-            q_row_sb = keep.tile([P, B * NQ], F32, name="q_row_sb")
-            nc.scalar.copy(out=q_row_sb[:], in_=q_row[:, 0 : B * NQ])
-            pos_col = turn_table("pos", pos_got, 5, chunk)
-            limit = keep.tile([P, B * CHUNKS, NQ], F32, name="vs_table")
-            for j in range(B * CHUNKS):
-                s = j // CHUNKS
-                nc.vector.tensor_scalar(
-                    limit[:, j, :], q_row_sb[:, s * NQ : (s + 1) * NQ], pos_col[:, j : j + 1], MASKED, ALU.is_lt, ALU.mult
-                )
-                c = j - SPANS[part_of[j]][0] // P
-                nc.tensor.matmul(
-                    score[part_of[j]][:, c * P : (c + 1) * P], limit[:, j, :], ident[:], is_transpose=True, start=c == 0, stop=False
-                )
-
-        k_first = keep.tile([P, PAIR, B * N], BF16, name="k_first")
-        k_last = keep.tile([P, PAIR, B * N], BF16, name="k_last", align_bytes=64)
-        k_bf = [keep.tile([P, z - a, PACK], BF16, name=f"k_bf{i}", align_bytes=64) for i, (a, z) in enumerate(SPANS)]
-        k_codes = [keep.tile([P, z - a], U32, name=f"k_codes{i}", align_bytes=64) for i, (a, z) in enumerate(SPANS)]
-        k_scales = [keep.tile([P, z - a], U8, name=f"k_scales{i}", align_bytes=64) for i, (a, z) in enumerate(SPANS)]
-
-        def gather_first(t, gather, a, z):
-            gather(k_first[:, t, a:z], k_pool[t], a, z)
-
-        def gather_last(t, gather, a, z):
-            gather(k_last[:, t - PAIR, a:z], k_pool[t], a, z)
-
-        def interleave_first(i):
-            nc.vector.tensor_copy(
-                out=k_bf[i][:, :, 0:PAIR], in_=k_first[:, :, SPANS[i][0] : SPANS[i][1]].rearrange("p t n -> p n t")
-            )
-
-        def interleave_last(i):
-            a, z = SPANS[i]
-            cut = z - (256 if i == PARTS - 1 else 0)
-            if cut < z:
-                nc.scalar.copy(out=k_bf[i][:, cut - a : z - a, PAIR:PACK], in_=k_last[:, :, cut:z].rearrange("p t n -> p n t"))
-            if cut > a:
-                nc.vector.tensor_copy(out=k_bf[i][:, 0 : cut - a, PAIR:PACK], in_=k_last[:, :, a:cut].rearrange("p t n -> p n t"))
-
-        def quantize_k(i):
-            quantize(k_codes[i], k_scales[i], k_bf[i][:].rearrange("p n t -> p (n t)"))
-
-        pos_got = gather_table("pos", gather_scalar)
-
-        ks_got = gather_table("ks", gather_vector)
-        vs_got = gather_table("vs", gather_vector)
-        build_masks(pos_got)
-        ks_turned = turn_table("ks", ks_got, 6, chunk)
-        gather_first(0, gather_scalar, 0, B * N)
-        gather_first(1, gather_scalar, 0, 1024)
-        for i in range(PARTS):
-            interleave_first(i)
-        vs_turned = turn_table("vs", vs_got, 7, dealt)
-        gather_last(2, gather_scalar, 0, 1024)
-        gather_last(3, gather_vector, 0, N)
-        gather_last(3, gather_scalar, N, B * N)
-
-        v_pool = tiles(E_BLOCKS, [P, T], F32, "v_pool")
-        for e in range(E_BLOCKS):
-            nc.sync.dma_start(v_pool[e][:], vT[e * P : (e + 1) * P, :])
-        scaled = [keep.tile([P, (z - a) // P, NQ], F32, name=f"scaled{i}", align_bytes=64) for i, (a, z) in enumerate(SPANS)]
+        scaled = {i: tile([P, PART], F32, f"scaled{i}")[:] for i in range(PARTS // 2)}
         lowest = tiles(PARTS, [P, 1], F32, "lowest")
-        kept = tiles(B, [P, N], F32, "kept")
-        sums = tiles(B, [P, EXPS], F32, "sums")
+        kept = {1: tile([P, N], F32, "kept1")[:]}
+        sums = tiles(B, [P, PAIR], F32, "sums")
         total = tiles(B, [P, 1], F32, "total")
         inv = tiles(B, [P, 1], F32, "inv")
-        prob = tiles(B, [P, PACK, P], F32, "prob")
         w_bf = tiles(B, [P, NQ, PACK], BF16, "w_bf")
         w_codes = tiles(B, [P, NQ], U32, "w_codes")
         w_scales = tiles(B, [P, NQ], U8, "w_scales")
-        v_got = {}
         v_bf = tiles(B, [P, DV * PACK], BF16, "v_bf")
         v_codes = tiles(B, [P, DV], U32, "v_codes")
         v_scales = tiles(B, [P, DV], U8, "v_scales")
         result = tiles(B, [P, DV], F32, "result")
-        turned = {}
+        raw, prob, turned, v_words, v_turned = {}, {}, {}, {}, {}
 
-        def scores(i):
-            a, z = SPANS[i]
-            s, first, count = a // N, a // P, (z - a) // P
-            ps = bank(4 + i)
-            for c in range(count):
+        def quantize(codes, scales, values):
+            nc.vector.quantize_mx(out=codes.bitcast(FP8X4), scales=scales, in_=values)
+
+        def gather_last(i, gather):
+            gather(k_pair[:, 1, i * PART : (i + 1) * PART], k_pool[3], i * PART, (i + 1) * PART)
+
+        def weave_last(i, copy):
+            copy(out=k_bf[i][:, :, PAIR:PACK], in_=k_pair[:, :, i * PART : (i + 1) * PART].rearrange("p t n -> p n t"))
+
+        def weave_q(s):
+            nc.vector.tensor_copy(out=q_bf[s][:], in_=q_raw[s][:].rearrange("p t q -> p q t"))
+
+        def quantize_q(s):
+            quantize(q_codes[s][:], q_scales[s][:], q_bf[s][:].rearrange("p q t -> p (q t)"))
+
+        def quantize_k(i):
+            quantize(k_codes[i][:], k_scales[i][:], k_bf[i][:].rearrange("p n t -> p (n t)"))
+
+        def multiply_k(i):
+            s = i * PART // N
+            raw[i] = bank(4 + i)
+            for c in range(PER_PART):
                 kc = slice(c * P, (c + 1) * P)
                 nc.tensor.matmul_mx(
-                    out=ps[:, kc], lhsT=k_codes[i][:, kc].bitcast(FP8X4), lhsT_scale=k_scales[i][:, kc],
+                    out=raw[i][:, kc], lhsT=k_codes[i][:, kc].bitcast(FP8X4), lhsT_scale=k_scales[i][:, kc],
                     rhs=q_codes[s][:].bitcast(FP8X4), rhs_scale=q_scales[s][:], start=True, stop=True,
                 )
-            if i in ():
-                nc.vector.tensor_tensor(
-                    scaled[i][:], ps[:, 0 : count * P].rearrange("p (c q) -> p c q", q=NQ),
-                    nks_col[:, first : first + count].unsqueeze(2).to_broadcast([P, count, NQ]), ALU.mult,
-                )
-            else:
-                for c in range(count):
-                    j = first + c
-                    nc.scalar.activation(scaled[i][:, c, :], ps[:, c * P : (c + 1) * P], ACT.Copy, scale=nks_col[:, j : j + 1])
-            for c in range(count):
+
+        def scale_scalar(i):
+            for c in range(PER_PART):
+                j = i * PER_PART + c
+                nc.scalar.activation(scaled[i][:, c * P : (c + 1) * P], raw[i][:, c * P : (c + 1) * P], ACT.Copy, scale=nks_col[:, j : j + 1])
+
+        def scale_vector(i):
+            for c in range(PER_PART):
+                j = i * PER_PART + c
+                nc.vector.tensor_scalar(scaled[i][:, c * P : (c + 1) * P], raw[i][:, c * P : (c + 1) * P], nks_col[:, j : j + 1], None, ALU.mult)
+
+        def turn_scores(i):
+            for c in range(PER_PART):
                 nc.tensor.matmul(
-                    score[i][:, c * P : (c + 1) * P], scaled[i][:, c, :], ident[:],
-                    is_transpose=True, start=False, stop=c == count - 1,
+                    score[i][:, c * P : (c + 1) * P], scaled[i][:, c * P : (c + 1) * P], ident[:],
+                    is_transpose=True, start=False, stop=c == PER_PART - 1,
                 )
 
         def row_min(i):
-            a, z = SPANS[i]
-            if z - a == N:
-                nc.vector.tensor_reduce(lowest[i][:], score[i][:], mybir.AxisListType.X, ALU.min)
-                return
-            start = lowest[i - 1][:] if a % N else None
+            a = i * PART % N
+            start = lowest[i - 1][:] if a else None
             nc.vector.tensor_scalar(
-                kept[a // N][:, a % N : a % N + z - a], score[i][:, 0 : z - a], 1.0, start, ALU.mult, ALU.min,
-                accum_out=lowest[i][:],
+                kept[i * PART // N][:, a : a + PART], score[i][:, 0:PART], 1.0, start, ALU.mult, ALU.min, accum_out=lowest[i][:]
             )
 
         def exponent(s):
-            last = part_of[(s + 1) * CHUNKS - 1]
-            whole = SPANS[last][1] - SPANS[last][0] == N
-            step = PACK // EXPS
-            for u in range(EXPS):
-                places = slice(u * step, (u + 1) * step)
-                if whole:
-                    dst, src = prob[s][:, places, :], score[last][:].rearrange("q (n t) -> q t n", t=PACK)[:, places, :]
-                else:
-                    dst = prob[s][:, places, :].rearrange("q t n -> q n t")
-                    src = kept[s][:].rearrange("q (n t) -> q n t", t=PACK)[:, :, places]
+            prob[s] = tile([P, PACK, P], F32, f"prob{s}")
+            last = (s + 1) * N // PART - 1
+            for u in range(PAIR):
+                places = slice(u * PAIR, (u + 1) * PAIR)
                 nc.scalar.activation(
-                    dst, src,
+                    prob[s][:, places, :].rearrange("q t n -> q n t"),
+                    kept[s].rearrange("q (n t) -> q n t", t=PACK)[:, :, places],
                     ACT.Exp, bias=lowest[last][:], scale=-1.0, accum_out=sums[s][:, u : u + 1],
                 )
 
         def turn_prob(s):
-            ps = bank(6 + s)
+            turned[s] = bank(2 * s)
             for t in range(PACK):
-                nc.tensor.transpose(ps[:, t * P : (t + 1) * P], prob[s][:, t, :], ident[:])
-            turned[s] = ps
+                nc.tensor.transpose(turned[s][:, t * P : (t + 1) * P], prob[s][:, t, :], ident[:])
 
         def weights(s):
             nc.vector.tensor_tensor(
                 w_bf[s][:], turned[s][:].rearrange("p (t q) -> p q t", t=PACK),
                 vs_col[:, s * PACK : (s + 1) * PACK].unsqueeze(1).to_broadcast([P, NQ, PACK]), ALU.mult,
             )
-            quantize(w_codes[s], w_scales[s], w_bf[s][:].rearrange("p q t -> p (q t)"))
+
+        def quantize_w(s):
+            quantize(w_codes[s][:], w_scales[s][:], w_bf[s][:].rearrange("p q t -> p (q t)"))
 
         def row_sum(s):
             nc.vector.tensor_reduce(total[s][:], sums[s][:], mybir.AxisListType.X, ALU.add)
             nc.vector.reciprocal(inv[s][:], total[s][:])
 
-        def gather_v(e, seqs, name, gather):
-            got = keep.tile([P, len(seqs) * N], BF16, name=name, align_bytes=64)
-            gather(got[:], v_pool[e], seqs[0] * N, (seqs[-1] + 1) * N)
-            for s in seqs:
-                v_got[e, s] = got[:, (s - seqs[0]) * N : (s - seqs[0] + 1) * N]
+        def gather_v_vector(e, s):
+            got = tile([P, N], BF16, f"v_got{e}{s}")
+            gather_vector(got[:].rearrange("p (u c two) -> p c u two", u=PAIR, two=2), v_pool[e], s * N, (s + 1) * N)
+            words = got[:].bitcast(F32)
+            v_words[e, s] = [words[:, u * P : (u + 1) * P] for u in range(PAIR)]
+
+        def gather_v_scalar(e, s):
+            got = tile([P, N], BF16, f"v_got{e}{s}")
+            gather_scalar(got[:], v_pool[e], s * N, (s + 1) * N)
+            words = got[:].bitcast(F32)
+            v_words[e, s] = [words[:, u : N // 2 : PAIR] for u in range(PAIR)]
+
+        def reuse_first_values():
+            spare = tile([P, T], F32, "v_pool0")
+            kept[0] = spare[:, 0:N]
+            for i in range(PARTS // 2, PARTS):
+                scaled[i] = spare[:, N + (i - 2) * PART : N + (i - 1) * PART]
 
         def turn_v(e, s):
-            ps = bank(4 - 4 * e + s)
-            words = v_got[e, s].bitcast(F32)
+            v_turned[e, s] = bank(4 + 2 * e + s)
             for u in range(PAIR):
-                nc.tensor.transpose(ps[:, u * P : (u + 1) * P], words[:, u : N // 2 : PAIR], ident[:])
+                nc.tensor.transpose(v_turned[e, s][:, u * P : (u + 1) * P], v_words[e, s][u], ident[:])
+
+        def copy_v(e, s):
             place = v_bf[s][:].bitcast(F32)[:, e * P * PAIR : (e + 1) * P * PAIR]
             nc.scalar.copy(
                 out=place.rearrange("p (c u) -> p c u", u=PAIR),
-                in_=ps[:, 0 : PAIR * P].rearrange("p (u c) -> p c u", u=PAIR),
+                in_=v_turned[e, s][:, 0 : PAIR * P].rearrange("p (u c) -> p c u", u=PAIR),
             )
+
+        def quantize_v(e, s):
             block = slice(e * P, (e + 1) * P)
             quantize(v_codes[s][:, block], v_scales[s][:, block], v_bf[s][:, e * P * PACK : (e + 1) * P * PACK])
 
         def values(s):
-            ps = bank(2 + s)
+            ps = bank(2 * s + 1)
             nc.tensor.matmul_mx(
                 out=ps[:, 0:DV], lhsT=w_codes[s][:].bitcast(FP8X4), lhsT_scale=w_scales[s][:],
                 rhs=v_codes[s][:].bitcast(FP8X4), rhs_scale=v_scales[s][:], start=True, stop=True,
@@ -302,30 +276,61 @@ def tile_attend_x_ks_draft_kernel(tc, qT, kT, vT, ks, vs, pos, qpos, offs, out):
             nc.scalar.activation(result[s][:], ps[:, 0:DV], ACT.Copy, scale=inv[s][:])
             nc.sync.dma_start(out[s], result[s][:])
 
-        nks_col = keep_columns("k_pool3", ks_turned, -1.0)
+        gather_last(0, gather_vector)
+        for i in range(1, PARTS):
+            gather_last(i, gather_scalar)
+        weave_q(0)
+        weave_last(0, nc.vector.tensor_copy)
+        weave_last(1, nc.vector.tensor_copy)
+        weave_last(2, nc.scalar.copy)
+        weave_last(3, nc.scalar.copy)
+        quantize_q(0)
+        quantize_k(0)
+        quantize_k(1)
+        weave_q(1)
+        quantize_k(2)
+        quantize_q(1)
+        quantize_k(3)
         for i in range(PARTS):
-            interleave_last(i)
-            quantize_k(i)
-            if i == 0:
-                interleave_q(0, nc.vector.tensor_copy)
-                quantize_q(0)
-            if SPANS[i][0] == N:
-                interleave_q(1, nc.scalar.copy)
-                quantize_q(1)
-            scores(i)
-            if i == 0:
-                vs_col = keep_columns("k_codes0", vs_turned, 1.0)
-            row_min(i)
-        for s in range(B):
-            exponent(s)
-            turn_prob(s)
-            weights(s)
-        gather_v(0, (0, 1), "v_got0", gather_scalar)
-        gather_v(1, (0,), "v_got1", gather_scalar)
-        gather_v(1, (1,), "scaled0", gather_vector)
-        for e in range(E_BLOCKS):
-            for s in range(B):
-                turn_v(e, s)
-        for s in range(B):
-            row_sum(s)
-            values(s)
+            multiply_k(i)
+        scale_scalar(0)
+        scale_scalar(1)
+        gather_v_vector(0, 0)
+        gather_v_scalar(0, 1)
+        reuse_first_values()
+        turn_scores(0)
+        turn_scores(1)
+        row_min(0)
+        row_min(1)
+        scale_scalar(2)
+        scale_vector(3)
+        turn_scores(2)
+        turn_scores(3)
+        row_min(2)
+        row_min(3)
+        exponent(0)
+        gather_v_vector(1, 0)
+        gather_v_scalar(1, 1)
+        turn_v(0, 0)
+        turn_prob(0)
+        turn_v(0, 1)
+        weights(0)
+        exponent(1)
+        turn_prob(1)
+        turn_v(1, 0)
+        turn_v(1, 1)
+        copy_v(0, 0)
+        copy_v(0, 1)
+        quantize_v(0, 0)
+        quantize_v(0, 1)
+        quantize_w(0)
+        row_sum(0)
+        weights(1)
+        copy_v(1, 0)
+        copy_v(1, 1)
+        quantize_v(1, 0)
+        quantize_v(1, 1)
+        quantize_w(1)
+        row_sum(1)
+        values(0)
+        values(1)

@@ -88,10 +88,16 @@ def tile_attend_x_ks_draft_kernel(tc, qT, kT, vT, ks, vs, pos, qpos, offs, out):
         for s in range(B):
             nc.tensor.transpose(q_row[:, s * NQ : (s + 1) * NQ], q_place[:, s : s + 1].to_broadcast([P, P]), ident[:])
 
-        def turn(got, index):
+        def chunk(j):
+            return slice(j * P, (j + 1) * P)
+
+        def dealt(j):
+            return slice(j // PACK * N + j % PACK, (j // PACK + 1) * N, PACK)
+
+        def turn(got, index, pick):
             ps = bank(index)
             for j in reversed(range(B * CHUNKS)):
-                nc.tensor.transpose(ps[:, j * SHIFT : j * SHIFT + P], got[:, j * P : (j + 1) * P], ident[:])
+                nc.tensor.transpose(ps[:, j * SHIFT : j * SHIFT + P], got[:, pick(j)], ident[:])
             return ps[:, ROW : ROW + B * CHUNKS * SHIFT : SHIFT]
 
         pos_got = tile([P, B * N], F32, "pos_got")
@@ -99,13 +105,13 @@ def tile_attend_x_ks_draft_kernel(tc, qT, kT, vT, ks, vs, pos, qpos, offs, out):
         vs_got = tile([P, B * N], F32, "vs_got")
         gather_scalar(pos_got[:], table["pos"], 0, B * N)
         gather_vector(ks_got[:], table["ks"], 0, B * N)
-        gather_vector(vs_got[:].rearrange("p (s t c) -> p s c t", s=B, t=PACK), table["vs"], 0, B * N)
+        gather_vector(vs_got[:], table["vs"], 0, B * N)
 
         score = [bank(i) for i in range(PARTS)]
         q_row_sb = tile([P, B * NQ], F32, "q_row_sb")
         nc.scalar.copy(out=q_row_sb[:], in_=q_row[:, 0 : B * NQ])
-        pos_col = turn(pos_got, 5)
-        ks_turned = turn(ks_got, 6)
+        pos_col = turn(pos_got, 5, chunk)
+        ks_turned = turn(ks_got, 6, chunk)
         limit = tile([P, B * CHUNKS, NQ], F32, "vs_table")
         for j in range(B * CHUNKS):
             s, c = j // CHUNKS, j % PER_PART
@@ -115,7 +121,7 @@ def tile_attend_x_ks_draft_kernel(tc, qT, kT, vT, ks, vs, pos, qpos, offs, out):
             nc.tensor.matmul(
                 score[j // PER_PART][:, c * P : (c + 1) * P], limit[:, j, :], ident[:], is_transpose=True, start=c == 0, stop=False
             )
-        vs_turned = turn(vs_got, 7)
+        vs_turned = turn(vs_got, 7, dealt)
         nks_col = tile([P, B * CHUNKS], F32, "nks_col")
         vs_col = tile([P, B * CHUNKS], F32, "vs_col")
         nc.vector.tensor_scalar(nks_col[:], ks_turned, -1.0, None, ALU.mult)
@@ -233,15 +239,9 @@ def tile_attend_x_ks_draft_kernel(tc, qT, kT, vT, ks, vs, pos, qpos, offs, out):
             nc.vector.tensor_reduce(total[s][:], sums[s][:], mybir.AxisListType.X, ALU.add)
             nc.vector.reciprocal(inv[s][:], total[s][:])
 
-        def gather_v_vector(e, s):
+        def gather_v(e, s, gather):
             got = tile([P, N], BF16, f"v_got{e}{s}")
-            gather_vector(got[:].rearrange("p (u c two) -> p c u two", u=PAIR, two=2), v_pool[e], s * N, (s + 1) * N)
-            words = got[:].bitcast(F32)
-            v_words[e, s] = [words[:, u * P : (u + 1) * P] for u in range(PAIR)]
-
-        def gather_v_scalar(e, s):
-            got = tile([P, N], BF16, f"v_got{e}{s}")
-            gather_scalar(got[:], v_pool[e], s * N, (s + 1) * N)
+            gather(got[:], v_pool[e], s * N, (s + 1) * N)
             words = got[:].bitcast(F32)
             v_words[e, s] = [words[:, u : N // 2 : PAIR] for u in range(PAIR)]
 
@@ -295,8 +295,8 @@ def tile_attend_x_ks_draft_kernel(tc, qT, kT, vT, ks, vs, pos, qpos, offs, out):
             multiply_k(i)
         scale_scalar(0)
         scale_scalar(1)
-        gather_v_vector(0, 0)
-        gather_v_scalar(0, 1)
+        gather_v(0, 0, gather_vector)
+        gather_v(0, 1, gather_scalar)
         reuse_first_values()
         turn_scores(0)
         turn_scores(1)
@@ -309,8 +309,8 @@ def tile_attend_x_ks_draft_kernel(tc, qT, kT, vT, ks, vs, pos, qpos, offs, out):
         row_min(2)
         row_min(3)
         exponent(0)
-        gather_v_vector(1, 0)
-        gather_v_scalar(1, 1)
+        gather_v(1, 0, gather_vector)
+        gather_v(1, 1, gather_scalar)
         turn_v(0, 0)
         turn_prob(0)
         turn_v(0, 1)

@@ -71,9 +71,9 @@ def tile_attend_x_ks_draft_kernel(tc, qT, kT, vT, ks, vs, pos, qpos, offs, out):
         fill(nc.gpsimd, "ks", FIRST_FILL, T)
         fill(nc.vector, "vs", 0, T // 2)
         fill(nc.gpsimd, "vs", T // 2, T)
+        nc.sync.dma_start(q_place[:], qpos.rearrange("b q o -> q (b o)"))
         for name, source in (("pos", pos), ("ks", ks), ("vs", vs)):
             nc.sync.dma_start(table[name][ROW:P, :], source[0:1, :])
-        nc.scalar.dma_start(q_place[:], qpos.rearrange("b q o -> q (b o)"))
         k_rows = kT.rearrange("(p t) n -> p t n", t=PACK)
         k_pool = tiles(PACK, [P, T], F32, "k_pool")
         for t in range(PACK):

@@ -107,19 +107,16 @@ def tile_attend_x_ks_draft_kernel(tc, qT, kT, vT, ks, vs, pos, qpos, offs, out):
         gather_vector(ks_got[:], table["ks"], 0, B * N)
         gather_vector(vs_got[:], table["vs"], 0, B * N)
 
-        score = [bank(i) for i in range(PARTS)]
+        score = {}
         q_row_sb = tile([P, B * NQ], F32, "q_row_sb")
         nc.scalar.copy(out=q_row_sb[:], in_=q_row[:, 0 : B * NQ])
         pos_col = turn(pos_got, 5, chunk)
         ks_turned = turn(ks_got, 6, chunk)
         limit = tile([P, B * CHUNKS, NQ], F32, "vs_table")
         for j in range(B * CHUNKS):
-            s, c = j // CHUNKS, j % PER_PART
+            s = j // CHUNKS
             nc.vector.tensor_scalar(
                 limit[:, j, :], q_row_sb[:, s * NQ : (s + 1) * NQ], pos_col[:, j : j + 1], MASKED, ALU.is_lt, ALU.mult
-            )
-            nc.tensor.matmul(
-                score[j // PER_PART][:, c * P : (c + 1) * P], limit[:, j, :], ident[:], is_transpose=True, start=c == 0, stop=False
             )
         vs_turned = turn(vs_got, 7, dealt)
         nks_col = tile([P, B * CHUNKS], F32, "nks_col")
@@ -186,22 +183,18 @@ def tile_attend_x_ks_draft_kernel(tc, qT, kT, vT, ks, vs, pos, qpos, offs, out):
                     rhs=q_codes[s][:].bitcast(FP8X4), rhs_scale=q_scales[s][:], start=True, stop=True,
                 )
 
-        def scale_scalar(i):
+        def scale(i):
             for c in range(PER_PART):
                 j = i * PER_PART + c
-                nc.scalar.activation(scaled[i][:, c * P : (c + 1) * P], raw[i][:, c * P : (c + 1) * P], ACT.Copy, scale=nks_col[:, j : j + 1])
-
-        def scale_vector(i):
-            for c in range(PER_PART):
-                j = i * PER_PART + c
-                nc.vector.tensor_scalar(scaled[i][:, c * P : (c + 1) * P], raw[i][:, c * P : (c + 1) * P], nks_col[:, j : j + 1], None, ALU.mult)
+                nc.vector.scalar_tensor_tensor(
+                    scaled[i][:, c * P : (c + 1) * P], raw[i][:, c * P : (c + 1) * P], nks_col[:, j : j + 1], limit[:, j, :],
+                    ALU.mult, ALU.add,
+                )
 
         def turn_scores(i):
+            score[i] = bank(i)
             for c in range(PER_PART):
-                nc.tensor.matmul(
-                    score[i][:, c * P : (c + 1) * P], scaled[i][:, c * P : (c + 1) * P], ident[:],
-                    is_transpose=True, start=False, stop=c == PER_PART - 1,
-                )
+                nc.tensor.transpose(score[i][:, c * P : (c + 1) * P], scaled[i][:, c * P : (c + 1) * P], ident[:])
 
         def row_min(i):
             a = i * PART % N
@@ -293,17 +286,17 @@ def tile_attend_x_ks_draft_kernel(tc, qT, kT, vT, ks, vs, pos, qpos, offs, out):
         quantize_k(3)
         for i in range(PARTS):
             multiply_k(i)
-        scale_scalar(0)
-        scale_scalar(1)
-        gather_v(0, 0, gather_vector)
+        scale(0)
+        scale(1)
+        gather_v(0, 0, gather_scalar)
         gather_v(0, 1, gather_scalar)
         reuse_first_values()
         turn_scores(0)
         turn_scores(1)
         row_min(0)
         row_min(1)
-        scale_scalar(2)
-        scale_vector(3)
+        scale(2)
+        scale(3)
         turn_scores(2)
         turn_scores(3)
         row_min(2)

@@ -111,18 +111,14 @@ def tile_attend_x_ks_draft_kernel(tc, qT, kT, vT, ks, vs, pos, qpos, offs, out):
         q_row_sb = tile([P, B * NQ], F32, "q_row_sb")
         nc.scalar.copy(out=q_row_sb[:], in_=q_row[:, 0 : B * NQ])
         pos_col = turn(pos_got, 5, chunk)
-        ks_turned = turn(ks_got, 6, chunk)
+        ks_turned = turn(ks_got, 3, chunk)
         limit = tile([P, B * CHUNKS, NQ], F32, "vs_table")
         for j in range(B * CHUNKS):
             s = j // CHUNKS
             nc.vector.tensor_scalar(
                 limit[:, j, :], q_row_sb[:, s * NQ : (s + 1) * NQ], pos_col[:, j : j + 1], MASKED, ALU.is_lt, ALU.mult
             )
-        vs_turned = turn(vs_got, 7, dealt)
-        nks_col = tile([P, B * CHUNKS], F32, "nks_col")
-        vs_col = tile([P, B * CHUNKS], F32, "vs_col")
-        nc.vector.tensor_scalar(nks_col[:], ks_turned, -1.0, None, ALU.mult)
-        nc.vector.tensor_copy(vs_col[:], vs_turned)
+        vs_turned = turn(vs_got, 2, dealt)
 
         k_first = tile([P, PAIR, B * N], BF16, "k_first")
         k_bf = tiles(PARTS, [P, PART, PACK], BF16, "k_bf")
@@ -140,16 +136,16 @@ def tile_attend_x_ks_draft_kernel(tc, qT, kT, vT, ks, vs, pos, qpos, offs, out):
         q_bf = tiles(B, [P, NQ, PACK], BF16, "q_bf")
         q_codes = tiles(B, [P, NQ], U32, "q_codes")
         q_scales = tiles(B, [P, NQ], U8, "q_scales")
-        scaled = {i: tile([P, PART], F32, f"scaled{i}")[:] for i in range(PARTS // 2)}
+        scaled = tiles(PARTS, [P, PART], F32, "scaled")
         lowest = tiles(PARTS, [P, 1], F32, "lowest")
-        kept = {1: tile([P, N], F32, "kept1")[:]}
+        kept = tiles(B, [P, N], F32, "kept")
         sums = tiles(B, [P, PAIR], F32, "sums")
         total = tiles(B, [P, 1], F32, "total")
         inv = tiles(B, [P, 1], F32, "inv")
         w_bf = tiles(B, [P, NQ, PACK], BF16, "w_bf")
         w_codes = tiles(B, [P, NQ], U32, "w_codes")
         w_scales = tiles(B, [P, NQ], U8, "w_scales")
-        v_bf = tiles(B, [P, DV * PACK], BF16, "v_bf")
+        v_bf = {}
         v_codes = tiles(B, [P, DV], U32, "v_codes")
         v_scales = tiles(B, [P, DV], U8, "v_scales")
         result = tiles(B, [P, DV], F32, "result")
@@ -187,8 +183,8 @@ def tile_attend_x_ks_draft_kernel(tc, qT, kT, vT, ks, vs, pos, qpos, offs, out):
             for c in range(PER_PART):
                 j = i * PER_PART + c
                 nc.vector.scalar_tensor_tensor(
-                    scaled[i][:, c * P : (c + 1) * P], raw[i][:, c * P : (c + 1) * P], nks_col[:, j : j + 1], limit[:, j, :],
-                    ALU.mult, ALU.add,
+                    scaled[i][:, c * P : (c + 1) * P], raw[i][:, c * P : (c + 1) * P], ks_turned[:, j : j + 1], limit[:, j, :],
+                    ALU.mult, ALU.subtract,
                 )
 
         def turn_scores(i):
@@ -200,17 +196,16 @@ def tile_attend_x_ks_draft_kernel(tc, qT, kT, vT, ks, vs, pos, qpos, offs, out):
             a = i * PART % N
             start = lowest[i - 1][:] if a else None
             nc.vector.tensor_scalar(
-                kept[i * PART // N][:, a : a + PART], score[i][:, 0:PART], 1.0, start, ALU.mult, ALU.min, accum_out=lowest[i][:]
+                kept[i * PART // N][:, a : a + PART], score[i][:, 0:PART], -1.0, start, ALU.mult, ALU.min, accum_out=lowest[i][:]
             )
 
         def exponent(s):
-            prob[s] = tile([P, PACK, P], F32, f"prob{s}")
             last = (s + 1) * N // PART - 1
             for u in range(PAIR):
                 places = slice(u * PAIR, (u + 1) * PAIR)
                 nc.scalar.activation(
                     prob[s][:, places, :].rearrange("q t n -> q n t"),
-                    kept[s].rearrange("q (n t) -> q n t", t=PACK)[:, :, places],
+                    kept[s][:].rearrange("q (n t) -> q n t", t=PACK)[:, :, places],
                     ACT.Exp, bias=lowest[last][:], scale=-1.0, accum_out=sums[s][:, u : u + 1],
                 )
 
@@ -238,27 +233,21 @@ def tile_attend_x_ks_draft_kernel(tc, qT, kT, vT, ks, vs, pos, qpos, offs, out):
             words = got[:].bitcast(F32)
             v_words[e, s] = [words[:, u : N // 2 : PAIR] for u in range(PAIR)]
 
-        def reuse_first_values():
-            spare = tile([P, T], F32, "v_pool0")
-            kept[0] = spare[:, 0:N]
-            for i in range(PARTS // 2, PARTS):
-                scaled[i] = spare[:, N + (i - 2) * PART : N + (i - 1) * PART]
-
         def turn_v(e, s):
             v_turned[e, s] = bank(4 + 2 * e + s)
             for u in range(PAIR):
                 nc.tensor.transpose(v_turned[e, s][:, u * P : (u + 1) * P], v_words[e, s][u], ident[:])
 
-        def copy_v(e, s):
-            place = v_bf[s][:].bitcast(F32)[:, e * P * PAIR : (e + 1) * P * PAIR]
-            nc.scalar.copy(
-                out=place.rearrange("p (c u) -> p c u", u=PAIR),
+        def copy_v(e, s, copy, name):
+            v_bf[e, s] = tile([P, P * PACK], BF16, name)
+            copy(
+                out=v_bf[e, s][:].bitcast(F32).rearrange("p (c u) -> p c u", u=PAIR),
                 in_=v_turned[e, s][:, 0 : PAIR * P].rearrange("p (u c) -> p c u", u=PAIR),
             )
 
         def quantize_v(e, s):
             block = slice(e * P, (e + 1) * P)
-            quantize(v_codes[s][:, block], v_scales[s][:, block], v_bf[s][:, e * P * PACK : (e + 1) * P * PACK])
+            quantize(v_codes[s][:, block], v_scales[s][:, block], v_bf[e, s][:])
 
         def values(s):
             ps = bank(2 * s + 1)
@@ -277,6 +266,8 @@ def tile_attend_x_ks_draft_kernel(tc, qT, kT, vT, ks, vs, pos, qpos, offs, out):
         weave_last(1, nc.vector.tensor_copy)
         weave_last(2, nc.scalar.copy)
         weave_last(3, nc.scalar.copy)
+        vs_col = tile([P, B * CHUNKS], F32, "k_pair")
+        nc.vector.tensor_copy(vs_col[:], vs_turned)
         quantize_q(0)
         quantize_k(0)
         quantize_k(1)
@@ -286,43 +277,32 @@ def tile_attend_x_ks_draft_kernel(tc, qT, kT, vT, ks, vs, pos, qpos, offs, out):
         quantize_k(3)
         for i in range(PARTS):
             multiply_k(i)
-        scale(0)
-        scale(1)
-        gather_v(0, 0, gather_scalar)
-        gather_v(0, 1, gather_scalar)
-        reuse_first_values()
-        turn_scores(0)
-        turn_scores(1)
-        row_min(0)
-        row_min(1)
-        scale(2)
-        scale(3)
-        turn_scores(2)
-        turn_scores(3)
-        row_min(2)
-        row_min(3)
-        exponent(0)
-        gather_v(1, 0, gather_vector)
-        gather_v(1, 1, gather_scalar)
-        turn_v(0, 0)
-        turn_prob(0)
-        turn_v(0, 1)
+        for i in range(PARTS):
+            scale(i)
+        for e in range(E_BLOCKS):
+            for s in range(B):
+                gather_v(e, s, gather_scalar)
+        for i in range(PARTS):
+            turn_scores(i)
+            row_min(i)
+        spare = tile([P, T], F32, "v_pool1")
+        for s in range(B):
+            prob[s] = spare[:, s * N : (s + 1) * N].rearrange("q (t n) -> q t n", t=PACK)
+            exponent(s)
+            turn_prob(s)
+        for e in range(E_BLOCKS):
+            for s in range(B):
+                turn_v(e, s)
         weights(0)
-        exponent(1)
-        turn_prob(1)
-        turn_v(1, 0)
-        turn_v(1, 1)
-        copy_v(0, 0)
-        copy_v(0, 1)
-        quantize_v(0, 0)
-        quantize_v(0, 1)
+        for s in range(B):
+            copy_v(0, s, nc.vector.tensor_copy, f"v_bf{s}")
+            quantize_v(0, s)
         quantize_w(0)
         row_sum(0)
         weights(1)
-        copy_v(1, 0)
-        copy_v(1, 1)
-        quantize_v(1, 0)
-        quantize_v(1, 1)
+        for s in range(B):
+            copy_v(1, s, nc.scalar.copy, f"kept{s}")
+            quantize_v(1, s)
         quantize_w(1)
         row_sum(1)
         values(0)

@@ -137,8 +137,7 @@ def tile_attend_x_ks_draft_kernel(tc, qT, kT, vT, ks, vs, pos, qpos, offs, out):
         q_codes = tiles(B, [P, NQ], U32, "q_codes")
         q_scales = tiles(B, [P, NQ], U8, "q_scales")
         scaled = tiles(PARTS, [P, PART], F32, "scaled")
-        lowest = tiles(PARTS, [P, 1], F32, "lowest")
-        kept = tiles(B, [P, N], F32, "kept")
+        shift = tiles(B, [P, 1], F32, "shift")
         sums = tiles(B, [P, PAIR], F32, "sums")
         total = tiles(B, [P, 1], F32, "total")
         inv = tiles(B, [P, 1], F32, "inv")
@@ -187,30 +186,25 @@ def tile_attend_x_ks_draft_kernel(tc, qT, kT, vT, ks, vs, pos, qpos, offs, out):
                     ALU.mult, ALU.subtract,
                 )
 
-        def turn_scores(i):
-            score[i] = bank(i)
-            for c in range(PER_PART):
-                nc.tensor.transpose(score[i][:, c * P : (c + 1) * P], scaled[i][:, c * P : (c + 1) * P], ident[:])
+        def turn_scores(s):
+            score[s] = bank(s)
+            for c in range(CHUNKS):
+                i, k = divmod(s * CHUNKS + c, PER_PART)
+                nc.tensor.transpose(score[s][:, c * P : (c + 1) * P], scaled[i][:, k * P : (k + 1) * P], ident[:])
 
-        def row_min(i):
-            a = i * PART % N
-            start = lowest[i - 1][:] if a else None
-            nc.vector.tensor_scalar(
-                kept[i * PART // N][:, a : a + PART], score[i][:, 0:PART], -1.0, start, ALU.mult, ALU.min, accum_out=lowest[i][:]
-            )
+        def row_max(s):
+            nc.vector.tensor_reduce(shift[s][:], score[s][:], mybir.AxisListType.X, ALU.max, negate=True)
 
         def exponent(s):
-            last = (s + 1) * N // PART - 1
             for u in range(PAIR):
                 places = slice(u * PAIR, (u + 1) * PAIR)
                 nc.scalar.activation(
-                    prob[s][:, places, :].rearrange("q t n -> q n t"),
-                    kept[s][:].rearrange("q (n t) -> q n t", t=PACK)[:, :, places],
-                    ACT.Exp, bias=lowest[last][:], scale=-1.0, accum_out=sums[s][:, u : u + 1],
+                    prob[s][:, places, :], score[s][:].rearrange("q (n t) -> q t n", t=PACK)[:, places, :],
+                    ACT.Exp, bias=shift[s][:], accum_out=sums[s][:, u : u + 1],
                 )
 
         def turn_prob(s):
-            turned[s] = bank(2 * s)
+            turned[s] = bank(2 + s)
             for t in range(PACK):
                 nc.tensor.transpose(turned[s][:, t * P : (t + 1) * P], prob[s][:, t, :], ident[:])
 
@@ -250,7 +244,7 @@ def tile_attend_x_ks_draft_kernel(tc, qT, kT, vT, ks, vs, pos, qpos, offs, out):
             quantize(v_codes[s][:, block], v_scales[s][:, block], v_bf[e, s][:])
 
         def values(s):
-            ps = bank(2 * s + 1)
+            ps = bank(s)
             nc.tensor.matmul_mx(
                 out=ps[:, 0:DV], lhsT=w_codes[s][:].bitcast(FP8X4), lhsT_scale=w_scales[s][:],
                 rhs=v_codes[s][:].bitcast(FP8X4), rhs_scale=v_scales[s][:], start=True, stop=True,
@@ -282,9 +276,9 @@ def tile_attend_x_ks_draft_kernel(tc, qT, kT, vT, ks, vs, pos, qpos, offs, out):
         for e in range(E_BLOCKS):
             for s in range(B):
                 gather_v(e, s, gather_scalar)
-        for i in range(PARTS):
-            turn_scores(i)
-            row_min(i)
+        for s in range(B):
+            turn_scores(s)
+            row_max(s)
         spare = tile([P, T], F32, "v_pool1")
         for s in range(B):
             prob[s] = spare[:, s * N : (s + 1) * N].rearrange("q (t n) -> q t n", t=PACK)
@@ -301,7 +295,7 @@ def tile_attend_x_ks_draft_kernel(tc, qT, kT, vT, ks, vs, pos, qpos, offs, out):
         row_sum(0)
         weights(1)
         for s in range(B):
-            copy_v(1, s, nc.scalar.copy, f"kept{s}")
+            copy_v(1, s, nc.scalar.copy, f"shift{s}")
             quantize_v(1, s)
         quantize_w(1)
         row_sum(1)

@@ -22,9 +22,13 @@ PART = 256
 PARTS = B * N // PART
 PER_PART = PART // P
 E_BLOCKS = DV // P
-MASKED = 1.0e30
+MASKED = -1.0e30
 FIRST_FILL = 256
 SHIFT = 16
+POOL_BYTES = 4 * T
+PROB_BYTES = 4 * N
+WOVEN_BYTES = 2 * N
+HELD = 2 * POOL_BYTES + WOVEN_BYTES
 
 FLOPS = 2 * B * NQ * N * (D + DV)
 BYTES = 4 * (B * D * NQ + (D + DV) * T + 3 * T + B * NQ + B * NQ * DV) + 2 * P * (B * N // 16)
@@ -34,6 +38,7 @@ def tile_attend_x_ks_draft_kernel(tc, qT, kT, vT, ks, vs, pos, qpos, offs, out):
     nc = tc.nc
     with ExitStack() as ctx:
         keep = ctx.enter_context(tc.tile_pool(name="keep", bufs=1))
+        reuse = ctx.enter_context(tc.tile_pool(name="reuse", bufs=1))
         psum = ctx.enter_context(tc.psum_pool(name="psum", bufs=1))
 
         def bank(index):
@@ -44,6 +49,9 @@ def tile_attend_x_ks_draft_kernel(tc, qT, kT, vT, ks, vs, pos, qpos, offs, out):
 
         def tiles(count, shape, dtype, name):
             return [tile(shape, dtype, f"{name}{i}") for i in range(count)]
+
+        def placed(shape, dtype, name, at):
+            return reuse.tile(shape, dtype, name=name, align_bytes=64, offset=at)
 
         offsets = keep.tile([P, B * N // 16], U16, name="offsets")
         nc.sync.dma_start(offsets[:], offs)
@@ -81,7 +89,7 @@ def tile_attend_x_ks_draft_kernel(tc, qT, kT, vT, ks, vs, pos, qpos, offs, out):
         q_raw = tiles(B, [P, PACK, NQ], F32, "q_raw")
         for s in range(B):
             nc.sync.dma_start(q_raw[s][:], qT[s].rearrange("(p t) q -> p t q", t=PACK))
-        v_pool = tiles(E_BLOCKS, [P, T], F32, "v_pool")
+        v_pool = [placed([P, T], F32, f"v_pool{e}", e * POOL_BYTES) for e in range(E_BLOCKS)]
         for e in range(E_BLOCKS):
             nc.sync.dma_start(v_pool[e][:], vT[e * P : (e + 1) * P, :])
         q_row = bank(4)
@@ -112,13 +120,19 @@ def tile_attend_x_ks_draft_kernel(tc, qT, kT, vT, ks, vs, pos, qpos, offs, out):
         nc.scalar.copy(out=q_row_sb[:], in_=q_row[:, 0 : B * NQ])
         pos_col = turn(pos_got, 5, chunk)
         ks_turned = turn(ks_got, 3, chunk)
-        limit = tile([P, B * CHUNKS, NQ], F32, "vs_table")
+        early = tile([P, B * CHUNKS * (NQ + 1)], F32, "vs_table")
+        limit = early[:, 0 : B * CHUNKS * NQ].rearrange("p (j q) -> p j q", q=NQ)
+        ks_col = early[:, B * CHUNKS * NQ :]
         for j in range(B * CHUNKS):
             s = j // CHUNKS
             nc.vector.tensor_scalar(
                 limit[:, j, :], q_row_sb[:, s * NQ : (s + 1) * NQ], pos_col[:, j : j + 1], MASKED, ALU.is_lt, ALU.mult
             )
+        nc.vector.tensor_copy(ks_col, ks_turned)
         vs_turned = turn(vs_got, 2, dealt)
+        score[0] = bank(0)
+        for c in range(CHUNKS):
+            nc.tensor.matmul(score[0][:, chunk(c)], lhsT=limit[:, c, :], rhs=ident[:], start=c == 0, stop=False, is_transpose=True)
 
         k_first = tile([P, PAIR, B * N], BF16, "k_first")
         k_bf = tiles(PARTS, [P, PART, PACK], BF16, "k_bf")
@@ -131,17 +145,19 @@ def tile_attend_x_ks_draft_kernel(tc, qT, kT, vT, ks, vs, pos, qpos, offs, out):
             nc.vector.tensor_copy(
                 out=k_bf[i][:, :, 0:PAIR], in_=k_first[:, :, i * PART : (i + 1) * PART].rearrange("p t n -> p n t")
             )
+        vs_col = tile([P, B * CHUNKS], F32, "k_first")
+        nc.vector.tensor_copy(vs_col[:], vs_turned)
         gather_scalar(k_pair[:, 0, :], k_pool[2], 0, B * N)
 
         q_bf = tiles(B, [P, NQ, PACK], BF16, "q_bf")
         q_codes = tiles(B, [P, NQ], U32, "q_codes")
         q_scales = tiles(B, [P, NQ], U8, "q_scales")
         scaled = tiles(PARTS, [P, PART], F32, "scaled")
-        shift = tiles(B, [P, 1], F32, "shift")
+        shift = [tile([P, 1], F32, "shift0")[:], placed([P, 32], F32, "shift1", HELD - 64)[:, 0:1]]
         sums = tiles(B, [P, PAIR], F32, "sums")
-        total = tiles(B, [P, 1], F32, "total")
+        total = [placed([P, 1], F32, "total0", POOL_BYTES + PROB_BYTES + 2 * WOVEN_BYTES), tile([P, 1], F32, "total1")]
         inv = tiles(B, [P, 1], F32, "inv")
-        w_bf = tiles(B, [P, NQ, PACK], BF16, "w_bf")
+        w_bf = [placed([P, NQ, PACK], BF16, "w_bf0", POOL_BYTES + PROB_BYTES), tile([P, NQ, PACK], BF16, "w_bf1")]
         w_codes = tiles(B, [P, NQ], U32, "w_codes")
         w_scales = tiles(B, [P, NQ], U8, "w_scales")
         v_bf = {}
@@ -181,26 +197,35 @@ def tile_attend_x_ks_draft_kernel(tc, qT, kT, vT, ks, vs, pos, qpos, offs, out):
         def scale(i):
             for c in range(PER_PART):
                 j = i * PER_PART + c
-                nc.vector.scalar_tensor_tensor(
-                    scaled[i][:, c * P : (c + 1) * P], raw[i][:, c * P : (c + 1) * P], ks_turned[:, j : j + 1], limit[:, j, :],
-                    ALU.mult, ALU.subtract,
-                )
+                if j < CHUNKS:
+                    nc.scalar.activation(scaled[i][:, chunk(c)], raw[i][:, chunk(c)], ACT.Copy, scale=ks_col[:, j : j + 1])
+                else:
+                    nc.vector.scalar_tensor_tensor(
+                        scaled[i][:, chunk(c)], raw[i][:, chunk(c)], ks_col[:, j : j + 1], limit[:, j, :], ALU.mult, ALU.add
+                    )
 
         def turn_scores(s):
-            score[s] = bank(s)
+            if s > 0:
+                score[s] = bank(s)
             for c in range(CHUNKS):
                 i, k = divmod(s * CHUNKS + c, PER_PART)
-                nc.tensor.transpose(score[s][:, c * P : (c + 1) * P], scaled[i][:, k * P : (k + 1) * P], ident[:])
+                if s > 0:
+                    nc.tensor.transpose(score[s][:, chunk(c)], scaled[i][:, chunk(k)], ident[:])
+                else:
+                    nc.tensor.matmul(
+                        score[s][:, chunk(c)], lhsT=scaled[i][:, chunk(k)], rhs=ident[:], start=False, stop=c == CHUNKS - 1,
+                        is_transpose=True,
+                    )
 
         def row_max(s):
-            nc.vector.tensor_reduce(shift[s][:], score[s][:], mybir.AxisListType.X, ALU.max, negate=True)
+            nc.vector.tensor_reduce(shift[s], score[s][:], mybir.AxisListType.X, ALU.max, negate=True)
 
         def exponent(s):
             for u in range(PAIR):
                 places = slice(u * PAIR, (u + 1) * PAIR)
                 nc.scalar.activation(
                     prob[s][:, places, :], score[s][:].rearrange("q (n t) -> q t n", t=PACK)[:, places, :],
-                    ACT.Exp, bias=shift[s][:], accum_out=sums[s][:, u : u + 1],
+                    ACT.Exp, bias=shift[s], accum_out=sums[s][:, u : u + 1],
                 )
 
         def turn_prob(s):
@@ -228,12 +253,12 @@ def tile_attend_x_ks_draft_kernel(tc, qT, kT, vT, ks, vs, pos, qpos, offs, out):
             v_words[e, s] = [words[:, u : N // 2 : PAIR] for u in range(PAIR)]
 
         def turn_v(e, s):
-            v_turned[e, s] = bank(4 + 2 * e + s)
+            v_turned[e, s] = bank(4 + 2 * s + 1 - e)
             for u in range(PAIR):
                 nc.tensor.transpose(v_turned[e, s][:, u * P : (u + 1) * P], v_words[e, s][u], ident[:])
 
-        def copy_v(e, s, copy, name):
-            v_bf[e, s] = tile([P, P * PACK], BF16, name)
+        def copy_v(e, s, copy, home):
+            v_bf[e, s] = home
             copy(
                 out=v_bf[e, s][:].bitcast(F32).rearrange("p (c u) -> p c u", u=PAIR),
                 in_=v_turned[e, s][:, 0 : PAIR * P].rearrange("p (u c) -> p c u", u=PAIR),
@@ -255,49 +280,49 @@ def tile_attend_x_ks_draft_kernel(tc, qT, kT, vT, ks, vs, pos, qpos, offs, out):
         gather_last(0, gather_vector)
         for i in range(1, PARTS):
             gather_last(i, gather_scalar)
-        weave_q(0)
         weave_last(0, nc.vector.tensor_copy)
         weave_last(1, nc.vector.tensor_copy)
         weave_last(2, nc.scalar.copy)
         weave_last(3, nc.scalar.copy)
-        vs_col = tile([P, B * CHUNKS], F32, "k_pair")
-        nc.vector.tensor_copy(vs_col[:], vs_turned)
-        quantize_q(0)
+        weave_q(0)
         quantize_k(0)
-        quantize_k(1)
         weave_q(1)
-        quantize_k(2)
+        quantize_q(0)
+        quantize_k(1)
         quantize_q(1)
+        quantize_k(2)
         quantize_k(3)
         for i in range(PARTS):
             multiply_k(i)
         for i in range(PARTS):
             scale(i)
-        for e in range(E_BLOCKS):
-            for s in range(B):
-                gather_v(e, s, gather_scalar)
         for s in range(B):
             turn_scores(s)
             row_max(s)
-        spare = tile([P, T], F32, "v_pool1")
         for s in range(B):
-            prob[s] = spare[:, s * N : (s + 1) * N].rearrange("q (t n) -> q t n", t=PACK)
+            gather_v(0, s, gather_scalar)
+        gather_v(1, 0, gather_vector)
+        gather_v(1, 1, gather_scalar)
+        for s in range(B):
+            prob[s] = placed([P, PACK, P], F32, f"prob{s}", s * POOL_BYTES)
             exponent(s)
             turn_prob(s)
         for e in range(E_BLOCKS):
             for s in range(B):
                 turn_v(e, s)
         weights(0)
-        for s in range(B):
-            copy_v(0, s, nc.vector.tensor_copy, f"v_bf{s}")
-            quantize_v(0, s)
+        copy_v(0, 0, nc.vector.tensor_copy, placed([P, N], BF16, "v_bf00", POOL_BYTES + PROB_BYTES + WOVEN_BYTES))
+        quantize_v(0, 0)
         quantize_w(0)
-        row_sum(0)
         weights(1)
-        for s in range(B):
-            copy_v(1, s, nc.scalar.copy, f"shift{s}")
-            quantize_v(1, s)
+        copy_v(1, 0, nc.scalar.copy, placed([P, N], BF16, "v_bf10", HELD))
+        copy_v(0, 1, nc.scalar.copy, placed([P, N], BF16, "v_bf01", HELD - WOVEN_BYTES))
+        copy_v(1, 1, nc.scalar.copy, tile([P, N], BF16, "v_bf11"))
+        quantize_v(1, 0)
+        row_sum(0)
+        quantize_v(0, 1)
         quantize_w(1)
+        quantize_v(1, 1)
         row_sum(1)
         values(0)
         values(1)

@@ -28,7 +28,8 @@ SHIFT = 16
 POOL_BYTES = 4 * T
 PROB_BYTES = 4 * N
 WOVEN_BYTES = 2 * N
-HELD = 2 * POOL_BYTES + WOVEN_BYTES
+SHIFT_AT = PROB_BYTES + 3 * WOVEN_BYTES - 64
+SCALAR_SHARE = 128
 
 FLOPS = 2 * B * NQ * N * (D + DV)
 BYTES = 4 * (B * D * NQ + (D + DV) * T + 3 * T + B * NQ + B * NQ * DV) + 2 * P * (B * N // 16)
@@ -52,6 +53,9 @@ def tile_attend_x_ks_draft_kernel(tc, qT, kT, vT, ks, vs, pos, qpos, offs, out):
 
         def placed(shape, dtype, name, at):
             return reuse.tile(shape, dtype, name=name, align_bytes=64, offset=at)
+
+        def behind_values(shape, dtype, name, at):
+            return placed(shape, dtype, name, POOL_BYTES + at)
 
         offsets = keep.tile([P, B * N // 16], U16, name="offsets")
         nc.sync.dma_start(offsets[:], offs)
@@ -153,11 +157,11 @@ def tile_attend_x_ks_draft_kernel(tc, qT, kT, vT, ks, vs, pos, qpos, offs, out):
         q_codes = tiles(B, [P, NQ], U32, "q_codes")
         q_scales = tiles(B, [P, NQ], U8, "q_scales")
         scaled = tiles(PARTS, [P, PART], F32, "scaled")
-        shift = [tile([P, 1], F32, "shift0")[:], placed([P, 32], F32, "shift1", HELD - 64)[:, 0:1]]
+        shift = {0: tile([P, 1], F32, "shift0")[:]}
         sums = tiles(B, [P, PAIR], F32, "sums")
-        total = [placed([P, 1], F32, "total0", POOL_BYTES + PROB_BYTES + 2 * WOVEN_BYTES), tile([P, 1], F32, "total1")]
+        total = tiles(B, [P, 1], F32, "total")
         inv = tiles(B, [P, 1], F32, "inv")
-        w_bf = [placed([P, NQ, PACK], BF16, "w_bf0", POOL_BYTES + PROB_BYTES), tile([P, NQ, PACK], BF16, "w_bf1")]
+        w_bf = {1: tile([P, NQ, PACK], BF16, "w_bf1")}
         w_codes = tiles(B, [P, NQ], U32, "w_codes")
         w_scales = tiles(B, [P, NQ], U8, "w_scales")
         v_bf = {}
@@ -246,9 +250,11 @@ def tile_attend_x_ks_draft_kernel(tc, qT, kT, vT, ks, vs, pos, qpos, offs, out):
             nc.vector.tensor_reduce(total[s][:], sums[s][:], mybir.AxisListType.X, ALU.add)
             nc.vector.reciprocal(inv[s][:], total[s][:])
 
-        def gather_v(e, s, gather):
+        def gather_v(e, s, cut):
             got = tile([P, N], BF16, f"v_got{e}{s}")
-            gather(got[:], v_pool[e], s * N, (s + 1) * N)
+            gather_scalar(got[:, 0:cut], v_pool[e], s * N, s * N + cut)
+            if cut < N:
+                gather_vector(got[:, cut:N], v_pool[e], s * N + cut, (s + 1) * N)
             words = got[:].bitcast(F32)
             v_words[e, s] = [words[:, u : N // 2 : PAIR] for u in range(PAIR)]
 
@@ -268,13 +274,24 @@ def tile_attend_x_ks_draft_kernel(tc, qT, kT, vT, ks, vs, pos, qpos, offs, out):
             block = slice(e * P, (e + 1) * P)
             quantize(v_codes[s][:, block], v_scales[s][:, block], v_bf[e, s][:])
 
+        def multiply_v(s, ps, a, z):
+            nc.tensor.matmul_mx(
+                out=ps[:, 0 : z - a], lhsT=w_codes[s][:].bitcast(FP8X4), lhsT_scale=w_scales[s][:],
+                rhs=v_codes[s][:, a:z].bitcast(FP8X4), rhs_scale=v_scales[s][:, a:z], start=True, stop=True,
+            )
+
         def values(s):
             ps = bank(s)
-            nc.tensor.matmul_mx(
-                out=ps[:, 0:DV], lhsT=w_codes[s][:].bitcast(FP8X4), lhsT_scale=w_scales[s][:],
-                rhs=v_codes[s][:].bitcast(FP8X4), rhs_scale=v_scales[s][:], start=True, stop=True,
-            )
+            multiply_v(s, ps, 0, DV)
             nc.scalar.activation(result[s][:], ps[:, 0:DV], ACT.Copy, scale=inv[s][:])
+            nc.sync.dma_start(out[s], result[s][:])
+
+        def values_in_halves(s):
+            low, high = bank(s), bank(2)
+            multiply_v(s, low, 0, P)
+            multiply_v(s, high, P, DV)
+            nc.vector.tensor_scalar(result[s][:, 0:P], low[:, 0:P], inv[s][:], None, ALU.mult)
+            nc.scalar.activation(result[s][:, P:DV], high[:, 0:P], ACT.Copy, scale=inv[s][:])
             nc.sync.dma_start(out[s], result[s][:])
 
         gather_last(0, gather_vector)
@@ -298,31 +315,34 @@ def tile_attend_x_ks_draft_kernel(tc, qT, kT, vT, ks, vs, pos, qpos, offs, out):
             scale(i)
         for s in range(B):
             turn_scores(s)
-            row_max(s)
+        row_max(0)
         for s in range(B):
-            gather_v(0, s, gather_scalar)
-        gather_v(1, 0, gather_vector)
-        gather_v(1, 1, gather_scalar)
+            gather_v(0, s, N)
+        gather_v(1, 0, N)
+        gather_v(1, 1, SCALAR_SHARE)
+        shift[1] = behind_values([P, 32], F32, "shift1", SHIFT_AT)[:, 0:1]
+        row_max(1)
         for s in range(B):
-            prob[s] = placed([P, PACK, P], F32, f"prob{s}", s * POOL_BYTES)
+            prob[s] = behind_values([P, PACK, P], F32, "prob0", 0) if s == 0 else tile([P, PACK, P], F32, "prob1")
             exponent(s)
             turn_prob(s)
         for e in range(E_BLOCKS):
             for s in range(B):
                 turn_v(e, s)
-        weights(0)
-        copy_v(0, 0, nc.vector.tensor_copy, placed([P, N], BF16, "v_bf00", POOL_BYTES + PROB_BYTES + WOVEN_BYTES))
-        quantize_v(0, 0)
-        quantize_w(0)
-        weights(1)
-        copy_v(1, 0, nc.scalar.copy, placed([P, N], BF16, "v_bf10", HELD))
-        copy_v(0, 1, nc.scalar.copy, placed([P, N], BF16, "v_bf01", HELD - WOVEN_BYTES))
-        copy_v(1, 1, nc.scalar.copy, tile([P, N], BF16, "v_bf11"))
-        quantize_v(1, 0)
+        for e in range(E_BLOCKS):
+            copy_v(e, 0, nc.vector.tensor_copy, behind_values([P, N], BF16, f"v_bf{e}0", PROB_BYTES + e * WOVEN_BYTES))
+        for e in range(E_BLOCKS):
+            quantize_v(e, 0)
         row_sum(0)
-        quantize_v(0, 1)
+        w_bf[0] = behind_values([P, NQ, PACK], BF16, "w_bf0", PROB_BYTES)
+        weights(0)
+        weights(1)
+        for e in range(E_BLOCKS):
+            copy_v(e, 1, nc.scalar.copy, behind_values([P, N], BF16, f"v_bf{e}1", PROB_BYTES + (2 + e) * WOVEN_BYTES))
+        quantize_w(0)
+        for e in range(E_BLOCKS):
+            quantize_v(e, 1)
         quantize_w(1)
-        quantize_v(1, 1)
         row_sum(1)
         values(0)
-        values(1)
+        values_in_halves(1)

@@ -134,9 +134,6 @@ def tile_attend_x_ks_draft_kernel(tc, qT, kT, vT, ks, vs, pos, qpos, offs, out):
             )
         nc.vector.tensor_copy(ks_col, ks_turned)
         vs_turned = turn(vs_got, 2, dealt)
-        score[0] = bank(0)
-        for c in range(CHUNKS):
-            nc.tensor.matmul(score[0][:, chunk(c)], lhsT=limit[:, c, :], rhs=ident[:], start=c == 0, stop=False, is_transpose=True)
 
         k_first = tile([P, PAIR, B * N], BF16, "k_first")
         k_bf = tiles(PARTS, [P, PART, PACK], BF16, "k_bf")
@@ -201,25 +198,15 @@ def tile_attend_x_ks_draft_kernel(tc, qT, kT, vT, ks, vs, pos, qpos, offs, out):
         def scale(i):
             for c in range(PER_PART):
                 j = i * PER_PART + c
-                if j < CHUNKS:
-                    nc.scalar.activation(scaled[i][:, chunk(c)], raw[i][:, chunk(c)], ACT.Copy, scale=ks_col[:, j : j + 1])
-                else:
-                    nc.vector.scalar_tensor_tensor(
-                        scaled[i][:, chunk(c)], raw[i][:, chunk(c)], ks_col[:, j : j + 1], limit[:, j, :], ALU.mult, ALU.add
-                    )
+                nc.vector.scalar_tensor_tensor(
+                    scaled[i][:, chunk(c)], raw[i][:, chunk(c)], ks_col[:, j : j + 1], limit[:, j, :], ALU.mult, ALU.add
+                )
 
         def turn_scores(s):
-            if s > 0:
-                score[s] = bank(s)
+            score[s] = bank(s)
             for c in range(CHUNKS):
                 i, k = divmod(s * CHUNKS + c, PER_PART)
-                if s > 0:
-                    nc.tensor.transpose(score[s][:, chunk(c)], scaled[i][:, chunk(k)], ident[:])
-                else:
-                    nc.tensor.matmul(
-                        score[s][:, chunk(c)], lhsT=scaled[i][:, chunk(k)], rhs=ident[:], start=False, stop=c == CHUNKS - 1,
-                        is_transpose=True,
-                    )
+                nc.tensor.transpose(score[s][:, chunk(c)], scaled[i][:, chunk(k)], ident[:])
 
         def row_max(s):
             nc.vector.tensor_reduce(shift[s], score[s][:], mybir.AxisListType.X, ALU.max, negate=True)

@@ -79,10 +79,9 @@ def tile_attend_x_ks_draft_kernel(tc, qT, kT, vT, ks, vs, pos, qpos, offs, out):
             engine.memset(table[name][0:ROW, a:z].bitcast(U32), 0)
 
         fill(nc.vector, "pos", 0, T)
-        fill(nc.gpsimd, "ks", 0, FIRST_FILL)
-        fill(nc.gpsimd, "ks", FIRST_FILL, T)
-        fill(nc.vector, "vs", 0, T // 2)
-        fill(nc.gpsimd, "vs", T // 2, T)
+        fill(nc.vector, "ks", 0, T)
+        fill(nc.gpsimd, "vs", 0, FIRST_FILL)
+        fill(nc.gpsimd, "vs", FIRST_FILL, T)
         nc.sync.dma_start(q_place[:], qpos.rearrange("b q o -> q (b o)"))
         for name, source in (("pos", pos), ("ks", ks), ("vs", vs)):
             nc.sync.dma_start(table[name][ROW:P, :], source[0:1, :])

@@ -58,7 +58,6 @@ def tile_attend_x_ks_draft_kernel(tc, qT, kT, vT, ks, vs, pos, qpos, offs, out):
             return placed(shape, dtype, name, POOL_BYTES + at)
 
         offsets = keep.tile([P, B * N // 16], U16, name="offsets")
-        nc.sync.dma_start(offsets[:], offs)
 
         def gather_vector(dst, window, a, z):
             nc.vector.tensor_copy(dst, window[:].indirect(offsets[:, a // 16 : z // 16]))
@@ -79,12 +78,15 @@ def tile_attend_x_ks_draft_kernel(tc, qT, kT, vT, ks, vs, pos, qpos, offs, out):
             engine.memset(table[name][0:ROW, a:z].bitcast(U32), 0)
 
         fill(nc.vector, "pos", 0, T)
-        fill(nc.vector, "ks", 0, T)
-        fill(nc.gpsimd, "vs", 0, FIRST_FILL)
-        fill(nc.gpsimd, "vs", FIRST_FILL, T)
+        fill(nc.gpsimd, "ks", 0, FIRST_FILL)
+        fill(nc.gpsimd, "ks", FIRST_FILL, T)
+        fill(nc.vector, "vs", 0, T // 2)
+        fill(nc.gpsimd, "vs", T // 2, T)
+        nc.sync.dma_start(table["pos"][ROW:P, :], pos[0:1, :])
+        nc.sync.dma_start(offsets[:], offs)
+        nc.sync.dma_start(table["ks"][ROW:P, :], ks[0:1, :])
         nc.sync.dma_start(q_place[:], qpos.rearrange("b q o -> q (b o)"))
-        for name, source in (("pos", pos), ("ks", ks), ("vs", vs)):
-            nc.sync.dma_start(table[name][ROW:P, :], source[0:1, :])
+        nc.sync.dma_start(table["vs"][ROW:P, :], vs[0:1, :])
         k_rows = kT.rearrange("(p t) n -> p t n", t=PACK)
         k_pool = tiles(PACK, [P, T], F32, "k_pool")
         for t in range(PACK):
@@ -120,7 +122,7 @@ def tile_attend_x_ks_draft_kernel(tc, qT, kT, vT, ks, vs, pos, qpos, offs, out):
 
         score = {}
         q_row_sb = tile([P, B * NQ], F32, "q_row_sb")
-        nc.scalar.copy(out=q_row_sb[:], in_=q_row[:, 0 : B * NQ])
+        nc.vector.tensor_copy(q_row_sb[:], q_row[:, 0 : B * NQ])
         pos_col = turn(pos_got, 5, chunk)
         ks_turned = turn(ks_got, 3, chunk)
         early = tile([P, B * CHUNKS * (NQ + 1)], F32, "vs_table")

from contextlib import ExitStack

import concourse.mybir as mybir
from concourse.masks import make_identity

F32 = mybir.dt.float32
BF16 = mybir.dt.bfloat16
U32 = mybir.dt.uint32
U16 = mybir.dt.uint16
U8 = mybir.dt.uint8
FP8X4 = mybir.dt.float8_e4m3fn_x4
ALU = mybir.AluOpType
ACT = mybir.ActivationFunctionType

B, NQ, D, DV, N, T = 2, 128, 512, 256, 512, 2048
P = 128
ROW = P - 1
PACK = 4
PAIR = PACK // 2
CHUNKS = N // P
PART = 256
PARTS = B * N // PART
PER_PART = PART // P
E_BLOCKS = DV // P
MASKED = -1.0e30
FIRST_FILL = 256
SHIFT = 16
POOL_BYTES = 4 * T
PROB_BYTES = 4 * N
WOVEN_BYTES = 2 * N
SHIFT_AT = PROB_BYTES + 3 * WOVEN_BYTES - 64
SCALAR_SHARE = 128

FLOPS = 2 * B * NQ * N * (D + DV)
BYTES = 4 * (B * D * NQ + (D + DV) * T + 3 * T + B * NQ + B * NQ * DV) + 2 * P * (B * N // 16)


def tile_attend_x_ks_draft_kernel(tc, qT, kT, vT, ks, vs, pos, qpos, offs, out):
    nc = tc.nc
    with ExitStack() as ctx:
        keep = ctx.enter_context(tc.tile_pool(name="keep", bufs=1))
        reuse = ctx.enter_context(tc.tile_pool(name="reuse", bufs=1))
        psum = ctx.enter_context(tc.psum_pool(name="psum", bufs=1))

        def bank(index):
            return psum.tile([P, 512], F32, name=f"bank{index}")

        def tile(shape, dtype, name):
            return keep.tile(shape, dtype, name=name, align_bytes=64)

        def tiles(count, shape, dtype, name):
            return [tile(shape, dtype, f"{name}{i}") for i in range(count)]

        def placed(shape, dtype, name, at):
            return reuse.tile(shape, dtype, name=name, align_bytes=64, offset=at)

        def behind_values(shape, dtype, name, at):
            return placed(shape, dtype, name, POOL_BYTES + at)

        offsets = keep.tile([P, B * N // 16], U16, name="offsets")

        def gather_vector(dst, window, a, z):
            nc.vector.tensor_copy(dst, window[:].indirect(offsets[:, a // 16 : z // 16]))

        def gather_scalar(dst, window, a, z):
            nc.scalar.activation(dst, window[:].indirect(offsets[:, a // 16 : z // 16]), ACT.Copy)

        warm = tile([P, 1], F32, "warm")
        warm_out = tile([P, 1], F32, "warm_out")
        nc.vector.memset(warm[:], 0.0)
        nc.scalar.activation(warm_out[:], warm[:], ACT.Exp)
        ident = tile([P, P], F32, "ident")
        make_identity(nc, ident[:])
        table = {name: tile([P, T], F32, name + "_table") for name in ("pos", "ks", "vs")}
        q_place = tile([P, B], F32, "q_place")

        def fill(engine, name, a, z):
            engine.memset(table[name][0:ROW, a:z].bitcast(U32), 0)

        fill(nc.vector, "pos", 0, T)
        fill(nc.gpsimd, "ks", 0, FIRST_FILL)
        fill(nc.gpsimd, "ks", FIRST_FILL, T)
        fill(nc.vector, "vs", 0, T // 2)
        fill(nc.gpsimd, "vs", T // 2, T)
        nc.sync.dma_start(table["pos"][ROW:P, :], pos[0:1, :])
        nc.sync.dma_start(offsets[:], offs)
        nc.sync.dma_start(table["ks"][ROW:P, :], ks[0:1, :])
        nc.sync.dma_start(q_place[:], qpos.rearrange("b q o -> q (b o)"))
        nc.sync.dma_start(table["vs"][ROW:P, :], vs[0:1, :])
        k_rows = kT.rearrange("(p t) n -> p t n", t=PACK)
        k_pool = tiles(PACK, [P, T], F32, "k_pool")
        for t in range(PACK):
            nc.sync.dma_start(k_pool[t][:], k_rows[:, t, :])
        q_raw = tiles(B, [P, PACK, NQ], F32, "q_raw")
        for s in range(B):
            nc.sync.dma_start(q_raw[s][:], qT[s].rearrange("(p t) q -> p t q", t=PACK))
        v_pool = [placed([P, T], F32, f"v_pool{e}", e * POOL_BYTES) for e in range(E_BLOCKS)]
        for e in range(E_BLOCKS):
            nc.sync.dma_start(v_pool[e][:], vT[e * P : (e + 1) * P, :])
        q_row = bank(4)
        for s in range(B):
            nc.tensor.transpose(q_row[:, s * NQ : (s + 1) * NQ], q_place[:, s : s + 1].to_broadcast([P, P]), ident[:])

        def chunk(j):
            return slice(j * P, (j + 1) * P)

        def dealt(j):
            return slice(j // PACK * N + j % PACK, (j // PACK + 1) * N, PACK)

        def turn(got, index, pick):
            ps = bank(index)
            for j in reversed(range(B * CHUNKS)):
                nc.tensor.transpose(ps[:, j * SHIFT : j * SHIFT + P], got[:, pick(j)], ident[:])
            return ps[:, ROW : ROW + B * CHUNKS * SHIFT : SHIFT]

        pos_got = tile([P, B * N], F32, "pos_got")
        ks_got = tile([P, B * N], F32, "ks_got")
        vs_got = tile([P, B * N], F32, "vs_got")
        gather_scalar(pos_got[:], table["pos"], 0, B * N)
        gather_vector(ks_got[:], table["ks"], 0, B * N)
        gather_vector(vs_got[:], table["vs"], 0, B * N)

        score = {}
        q_row_sb = tile([P, B * NQ], F32, "q_row_sb")
        nc.vector.tensor_copy(q_row_sb[:], q_row[:, 0 : B * NQ])
        pos_col = turn(pos_got, 5, chunk)
        ks_turned = turn(ks_got, 3, chunk)
        early = tile([P, B * CHUNKS * (NQ + 1)], F32, "vs_table")
        limit = early[:, 0 : B * CHUNKS * NQ].rearrange("p (j q) -> p j q", q=NQ)
        ks_col = early[:, B * CHUNKS * NQ :]
        for j in range(B * CHUNKS):
            s = j // CHUNKS
            nc.vector.tensor_scalar(
                limit[:, j, :], q_row_sb[:, s * NQ : (s + 1) * NQ], pos_col[:, j : j + 1], MASKED, ALU.is_lt, ALU.mult
            )
        nc.vector.tensor_copy(ks_col, ks_turned)
        vs_turned = turn(vs_got, 2, dealt)

        k_first = tile([P, PAIR, B * N], BF16, "k_first")
        k_bf = tiles(PARTS, [P, PART, PACK], BF16, "k_bf")
        k_codes = tiles(PARTS, [P, PART], U32, "k_codes")
        k_scales = tiles(PARTS, [P, PART], U8, "k_scales")
        k_pair = tile([P, PAIR, B * N], BF16, "k_pair")
        for t in range(PAIR):
            gather_scalar(k_first[:, t, :], k_pool[t], 0, B * N)
        for i in range(PARTS):
            nc.vector.tensor_copy(
                out=k_bf[i][:, :, 0:PAIR], in_=k_first[:, :, i * PART : (i + 1) * PART].rearrange("p t n -> p n t")
            )
        vs_col = tile([P, B * CHUNKS], F32, "k_first")
        nc.vector.tensor_copy(vs_col[:], vs_turned)
        gather_scalar(k_pair[:, 0, :], k_pool[2], 0, B * N)

        q_bf = tiles(B, [P, NQ, PACK], BF16, "q_bf")
        q_codes = tiles(B, [P, NQ], U32, "q_codes")
        q_scales = tiles(B, [P, NQ], U8, "q_scales")
        scaled = tiles(PARTS, [P, PART], F32, "scaled")
        shift = {0: tile([P, 1], F32, "shift0")[:]}
        sums = tiles(B, [P, PAIR], F32, "sums")
        total = tiles(B, [P, 1], F32, "total")
        inv = tiles(B, [P, 1], F32, "inv")
        w_bf = {1: tile([P, NQ, PACK], BF16, "w_bf1")}
        w_codes = tiles(B, [P, NQ], U32, "w_codes")
        w_scales = tiles(B, [P, NQ], U8, "w_scales")
        v_bf = {}
        v_codes = tiles(B, [P, DV], U32, "v_codes")
        v_scales = tiles(B, [P, DV], U8, "v_scales")
        result = tiles(B, [P, DV], F32, "result")
        raw, prob, turned, v_words, v_turned = {}, {}, {}, {}, {}

        def quantize(codes, scales, values):
            nc.vector.quantize_mx(out=codes.bitcast(FP8X4), scales=scales, in_=values)

        def gather_last(i, gather):
            gather(k_pair[:, 1, i * PART : (i + 1) * PART], k_pool[3], i * PART, (i + 1) * PART)

        def weave_last(i, copy):
            copy(out=k_bf[i][:, :, PAIR:PACK], in_=k_pair[:, :, i * PART : (i + 1) * PART].rearrange("p t n -> p n t"))

        def weave_q(s):
            nc.vector.tensor_copy(out=q_bf[s][:], in_=q_raw[s][:].rearrange("p t q -> p q t"))

        def quantize_q(s):
            quantize(q_codes[s][:], q_scales[s][:], q_bf[s][:].rearrange("p q t -> p (q t)"))

        def quantize_k(i):
            quantize(k_codes[i][:], k_scales[i][:], k_bf[i][:].rearrange("p n t -> p (n t)"))

        def multiply_k(i):
            s = i * PART // N
            raw[i] = bank(4 + i)
            for c in range(PER_PART):
                kc = slice(c * P, (c + 1) * P)
                nc.tensor.matmul_mx(
                    out=raw[i][:, kc], lhsT=k_codes[i][:, kc].bitcast(FP8X4), lhsT_scale=k_scales[i][:, kc],
                    rhs=q_codes[s][:].bitcast(FP8X4), rhs_scale=q_scales[s][:], start=True, stop=True,
                )

        def scale(i):
            for c in range(PER_PART):
                j = i * PER_PART + c
                nc.vector.scalar_tensor_tensor(
                    scaled[i][:, chunk(c)], raw[i][:, chunk(c)], ks_col[:, j : j + 1], limit[:, j, :], ALU.mult, ALU.add
                )

        def turn_scores(s):
            score[s] = bank(s)
            for c in range(CHUNKS):
                i, k = divmod(s * CHUNKS + c, PER_PART)
                nc.tensor.transpose(score[s][:, chunk(c)], scaled[i][:, chunk(k)], ident[:])

        def row_max(s):
            nc.vector.tensor_reduce(shift[s], score[s][:], mybir.AxisListType.X, ALU.max, negate=True)

        def exponent(s):
            for u in range(PAIR):
                places = slice(u * PAIR, (u + 1) * PAIR)
                nc.scalar.activation(
                    prob[s][:, places, :], score[s][:].rearrange("q (n t) -> q t n", t=PACK)[:, places, :],
                    ACT.Exp, bias=shift[s], accum_out=sums[s][:, u : u + 1],
                )

        def turn_prob(s):
            turned[s] = bank(2 + s)
            for t in range(PACK):
                nc.tensor.transpose(turned[s][:, t * P : (t + 1) * P], prob[s][:, t, :], ident[:])

        def weights(s):
            nc.vector.tensor_tensor(
                w_bf[s][:], turned[s][:].rearrange("p (t q) -> p q t", t=PACK),
                vs_col[:, s * PACK : (s + 1) * PACK].unsqueeze(1).to_broadcast([P, NQ, PACK]), ALU.mult,
            )

        def quantize_w(s):
            quantize(w_codes[s][:], w_scales[s][:], w_bf[s][:].rearrange("p q t -> p (q t)"))

        def row_sum(s):
            nc.vector.tensor_reduce(total[s][:], sums[s][:], mybir.AxisListType.X, ALU.add)
            nc.vector.reciprocal(inv[s][:], total[s][:])

        def gather_v(e, s, cut):
            got = tile([P, N], BF16, f"v_got{e}{s}")
            gather_scalar(got[:, 0:cut], v_pool[e], s * N, s * N + cut)
            if cut < N:
                gather_vector(got[:, cut:N], v_pool[e], s * N + cut, (s + 1) * N)
            words = got[:].bitcast(F32)
            v_words[e, s] = [words[:, u : N // 2 : PAIR] for u in range(PAIR)]

        def turn_v(e, s):
            v_turned[e, s] = bank(4 + 2 * s + 1 - e)
            for u in range(PAIR):
                nc.tensor.transpose(v_turned[e, s][:, u * P : (u + 1) * P], v_words[e, s][u], ident[:])

        def copy_v(e, s, copy, home):
            v_bf[e, s] = home
            copy(
                out=v_bf[e, s][:].bitcast(F32).rearrange("p (c u) -> p c u", u=PAIR),
                in_=v_turned[e, s][:, 0 : PAIR * P].rearrange("p (u c) -> p c u", u=PAIR),
            )

        def quantize_v(e, s):
            block = slice(e * P, (e + 1) * P)
            quantize(v_codes[s][:, block], v_scales[s][:, block], v_bf[e, s][:])

        def multiply_v(s, ps, a, z):
            nc.tensor.matmul_mx(
                out=ps[:, 0 : z - a], lhsT=w_codes[s][:].bitcast(FP8X4), lhsT_scale=w_scales[s][:],
                rhs=v_codes[s][:, a:z].bitcast(FP8X4), rhs_scale=v_scales[s][:, a:z], start=True, stop=True,
            )

        def values(s):
            ps = bank(s)
            multiply_v(s, ps, 0, DV)
            nc.scalar.activation(result[s][:], ps[:, 0:DV], ACT.Copy, scale=inv[s][:])
            nc.sync.dma_start(out[s], result[s][:])

        def values_in_halves(s):
            low, high = bank(s), bank(2)
            multiply_v(s, low, 0, P)
            multiply_v(s, high, P, DV)
            nc.vector.tensor_scalar(result[s][:, 0:P], low[:, 0:P], inv[s][:], None, ALU.mult)
            nc.scalar.activation(result[s][:, P:DV], high[:, 0:P], ACT.Copy, scale=inv[s][:])
            nc.sync.dma_start(out[s], result[s][:])

        gather_last(0, gather_vector)
        for i in range(1, PARTS):
            gather_last(i, gather_scalar)
        weave_last(0, nc.vector.tensor_copy)
        weave_last(1, nc.vector.tensor_copy)
        weave_last(2, nc.scalar.copy)
        weave_last(3, nc.scalar.copy)
        weave_q(0)
        quantize_k(0)
        weave_q(1)
        quantize_q(0)
        quantize_k(1)
        quantize_q(1)
        quantize_k(2)
        quantize_k(3)
        for i in range(PARTS):
            multiply_k(i)
        for i in range(PARTS):
            scale(i)
        for s in range(B):
            turn_scores(s)
        row_max(0)
        for s in range(B):
            gather_v(0, s, N)
        gather_v(1, 0, N)
        gather_v(1, 1, SCALAR_SHARE)
        shift[1] = behind_values([P, 32], F32, "shift1", SHIFT_AT)[:, 0:1]
        row_max(1)
        for s in range(B):
            prob[s] = behind_values([P, PACK, P], F32, "prob0", 0) if s == 0 else tile([P, PACK, P], F32, "prob1")
            exponent(s)
            turn_prob(s)
        for e in range(E_BLOCKS):
            for s in range(B):
                turn_v(e, s)
        for e in range(E_BLOCKS):
            copy_v(e, 0, nc.vector.tensor_copy, behind_values([P, N], BF16, f"v_bf{e}0", PROB_BYTES + e * WOVEN_BYTES))
        for e in range(E_BLOCKS):
            quantize_v(e, 0)
        row_sum(0)
        w_bf[0] = behind_values([P, NQ, PACK], BF16, "w_bf0", PROB_BYTES)
        weights(0)
        weights(1)
        for e in range(E_BLOCKS):
            copy_v(e, 1, nc.scalar.copy, behind_values([P, N], BF16, f"v_bf{e}1", PROB_BYTES + (2 + e) * WOVEN_BYTES))
        quantize_w(0)
        for e in range(E_BLOCKS):
            quantize_v(e, 1)
        quantize_w(1)
        row_sum(1)
        values(0)
        values_in_halves(1)
